import numpy as np, ml_dtypes
CORES = [9,25,41,57]
N = 4
BF = ml_dtypes.bfloat16
def gentries(a):
    return np.ascontiguousarray(a.reshape(8, 16, -1).transpose(0, 2, 1)).reshape(8, -1)
def gtable(e):
    e = np.asarray(e); return np.ascontiguousarray(e.reshape(8, -1, 16).transpose(0, 2, 1)).reshape(128, -1).astype(np.int32)
W, M, B, T, P, QU, TH = 4096, 1024, 256, 4, 2, 12, 254
def parts(rng):
    d = {}
    d["pr"] = (224 * rng.random((N, 8, 1, W)) ** 3 + 32 * rng.random((N, 8, 16, W))).astype(np.int64)
    d["ad"] = (np.exp2(rng.integers(2, 8, (N, 8, 1, W))) * rng.random((N, 8, 16, W))).astype(np.int64)
    d["mc"] = rng.integers(0, W, (N, 8, 16, M))
    d["gl"] = (224 * rng.random((N, 8, 1, M)) + 32 * rng.random((N, 8, 16, M))).astype(np.int64)
    d["z"] = (224 * rng.random((N, 8, 1, B)) + 32 * rng.random((N, 8, 16, B))).astype(np.int64)
    d["m"] = rng.integers(0, M, (N, 8, B))
    d["dv"] = (np.exp2(rng.integers(2, 8, (N, 8, 1, T * P))) * rng.random((N, 8, 16, T * P))).astype(np.int64)
    d["wt"] = rng.integers(0, 256, (N, 8, 16, 1))
    return d
def flat(a):
    return np.ascontiguousarray(np.reshape(a, (N, 128, -1)))
def pack(d):
    h = {k: flat(d[k]).astype(np.float32).astype(BF) for k in ("pr", "ad", "gl", "z", "dv", "wt")}
    return {"pr": h["pr"], "ad": h["ad"], "mc": flat(d["mc"]).astype(np.int32), "gl": h["gl"], "z0": h["z"], "m0": np.stack([gtable(a) for a in d["m"]]), "dv": h["dv"], "wt": h["wt"]}
def setup_inputs(rng):
    return pack(parts(rng))
def sized(rng, hi, *shape):
    return np.minimum((float(hi + 1) ** rng.random(shape[:-2] + (1, shape[-1])) * rng.random(shape)).astype(np.int64), hi)
def setup_inputs_spread(rng):
    d = parts(rng)
    d["pr"] = sized(rng, 255, N, 8, 16, W); d["ad"] = sized(rng, 127, N, 8, 16, W); d["dv"] = sized(rng, 255, N, 8, 16, T * P); d["wt"] = sized(rng, 255, N, 8, 16, 1)
    a = sized(rng, 255, N, 8, 16, M); d["gl"] = np.where(rng.random((N, 8, 1, M)) < 0.5, 255 - a, a)
    a = sized(rng, 255, N, 8, 16, B); d["z"] = np.where(rng.random((N, 8, 1, B)) < 0.6, rng.integers(0, 256, (N, 8, 16, B)), a)
    d["mc"] = np.minimum((W * rng.random((N, 8, 16, M)) ** 3).astype(np.int64), W - 1)
    d["m"] = np.minimum((M * rng.random((N, 8, B)) ** 2).astype(np.int64), M - 1)
    return pack(d)
def mix(rng, hi, *shape):
    q = rng.choice(np.array([0.0, 0.1, 0.5, 0.8, 0.9, 1.0]), shape[:-2] + (1, shape[-1]))
    return (rng.random(shape) < q).astype(np.int64) * hi
def setup_inputs_ends(rng):
    d = {"pr": mix(rng, 255, N, 8, 16, W), "ad": mix(rng, 127, N, 8, 16, W), "mc": mix(rng, W - 1, N, 8, 16, M), "gl": mix(rng, 255, N, 8, 16, M), "z": mix(rng, 255, N, 8, 16, B),
         "m": (M - 1) * rng.integers(0, 2, (N, 8, B)), "dv": mix(rng, 255, N, 8, 16, T * P), "wt": mix(rng, 255, N, 8, 16, 1)}
    pr, ad, mc, gl, z, m, dv, wt = [d[k] for k in ("pr", "ad", "mc", "gl", "z", "m", "dv", "wt")]; a = N - 1
    wt[:, 0, :8] = 0; wt[:, 0, 8:] = 255
    gl[0, :, :, 0] = 0; gl[0, :, :, M - 1] = 0
    gl[1, :, :, 0] = 0; gl[1, :, :, M - 1] = 255; m[1] = 0; m[1, 7, B - 1] = M - 1; z[1, 7, :, B - 1] = 0; dv[1, 7, :, :P] = 0
    pr[a, 7, :, 0] = 255; ad[a, 7, :, 0] = 127; ad[a, 7, :, W - 1] = 0; gl[a, 7, :, 0] = 255; gl[a, 7, :, M - 1] = 255
    mc[a, 7, :, 0] = 0; mc[a, 7, :, M - 1] = W - 1
    wt[a, 7] = 0; wt[a, 7, 15] = 255; wt[a, 7, 13:15] = 1
    for i in (0, 1, B - 2, B - 1): z[a, 7, :, i] = 255
    m[a, 7, 1] = 0; m[a, 7, B - 2] = 0; m[a, 7, B - 1] = M - 1
    m[a, 7, :B - 1] = np.where(np.all(z[a, 7, 13:, :B - 1] == 255, axis=0), 0, m[a, 7, :B - 1])
    wt[a, 6] = 255; gl[a, 6, :, 0] = 0; z[a, 6, :, 0] = 255; z[a, 6, :, B - 1] = 255; z[a, 6, :, 1] = 0; z[a, 6, :, B - 2] = 0
    m[a, 6, 0] = 0; m[a, 6, 1] = 0; m[a, 6, B - 2] = 0; m[a, 6, B - 1] = M - 1
    return pack(d)
def setup_inputs_corners(rng):
    d = parts(rng); pr, ad, mc, gl, z, m, dv, wt = [d[k] for k in ("pr", "ad", "mc", "gl", "z", "m", "dv", "wt")]
    m[:, 0] = 0; m[:, 1] = M - 1; m[:, 2] = np.arange(B); m[:, 3] = M - 1 - np.arange(B)
    wt[:, 0] = 0; wt[:, 1] = 255; dv[:, 4] = 255; dv[:, 5] = 0
    one = rng.integers(0, W, (N, 1, M)); one[:, 0, 0] = 0; one[:, 0, M - 1] = W - 1; mc[:, 4] = one; m[:, 4, 0] = 0; m[:, 4, B - 1] = M - 1
    gl[:, 5] = np.maximum(gl[:, 5], 1); goal = np.take_along_axis(gl[:, 5], m[:, 5][:, None, :], 2)
    c = rng.choice(np.array([0, QU - 1, QU, QU + 1, 16]), (N, 1, B)); place = np.argsort(np.argsort(rng.random((N, 16, B)), axis=1), axis=1)
    z[:, 5] = goal - (place >= c)
    ad[:, 6] = TH // 16; ad[:, 6, 15] = TH - 15 * (TH // 16) + rng.integers(-1, 2, (N, W))
    pr[:, 6] = np.maximum(pr[:, 6], 40); gl[:, 6] = np.maximum(gl[:, 6], 200); z[:, 6] = np.where(rng.random((N, 1, B)) < 0.7, 255, z[:, 6])
    pr[:, 7] = 255; gl[:, 7] = 255; z[:, 7] = 255 * rng.integers(0, 2, (N, 1, B)); wt[:, 7] = (255 * (np.arange(N) & 1)).reshape(N, 1, 1)
    return pack(d)
def setup_inputs_crowd(rng):
    d = parts(rng); pr, gl, z, m, dv, wt = [d[k] for k in ("pr", "gl", "z", "m", "dv", "wt")]
    gl[:, :6] = 0; m[:, :4] = np.argsort(rng.random((N, 4, M)), axis=-1)[..., :B]
    wt[:, :4] = 0; wt[:, :4, 0] = 1; wt[:, :4, 1] = 255
    c = np.full((N, 4, B), M - 1); c[:, 1, 0] = 0; c[:, 3] = rng.choice(np.array([0, 1, M // 2, M - 1]), (N, B))
    v = (c - 37 * m[:, :4]) & (M - 1); z[:, :4, 0] = v - 255 * (v // 255); z[:, :4, 1] = v // 255
    for i in range(N): gl[i, 2, :, m[i, 2, 0]] = 255
    z[:, 2, 2:, 0] = 100; dv[:, 2, :, :P] = 1
    for g in (4, 5):
        z[:, g] = z[:, g, :, :1].copy(); m[:, g] = m[:, g, :1].copy()
    z[:, 5, :, B - 1] = 255 - z[:, 5, :, 0]
    gl[:, 6] = 255
    pr[:, 7] = 255; gl[:, 7] = 255; z[:, 7] = 0; z[:, 7, :, B - 1] = 255; m[:, 7] = m[:, 7, :1].copy()
    return pack(d)
def setup_inputs_few(rng):
    d = parts(rng); d["z"] = np.minimum(d["z"], 254); d["dv"] = np.maximum(d["dv"], 1)
    mc, gl, z, m, wt = [d[k] for k in ("mc", "gl", "z", "m", "wt")]
    gl[1::2] = 255; z[1::2, 7, :, B - 1] = 255
    full = rng.permutation(np.array([0, 1, 3, 4]))
    for i in range(0, N, 2):
        g = int(full[(i // 2) & 3]); gl[i, g] = 0; m[i, g] = rng.permutation(M)[:B]
        wt[i, g] = 0; wt[i, g, 0] = 1; wt[i, g, 1] = 255
        a = rng.choice(np.array([11, 13, 23, 25, 27, 29]), B); u = W - 32 + a
        z[i, g, 1] = u // 255; z[i, g, 0] = u - 255 * (u // 255)
        mc[i, g, 15, m[i, g]] = W - 32 + ((-(a ** 7)) & 31)
    return pack(d)
def check_inputs(d):
    bad = []
    for k, hi in (("pr", 255), ("ad", 127), ("mc", W - 1), ("gl", 255), ("z0", 255), ("m0", M - 1), ("dv", 255), ("wt", 255)):
        a = np.asarray(d[k]).astype(np.float64)
        if not (np.min(a) >= 0 and np.max(a) <= hi): bad.append("range of " + k)
        elif np.any(a != np.floor(a)): bad.append("whole numbers of " + k)
    return bad
def reference(pr, ad, mc, gl, z0, m0, dv, wt):
    need_of, add_of, goal_of, z, dist, weight = [a.astype(np.float32).astype(np.int64).reshape(N, 8, 16, -1) for a in (pr, ad, gl, z0, dv, wt)]
    tb = mc.astype(np.int64).reshape(N, 8, 16, M); m = np.stack([gentries(a) for a in m0]).astype(np.int64)
    seen = [0] * N
    for t in range(T):
        for q in range(N):
            s = (q - t) % N; zz = z[s]; mm = m[s]
            o = np.take_along_axis(tb[q], mm[:, None, :], 2)
            ix = o.reshape(8, 1, 16 * B)
            p = np.take_along_axis(need_of[q], ix, 2).reshape(8, 16, 16, B); a = np.take_along_axis(add_of[q], ix, 2).reshape(8, 16, 16, B)
            K = [None] * 16 + [np.take_along_axis(goal_of[q], mm[:, None, :], 2)]
            for k in range(15, -1, -1): K[k] = np.maximum(p[:, :, k], K[k + 1] - a[:, :, k])
            K = np.stack(K)
            for j in range(P):
                met = np.add.reduce((zz[None] >= K).astype(np.int64), axis=2)
                best = np.max(np.where(met >= QU + (seen[q] & 1), np.arange(17).reshape(17, 1, 1), -1), axis=0)
                ak = np.take_along_axis(a, np.clip(best, 0, 15)[:, None, None, :], 2)[:, :, 0]
                new = np.abs(np.minimum(255, zz + ak) - dist[q, :, :, t * P + j][:, :, None])
                zz = np.where(((best >= 0) & (best < 16))[:, None, :], new, zz)
            goal = best == 16
            u = np.add.reduce(weight[q] * zz, axis=1) & (W - 1); to = (u + 37 * mm) & (M - 1)
            use = np.add.reduce(np.minimum(a, K[1:].transpose(1, 2, 0, 3)), axis=1)
            fresh = (((o * u[:, None, :]) >> 5) + o + 37 * np.arange(16).reshape(1, 16, 1)) & (W - 1)
            o = np.where(use < TH, fresh, o)
            for g in range(8):
                who = np.flatnonzero(goal[g]); where, first = np.unique(to[g, who], return_index=True)
                tb[q, g][:, where] = o[g][:, who[first]]
            z[s] = zz; m[s] = np.where(goal | (best < 0), to, mm); seen[q] = int(np.count_nonzero(goal))
    back = [(q - (T - 1)) % N for q in range(N)]
    return {"ymc": tb.reshape(N, 128, M).astype(np.float32), "yz": z[back].reshape(N, 128, B).astype(np.float32), "ym": np.stack([gtable(m[s]) for s in back]).astype(np.float32)}

@@ -1,0 +1,410 @@
+from concourse.mybir import dt, AluOpType as OP, AxisListType, ActivationFunctionType as AF
+
+F, H, I, U = "float32", "bfloat16", "int32", "uint16"
+SB = {
+    "MC": (1280, I), "MCF": (1280, F), "PR": (4096, H), "AD": (4096, H), "GL": (1024, H), "M0": (16, I),
+    "DV": (8, H), "WT": (1, H), "DH": (8, F), "DG": (1024, H), "OU": (256, U), "OF": (256, F), "Z": (256, H), "ZF": (256, F),
+    "KV": (144, F), "BASE": (8, F), "IOTA": (4096, F), "BT": (1280, H), "BTI": (1280, I), "YB": (256, H),
+    "ON": (256, H), "IDN": (128, H), "NID": (128, H), "I128": (128, H), "BLK": (128, H), "BLB": (128, H), "CST": (128, H), "CMB": (256, H),
+    "TH": (128, H), "MSK": (8, F), "PI": (1, I), "PR16": (1, I), "R16": (1, F), "R32": (1, F), "C37": (1, F), "PW": (1, F), "TM": (16, H), "GOB": (16, H),
+    "MI": (16, I), "MI2": (16, I), "MS": (16, U), "XU": (16, U), "UI": (16, I), "UI2": (16, I), "UU": (16, U), "XFU": (16, U),
+    "OG": (256, F), "PP": (256, I), "SS": (256, I), "TT": (256, I), "NW": (256, I), "JK": (256, H), "AC": (1, F), "AI": (1, I), "AP": (1, I), "AT": (1, F),
+}
+for _n in "I16 E16 PWR SX KD GO NN GN T36 BM MF CA CB UM YM XA X DM DVX DA DF XD XF".split(): SB[_n] = (16, F)
+for _h in "0123": SB["ZI" + _h], SB["MU" + _h] = (256, H), (16, U)
+for _h in "01":
+    for _n, _w, _d in (("G", 128, H), ("AB", 4112, H), ("PB", 4112, H), ("KB", 4096, H), ("KS", 144, F), ("KU", 8, U), ("VG", 128, H), ("SG", 128, H), ("T2", 128, H), ("R0", 128, H)):
+        SB[_n + _h] = (_w, _d)
+SCRATCH = {k: ("sbuf", [128, w], d) for k, (w, d) in SB.items()}
+for _h in "01":
+    SCRATCH["C" + _h] = ("sbuf", [128, 8, 16, 18], H)
+    for _x in "01": SCRATCH["BR" + _x + _h] = ("sbuf", [128, 8, 18], H)
+for _n in ("BD", "RM", "RMN", "RMC", "RMW"): SCRATCH[_n] = ("sbuf", [128, 16, 8, 16], H)
+for _b in range(8):
+    SCRATCH["P%d" % _b] = ("psum", [128, 512], F)
+LOADS = {"m0": 2.2, "mc": 4.5, "gl": 6, "z0": 6.5, "pr": 7, "ad": 9, "dv": 3, "wt": 3}
+SEMAPHORES = ["sV", "sA", "sT", "sG", "so0", "so1", "so2"] + ["ld_" + n for n in LOADS] + ["%s%d" % (n, t) for n in ("zi", "mi", "zl", "ml") for t in range(1, 4)]
+
+CYC, WAKE, CG, PF = 0.00104, 0.12, 1.56, 0.5
+NAS = (0, 8)
+CHS = (4, 4)
+EPS, DV = 0.1, 0.0
+OFF = "GG=-2.8 KD1=-8.8 AB10=-8 MCF=9.2 BASE=-3.2 AP=3 TH=-0.7 C1=-2.8 VG1=-3.6 XD=-5.7 AI=3.2 X10=8.9 MS=-1.8 UI=0.5 BTI=-3.7 BR=-2 RMC=-14.8 JK=-17.1 BLK=1 SS=-19.5 RMN=-18.9 C37=-4.4 AB13=-10.9 SX=-3.6 MU0=-12.1 DG=1.1 OF=1.3 TM=-0.1 G1=4.2 US1=3.9 AB01=-0.8"
+PIN = "VG0=V AB12=A AB11=A PB02=A AB02=A PB13=V PB01=V PB00=V AB03=V AB10=A"
+
+
+def build(T, topo, core, nxt):
+    ops, wr, rd, bk = [], {}, {}, {}
+
+    def op(eng, fn, reads, writes, cost, banks=(), done=None):
+        i = len(ops)
+        hard, soft = set(), set()
+        for k in reads:
+            if k in wr: hard.add(wr[k])
+        for k in writes:
+            if k in wr: hard.add(wr[k])
+            for r in rd.get(k, ()):
+                if r != i: (soft if ops[r]["eng"] == eng and len(eng) == 1 and ops[r]["done"] is None else hard).add(r)
+        for b in banks:
+            for r in bk.setdefault(b, []):
+                if ops[r]["eng"] != eng: hard.add(r)
+            bk[b].append(i)
+        for k in reads: rd.setdefault(k, []).append(i)
+        for k in writes:
+            wr[k] = i
+            rd[k] = []
+        ops.append({"eng": eng, "fn": fn, "hard": hard, "soft": soft - hard, "cost": cost, "done": done, "w": writes})
+
+    def V(fn, reads, writes, n, banks=(), f=1.0):
+        op("V", fn, reads, writes, max(64, n * f) * CYC + 0.02, banks)
+
+    def G(fn, reads, writes, cost):
+        op("G", fn, reads, writes, cost)
+
+    def copy(o, i, r, w, n, banks=(), f=1.0):
+        V(lambda q: q.tensor_copy(o, i), r, w, n, banks, f)
+
+    def ts(o, i, s1, o1, s2, o2, r, w, n, banks=(), f=1.0):
+        if o2 is None: V(lambda q: q.tensor_scalar(o, i, s1, None, o1), r, w, n, banks, f)
+        else: V(lambda q: q.tensor_scalar(o, i, s1, s2, o1, o2), r, w, n, banks, f)
+
+    def tt(o, a, b, f, r, w, n, banks=(), c=2.0):
+        V(lambda q: q.tensor_tensor(o, a, b, f), r, w, n, banks, c)
+
+    def act(o, i, func, r, w, n, banks=(), gather=False, **kw):
+        op("A", lambda q: q.activation(o, i, func, **kw), r, w, 0.08 + n * CG * CYC if gather else max(64, n) * CYC + 0.05, banks)
+
+    def gath(o, i, neg, r, w, n):
+        def fn(q, e):
+            if e == "A": return q.activation(o, i, AF.Copy, scale=-1.0 if neg else 1.0)
+            return q.tensor_scalar(o, i, -1.0, None, OP.mult) if neg else q.tensor_copy(o, i)
+        op("VA", fn, r, w, 0.08 + n * CG * CYC)
+
+    def fill(o, c, w, n):
+        V(lambda q: q.memset(o, c), [], [w], n, (), 0.5)
+
+    def mm(lst, r, w, n, banks):
+        def fn(q):
+            x = None
+            for (o, l, rr, s, e) in lst: x = q.matmul(o, l, rr, s, e)
+            return x
+        op("T", fn, r, w, n * CYC * PF + 0.05, banks)
+
+    def load(q, name, dst, key):
+        op(q, lambda e: e.dma_start(dst, T[name][:]), [], [key], 0.1, (), ("ld_" + name, 16, LOADS[name]))
+
+    load("S", "m0", T.M0[:], "M0"); load("S", "mc", T.MC[:, 0:1024], "MC"); load("S", "pr", T.PR[:], "PR"); load("S", "ad", T.AD[:], "AD")
+    load("A", "wt", T.WT[:], "WT"); load("A", "dv", T.DV[:], "DV"); load("A", "z0", T.ZI0[:], "ZI0"); load("A", "gl", T.GL[:], "GL")
+    fill(T.ON[:], 1.0, "ON", 256)
+    RM, imp = T.RM[:], {"allow_small_or_imprecise_dtypes": True}
+    G(lambda q: q.iota(T.PI[:], [[0, 1]], 0, 1), [], ["PI"], 0.2)
+    G(lambda q: q.iota(T.I16[:], [[1, 16]], 0, 0, **imp), [], ["I16"], 0.2)
+    G(lambda q: q.affine_select(T.IDN[:], T.ON[:, 0:128], [[-1, 128]], OP.is_equal, 0.0, 0, 1), ["ON"], ["IDN"], 0.5)
+    G(lambda q: q.affine_select(T.BLB[:], T.ON[:, 0:128], [[-16, 8], [0, 16]], OP.is_ge, 0.0, 0, 1), ["ON"], ["BLB"], 0.5)
+    G(lambda q: q.affine_select(T.BLK[:], T.BLB[:], [[16, 8], [0, 16]], OP.is_ge, 0.0, 15, -1), ["BLB"], ["BLK"], 0.5)
+    G(lambda q: q.iota(T.KV[:], [[512, 8], [2, 18]], 14, 0, **imp), [], ["KV"], 0.5)
+    G(lambda q: q.iota(T.SX[:], [[16, 16]], 1024, 0, **imp), [], ["SX"], 0.2)
+    G(lambda q: q.affine_select(T.CMB[:], T.ON[:], [[-1, 16], [1, 16]], OP.is_equal, 0.0, 0, 0), ["ON"], ["CMB"], 0.5)
+    G(lambda q: q.iota(T.IOTA[:], [[1, 4096]], 0, 0, **imp), ["BLK", "CMB", "IDN", "KV", "SX", "I16", "PI"], ["IOTA"], 8.0)
+    copy(T.MSK[:], T.BLK[:, 0:128:16], ["BLK"], ["MSK"], 8)
+    for x in range(8): ts(T.RM[:, :, x, :], T.CMB[:], T.MSK[:, x:x + 1], OP.mult, None, None, ["MSK", "CMB"], [("RM", x)], 256, (), 0.5)
+    RMK = [("RM", x) for x in range(8)]
+    for h in range(2):
+        AB, PB = T["AB%d" % h], T["PB%d" % h]
+        if h: act(AB[:, 15:4112:2], T.AB0[:, 15:4112:2], AF.Copy, ["ABo0"], ["ABo1"], 2049)
+        else:
+            fill(AB[:, 15:4112:2], 0.0, "ABo0", 2049)
+            fill(AB[:, 15:4112:32], -256.0, "ABo0", 129)
+        act(PB[:, 18:4112:2], T.AB0[:, 15:4108:2], AF.Copy, ["ABo0"], ["PBz%d" % h], 2047, scale=0.0)
+        fill(T["C%d" % h][:, :, :, 0], 1.0, ("C", h, 0), 128)
+    for h in range(2):
+        for x in range(2):
+            if NAS[h]: fill(T["BR%d%d" % (x, h)][:, :, 18 - NAS[h]:18], 2.0 - x, ("BR", h), 144)
+            fill(T["BR%d%d" % (x, h)][:, :, 0:18 - NAS[h]], 1.0 - x, ("BR", h), 144)
+    fill(T.CST[:], 2048.0, "CST", 128)
+    fill(T.TH[:], -1472.0, "TH", 128)
+    ts(T.PR16[:], T.PI[:], 15, OP.bitwise_and, None, None, ["PI"], ["PR16"], 1)
+    copy(T.R16[:], T.PR16[:], ["PR16"], ["R16"], 1)
+    ts(T.R32[:], T.R16[:], 32.0, OP.mult, None, None, ["R16"], ["R32"], 1)
+    ts(T.C37[:], T.R16[:], 37.0, OP.mult, None, None, ["R16"], ["C37"], 1)
+    ts(T.KV[:], T.KV[:], T.R32[:, 0:1], OP.add, None, None, ["R32", "KV"], ["KV"], 144)
+    ts(T.KV[:, 0:144:18], T.KV[:, 0:144:18], 1.0, OP.add, None, None, ["KV"], ["KV"], 8)
+    ts(T.KV[:, 17:144:18], T.KV[:, 17:144:18], -1.0, OP.add, None, None, ["KV"], ["KV"], 8)
+    ts(T.BASE[:], T.KV[:, 0:144:18], 1.0, OP.add, None, None, ["KV"], ["BASE"], 8)
+    ts(T.SX[:], T.SX[:], T.R16[:, 0:1], OP.add, None, None, ["R16", "SX"], ["SX"], 16)
+    ts(T.E16[:], T.I16[:], T.R16[:, 0:1], OP.is_equal, None, None, ["R16", "I16"], ["E16"], 16)
+    ts(T.TM[:], T.I16[:], T.R16[:, 0:1], OP.is_ge, -64.0, OP.mult, ["R16", "I16"], ["TM"], 16)
+    for b in range(16): fill(T.PWR[:, b:b + 1], 2.0 ** -b, ("PWR", b), 1)
+    tt(T.E16[:], T.E16[:], T.PWR[:], OP.mult, ["E16"] + [("PWR", b) for b in range(16)], ["E16"], 16)
+    V(lambda q: q.tensor_reduce(T.PW[:], T.E16[:], AxisListType.X, OP.add), ["E16"], ["PW"], 16)
+    ts(T.BTI[:], T.IOTA[:, 0:1280], T.PW[:, 0:1], OP.mult, -0.5 + 2.0 ** -13, OP.add, ["IOTA", "PW"], ["BTI"], 1280)
+    ts(T.BTI[:], T.BTI[:], 1, OP.bitwise_and, None, None, ["BTI"], ["BTI"], 1280)
+    ts(T.BT[:], T.BTI[:], 2.0, OP.mult, -1.0, OP.add, ["BTI"], ["BT"], 1280)
+    ts(T.NID[:], T.IDN[:], -1.0, OP.mult, None, None, ["IDN"], ["NID"], 128, (), 0.5)
+    ts(T.I128[:], T.IDN[:], 128.0, OP.mult, None, None, ["IDN"], ["I128"], 128, (), 0.5)
+    act(T.RMC[:], RM, AF.Copy, RMK, ["RMC"], 2048, scale=16384.0)
+    act(T.RMN[:], RM, AF.Copy, RMK, ["RMN"], 2048, scale=-1.0)
+    ts(T.RMW[:], RM, T.WT[:, 0:1], OP.mult, None, None, RMK + ["WT"], ["RMW"], 2048, (), 0.5)
+    ts(T.DH[:], T.DV[:], -0.5, OP.mult, None, None, ["DV"], ["DH"], 8)
+    for j in range(8):
+        ts(T.DG[:, 128 * j:128 * j + 128], T.IDN[:], T.DH[:, j:j + 1], OP.mult, None, None, ["IDN", "DH"], [("DG", j)], 128, (), 0.5)
+    copy(T.MU0[:], T.M0[:], ["M0"], ["MU0"], 16)
+
+    for t in range(4):
+        ZI, MU = T["ZI%d" % t], T["MU%d" % t]
+        zk, mk = "ZI%d" % t, "MU%d" % t
+        if t:
+            nw = len(topo.engines(core, nxt))
+            op("", None, [zk + "s"], [zk], 0, (), ("zi%d" % t, nw, 3.0))
+            op("", None, [mk + "s"], [mk], 0, (), ("mi%d" % t, nw, 3.0))
+        for h in range(2):
+            a = 128 * h
+            copy(T.OU[:, a:a + 128], T.MC[:, 0:1024].indirect(MU[:, 8 * h:8 * h + 8]), ["MC", mk], [("OU", h)], 128, (), CG)
+            act(T["G%d" % h][:], T.GL[:].indirect(MU[:, 8 * h:8 * h + 8]), AF.Copy, ["GL", mk], ["G%d" % h], 128, gather=True)
+        copy(T.MF[:], MU[:], [mk], ["MF"], 16)
+        for h in range(2):
+            Zb, Xb, Eb = T["P%d" % h], T["P%d" % (2 + h)], T["P%d" % (6 + h)]
+            AB, PB, KB, C = T["AB%d" % h], T["PB%d" % h], T["KB%d" % h], T["C%d" % h]
+            KS, KU, vg, sg, T2, R0, G_ = [T[n + str(h)] for n in ("KS", "KU", "VG", "SG", "T2", "R0", "G")]
+            a, b, ch, NA = 128 * h, 128 * h + 128, CHS[h], NAS[h]
+            mm([(Zb[:, 0:128], T.IDN[:], ZI[:, a:b], True, True)], [zk, "IDN"], ["ZP%d" % h], 128, [h])
+            n = 128 // ch
+            for c in range(ch):
+                lo, s0 = 32 * n * c, a + n * c
+                gath(PB[:, 15 + lo:15 + lo + 32 * n:2], T.PR[:].indirect(T.OU[:, s0:s0 + n]), False, ["PR", ("OU", h)], [("PB", h, c)], 16 * n)
+                gath(AB[:, 16 + lo:16 + lo + 32 * n:2], T.AD[:].indirect(T.OU[:, s0:s0 + n]), True, ["AD", ("OU", h)], [("AB", h, c)], 16 * n)
+            pk, ak = [("PB", h, c) for c in range(ch)], [("AB", h, c) for c in range(ch)]
+            copy(PB[:, 16:4112:32], PB[:, 15:4111:32], pk + ["PBz%d" % h], ["P0%d" % h], 128, (), 0.5)
+            copy(PB[:, 47:4112:32], G_[:], ["G%d" % h, "P0%d" % h], pk, 128, (), 0.5)
+            V(lambda q, KB=KB, AB=AB, PB=PB: q.tensor_tensor_scan(KB[:, ::-1], AB[:, 4111:15:-1], PB[:, 4111:15:-1], 0.0, OP.add, OP.max),
+              pk + ak + ["P0%d" % h, "PBz%d" % h, "ABo%d" % h], ["KB%d" % h], 4096, (), 0.5)
+            mm([(Eb[:, 0:128], T.IDN[:], KB[:, 1:4096:32], True, False), (Eb[:, 0:128], T.IDN[:], AB[:, 16:4112:32], False, True)],
+               ["IDN", "KB%d" % h] + ak, ["E0%d" % h], 256, [6 + h])
+            act(R0[:], Eb[:, 0:128], AF.Relu, ["E0%d" % h], ["R0%d" % h], 128, [6 + h])
+            us = T["P%d" % (4 + h)][:, 384 * h:384 * h + 128]
+            for k in range(16):
+                if k % 4 == 0: lst = []
+                lst.append((us, T.RM[:, k, :, :], KB[:, 2 * k + 1:4096:32], k == 0, False))
+                lst.append((us, T.RMN[:, k, :, :], KB[:, 2 * k:4096:32] if k else R0[:], False, k == 15))
+                if k % 4 == 3: mm(lst, RMK + ["RMN", "KB%d" % h, "R0%d" % h, ("UO", h, k)], [("US", h, k), ("UO", h, k - 4)], 8 * 128, [4 + h])
+            zsrc, zkey = ZI[:, a:b], zk
+            kpos = [2 * k - 1 if k else 0 for k in range(17)]
+            for j in range(2):
+                for B, bank, ks in ((T.P7, 7, range(17 - NA, 17 - NA + min(4, NA))), (T.P6, 6, range(17 - NA + min(4, NA), 17))):
+                    if not ks: continue
+                    lst = []
+                    for i, k in enumerate(ks):
+                        lst.append((B[:, 128 * i:128 * i + 128], T.IDN[:], zsrc, True, False))
+                        lst.append((B[:, 128 * i:128 * i + 128], T.NID[:], KB[:, kpos[k]:4096:32], False, True))
+                    mm(lst, ["IDN", "NID", zkey, "KB%d" % h], [("D", h, bank)], 128 * len(lst), [bank])
+                    for i, k in enumerate(ks):
+                        act(C[:, :, :, k + 1], B[:, 128 * i:128 * i + 128], AF.Sign, [("D", h, bank)], [("C", h, k + 1)], 128, [bank], bias=0.5)
+                for k in range(17 - NA):
+                    tt(C[:, :, :, k + 1], KB[:, kpos[k]:4096:32], Zb[:, 0:128], OP.is_le, ["KB%d" % h, "ZP%d" % h], [("C", h, k + 1)], 128, [h], 1.0)
+                cp = Xb[:, 0:144]
+                lst = [(cp, T.TH[:], T["BR0%d" % h][:], True, False)] + ([(cp, T.CST[:], T["BR1%d" % h][:], False, False)] if NA else [])
+                lst += [(cp, T.RMC[:, r, :, :], C[:, :, r, :], False, r == 15) for r in range(16)]
+                mm(lst, [("C", h, k) for k in range(18)] + [("BR", h)] + ["RMC", "CST", "TH"], ["CP%d" % h], 18 * 144, [2 + h])
+                V(lambda q, KS=KS, cp=cp: q.tensor_tensor_scan(KS[:], cp, T.KV[:], 0.0, OP.max, OP.min), ["CP%d" % h, "KV"], ["KS%d" % h], 144, [2 + h])
+                copy(KU[:], KS[:, 17:144:18], ["KS%d" % h], ["KU%d" % h], 8)
+                abk = ak + ["ABo%d" % h, "KU%d" % h]
+                act(sg[:], AB[:].indirect(KU[:]), AF.Sign, abk, ["SG%d" % h], 128, gather=True, bias=192.0)
+                gath(vg[:], AB[:].indirect(KU[:]), False, abk, ["VG%d" % h], 128)
+                xs, dj = Xb[:, 144:272], 2 * t + j
+                mm([(xs, T.IDN[:], zsrc, True, False), (xs, T.NID[:], vg[:], False, False), (xs, T.I128[:], sg[:], False, True)],
+                   [zkey, "IDN", "NID", "I128", "VG%d" % h, "SG%d" % h], ["X1%d" % h], 384, [2 + h])
+                ts(T2[:], xs, 383.0, OP.min, 128.0, OP.subtract, ["X1%d" % h], ["T2%d" % h], 128, [2 + h])
+                mm([(xs, T.IDN[:], T2[:], True, False), (xs, T.DG[:, 128 * dj:128 * dj + 128], sg[:], False, True)],
+                   ["IDN", ("DG", dj), "T2%d" % h, "SG%d" % h], ["X1%d" % h], 256, [2 + h])
+                bias, xr = T.DH[:, dj:dj + 1], ["X1%d" % h, "DH"]
+                if j == 0: act(Zb[:, 0:128], xs, AF.Abs, xr, ["ZP%d" % h], 128, [h, 2 + h], bias=bias)
+                act(T.Z[:, a:b], xs, AF.Abs, xr, ["Z%d" % h], 128, [2 + h], bias=bias)
+                if t == 3 and j == 1: act(T.ZF[:, a:b], xs, AF.Abs, xr, ["ZF%d" % h], 128, [2 + h], bias=bias)
+                zsrc, zkey = T.Z[:, a:b], "Z%d" % h
+            ul = T.P2[:, 400 + 8 * h:408 + 8 * h]
+            mm([(ul, T.RMW[:, r, :, :], T.Z[:, a + r:b:16], r == 0, r == 15) for r in range(16)], ["RMW", "Z%d" % h], [("UL", h)], 1024, [2])
+            tt(T.KD[:, 8 * h:8 * h + 8], KS[:, 17:144:18], T.BASE[:], OP.subtract, ["KS%d" % h, "BASE"], [("KD", h)], 8)
+
+        def send(q, src, name, sem):
+            rid, pid, _ = topo.addr(nxt)
+            q.remote_dma(T[name][:], src[:], T.sem[sem % "i"], T.sem[sem % "l"], pid, rid, topo.mask(core, nxt))
+        n1, ne = t + 1, len(topo.engines(core, nxt))
+        if t < 3:
+            op("G", lambda q, n1=n1: send(q, T.Z, "ZI%d" % n1, "z%%s%d" % n1), ["Z0", "Z1"], ["ZI%ds" % n1], 0.5, (), ("zl%d" % n1, ne, 2.0))
+        KDK, ULK = [("KD", 0), ("KD", 1)], [("UL", 0), ("UL", 1)]
+        copy(T.OF[:], T.OU[:], [("OU", 0), ("OU", 1)], ["OF"], 256)
+        for h in range(2):
+            us, a, uk = T["P%d" % (4 + h)][:, 384 * h:384 * h + 128], 128 * h, [("US", h, k) for k in (3, 7, 11, 15)]
+            ts(T.P4[:, 128 + a:256 + a], us, 254.0, OP.is_lt, None, None, uk, [("GG", h)], 128, [4, 5])
+            ts(T.P5[:, a:a + 128], us, 254.0, OP.is_lt, T.C37[:, 0:1], OP.mult, uk + ["C37"], [("W0", h)], 128, [4, 5])
+        tt(T.OG[:], T.OF[:], T.P4[:, 128:384], OP.mult, ["OF", ("GG", 0), ("GG", 1)], ["OG"], 256, [4], 1.0)
+        tt(T.P5[:, 0:256], T.OF[:], T.P5[:, 0:256], OP.add, ["OF", ("W0", 0), ("W0", 1)], ["W1"], 256, [5], 1.0)
+        ts(T.GO[:], T.KD[:], 31.0, OP.is_equal, None, None, KDK, ["GO"], 16)
+        ts(T.NN[:], T.KD[:], 0.0, OP.is_lt, None, None, KDK, ["NN"], 16)
+        tt(T.GN[:], T.GO[:], T.NN[:], OP.add, ["GO", "NN"], ["GN"], 16)
+        ts(T.T36[:], T.GN[:], 36.0, OP.mult, 1.0, OP.add, ["GN"], ["T36"], 16)
+        tt(T.BM[:], T.T36[:], T.MF[:], OP.mult, ["T36", "MF"], ["BM"], 16)
+        ts(T.CA[:], T.GO[:], -1.0, OP.mult, 1.0, OP.add, ["GO"], ["CA"], 16)
+        tt(T.CB[:], T.CA[:], T.SX[:], OP.mult, ["CA", "SX"], ["CB"], 16)
+        UL = T.P2[:, 400:416]
+        tt(T.UM[:], T.GN[:], UL, OP.mult, ULK + ["GN"], ["UM"], 16, [2])
+        copy(T.UI[:], UL, ULK, ["UI"], 16, [2])
+        tt(T.MI[:], T.UM[:], T.BM[:], OP.add, ["UM", "BM"], ["MI"], 16)
+        ts(T.MI2[:], T.MI[:], 1023, OP.bitwise_and, None, None, ["MI"], ["MI2"], 16)
+        if t < 3:
+            copy(T.MS[:], T.MI2[:], ["MI2"], ["MS"], 16)
+            op("G", lambda q, n1=n1: send(q, T.MS, "MU%d" % n1, "m%%s%d" % n1), ["MS"], ["MU%ds" % n1], 0.5, (), ("ml%d" % n1, ne, 2.0))
+        else:
+            copy(T.YM[:], T.MI2[:], ["MI2"], ["YM"], 16)
+        tt(T.XA[:], T.MI2[:], T.GO[:], OP.mult, ["MI2", "GO"], ["XA"], 16)
+        tt(T.X[:], T.XA[:], T.CB[:], OP.add, ["XA", "CB"], ["X"], 16)
+        copy(T.XU[:], T.X[:], ["X"], ["XU"], 16)
+        ts(T.UI2[:], T.UI[:], 4095, OP.bitwise_and, None, None, ["UI"], ["UI2"], 16)
+        copy(T.UU[:], T.UI2[:], ["UI2"], ["UU"], 16)
+        tt(T.DM[:], T.SX[:], T.X[:], OP.subtract, ["SX", "X"], ["DM"], 16)
+        act(T.YB[:], T.BT[:].indirect(T.XU[:]), AF.Copy, ["BT", "XU"], ["YB"], 256, gather=True)
+        for gg in range(8):
+            if gg in (1, 4, 7): act(T.BD[:, :, gg, :], T.YB[:], AF.Copy, ["YB", "MSK"], [("BD", gg)], 256, scale=T.MSK[:, gg:gg + 1])
+            else: ts(T.BD[:, :, gg, :], T.YB[:], T.MSK[:, gg:gg + 1], OP.mult, None, None, ["YB", "MSK"], [("BD", gg)], 256, (), 0.5)
+        for cs, bank in (((14, 15), 1), ((12, 13), 3), ((10, 11), 0), ((7, 8, 9), 7), ((0, 1, 2, 3, 4, 5, 6), 6)):
+            off, P, lst, red = 0, T["P%d" % bank], [], []
+            for c in cs:
+                lh, nn = T.BD[:, c, :, :], 16 * c + 16
+                if c: lst.append((P[:, off:off + 16 * c], lh, T.YB[:, 0:16 * c], True, True))
+                lst.append((P[:, off + 16 * c:off + nn], lh, T.YB[:, 16 * c:nn], True, False))
+                lst.append((P[:, off + 16 * c:off + nn], T.IDN[:], T.TM[:], False, True))
+                red.append((c, off, nn))
+                off += nn
+            mm(lst, [("BD", gg) for gg in range(8)] + ["YB", "IDN", "TM"], [("E", bank)], off + 100 * len(cs), [bank])
+            for c, o, nn in red:
+                if c < 10: V(lambda q, c=c, o=o, nn=nn, P=P: q.tensor_reduce(T.DVX[:, c:c + 1], P[:, o:o + nn], AxisListType.X, OP.max), [("E", bank)], [("DF", c)], nn, [bank])
+                else: act(T.JK[:, 0:nn], P[:, o:o + nn], AF.Relu, [("E", bank)], ["JK", ("DF", c)], nn, [bank], bias=-15.0, accum_out=T.DA[:, c:c + 1])
+        ts(T.DF[:, 0:10], T.DVX[:, 0:10], 15.5, OP.is_ge, None, None, [("DF", c) for c in range(10)], ["DF0"], 10)
+        ts(T.DF[:, 10:16], T.DA[:, 10:16], 0.5, OP.is_ge, None, None, [("DF", c) for c in range(10, 16)], ["DF1"], 6)
+        tt(T.XD[:], T.DF[:], T.DM[:], OP.mult, ["DF0", "DF1", "DM"], ["XD"], 16)
+        tt(T.XF[:], T.XD[:], T.X[:], OP.add, ["XD", "X"], ["XF"], 16)
+        copy(T.XFU[:], T.XF[:], ["XF"], ["XFU"], 16)
+        V(lambda q: q.tensor_tensor(T.PP[:], T.IOTA[:].indirect(T.UU[:]), T.OG[:], OP.mult), ["IOTA", "UU", "OG"], ["PP"], 256, (), CG)
+        ts(T.SS[:], T.PP[:], 5, OP.arith_shift_right, None, None, ["PP"], ["SS"], 256)
+        tt(T.TT[:], T.SS[:], T.P5[:, 0:256], OP.add, ["SS", "W1"], ["TT"], 256, [5], 1.0)
+        ts(T.NW[:], T.TT[:], 4095, OP.bitwise_and, None, None, ["TT"], ["NW"], 256)
+        if t < 3:
+            copy(T.MC[:].indirect(T.XFU[:]), T.NW[:], ["NW", "XFU"], ["MC"], 256, (), 3.8)
+            ts(T.GOB[:], T.KD[:], 31.0, OP.is_equal, None, None, KDK, ["GOB"], 16)
+            mm([(T.P7[:, 496:512], T.ON[:, 0:128], T.GOB[:], True, True)], ["ON", "GOB"], ["APS"], 64, [7])
+            V(lambda q: q.tensor_reduce(T.AC[:], T.P7[:, 496:512], AxisListType.X, OP.add), ["APS"], ["AC"], 16, [7])
+            copy(T.AI[:], T.AC[:], ["AC"], ["AI"], 1)
+            ts(T.AP[:], T.AI[:], 1, OP.bitwise_and, None, None, ["AI"], ["AP"], 1)
+            ts(T.AT[:], T.AP[:], -128.0, OP.mult, -1472.0, OP.add, ["AP"], ["AT"], 1)
+            ts(T.TH[:], T.ON[:, 0:128], T.AT[:, 0:1], OP.mult, None, None, ["ON", "AT"], ["TH"], 128, (), 0.5)
+        else:
+            copy(T.MCF[:, 0:1024], T.MC[:, 0:1024], ["MC"], ["MCF"], 1024)
+            copy(T.MCF[:].indirect(T.XFU[:]), T.NW[:], ["NW", "XFU"], ["MCF"], 256, (), 3.8)
+            op("S", lambda q: q.dma_start(T.yz[:], T.ZF[:]), ["ZF0", "ZF1"], [], 0.1, (), ("so0", 16, 2))
+            op("S", lambda q: q.dma_start(T.ym[:], T.YM[:]), ["YM"], [], 0.1, (), ("so1", 16, 2))
+            op("S", lambda q: q.dma_start(T.ymc[:], T.MCF[:, 0:1024]), ["MCF"], [], 0.1, (), ("so2", 16, 4))
+    return ops
+
+
+def name_of(o):
+    w = o["w"][0] if o["w"] else "out"
+    if not isinstance(w, tuple): return w
+    piece = w[0] in ("PB", "AB")
+    return w[0] + (str(w[1]) if piece or w[0] in ("C", "OU", "US", "UL", "KD", "D") else "") + (str(w[2]) if piece else "")
+
+
+def schedule(ops):
+    off = {k: float(v) for k, v in (x.split("=") for x in OFF.split())}
+    pin = dict(x.split("=") for x in PIN.split())
+    n = len(ops)
+    kids = [[] for _ in ops]
+    need = [0] * n
+    for i, o in enumerate(ops):
+        for d in o["hard"] | o["soft"]:
+            kids[d].append(i)
+            need[i] += 1
+    lat = [o["done"][2] if o["done"] else o["cost"] for o in ops]
+    prio = [0.0] * n
+    for i in range(n - 1, -1, -1):
+        prio[i] = lat[i] + 0.08 + max([prio[k] for k in kids[i]] + [0.0])
+    prio = [p + off.get(name_of(o), 0.0) for p, o in zip(prio, ops)]
+    for o in ops:
+        if len(o["eng"]) > 1: o["cand"] = pin.get(name_of(o), o["eng"])
+        else: o["cand"] = o["eng"]
+    free, fin, start, est = dict.fromkeys("VATGS", 0.0), [0.0] * n, [0.0] * n, [0.0] * n
+    ready = [i for i in range(n) if need[i] == 0]
+    order = []
+    while ready:
+        beg = []
+        for i in ready:
+            e = ops[i]["cand"]
+            beg.append(est[i] if not e else max(est[i], free[e]) if len(e) == 1 else max(est[i], min(free["V"] + DV, free["A"])))
+        m = min(beg) + EPS
+        best = None
+        for i, b in zip(ready, beg):
+            if b <= m and (best is None or prio[i] > prio[best[0]]): best = (i, b)
+        i, b = best
+        o = ops[i]
+        ready.remove(i)
+        e = o["cand"]
+        if len(e) > 1: e = "V" if free["V"] + DV <= free["A"] else "A"
+        if len(o["eng"]) > 1: o["fn"] = (lambda f, e: lambda q: f(q, e))(o["fn"], e)
+        o["eng"] = o["cand"] = e
+        if e:
+            b = max(est[i], free[e])
+            free[e] = b + o["cost"]
+        start[i], fin[i] = b, b + lat[i]
+        order.append(i)
+        for k in kids[i]:
+            need[k] -= 1
+            w = 0.06 if ops[k]["cand"] == e else WAKE
+            est[k] = max(est[k], fin[i] + w if i in ops[k]["hard"] else start[i])
+            if need[k] == 0: ready.append(k)
+    return order, start, fin
+
+
+def rank_program(g, core, T, topo):
+    rank = T.rank_of(core)
+    if rank is None:
+        return
+    nxt = T.cores[(rank + 1) % len(T.cores)]
+    ops = build(T, topo, core, nxt)
+    order, _, _ = schedule(ops)
+    Q = {"V": g.vector, "A": g.scalar, "T": g.tensor, "G": g, "S": g.sync}
+    cnt = {e: 0 for e in Q}
+    done, know = {}, {}
+    known = {e: {} for e in Q}
+    for i in order:
+        o = ops[i]
+        e = o["eng"]
+        if not e:
+            done[i] = o["done"][:2]
+            know[i] = {done[i][0]: done[i][1]}
+            continue
+        kn = known[e]
+        wants = {}
+        for d in o["hard"]:
+            s, v = done[d]
+            if kn.get(s, 0) < v and wants.get(s, (0, 0))[0] < v: wants[s] = (v, d)
+        for s in sorted(wants, key=lambda s: -wants[s][1]):
+            v, d = wants[s]
+            if kn.get(s, 0) >= v: continue
+            Q[e].wait_ge(T.sem[s], v)
+            for a, b in know[d].items():
+                if kn.get(a, 0) < b: kn[a] = b
+        x = o["fn"](Q[e])
+        if o["done"]:
+            done[i] = o["done"][:2]
+            if x is not None: x.then_inc(T.sem[done[i][0]], done[i][1])
+        else:
+            cnt[e] += 1
+            done[i] = ("s" + e, cnt[e])
+            x.then_inc(T.sem["s" + e], 1)
+        know[i] = dict(kn)
+        know[i][done[i][0]] = done[i][1]
+    kn = known["S"]
+    for i in reversed(order):
+        s, v = done[i]
+        if kn.get(s, 0) < v:
+            g.sync.wait_ge(T.sem[s], v)
+            kn[s] = v

@@ -1,364 +1,369 @@
-from concourse.mybir import dt, AluOpType as OP, AxisListType, ActivationFunctionType as AF
+import numpy as np
+from concourse.mybir import AluOpType as OP, ActivationFunctionType as AF
 
 F, H, I, U = "float32", "bfloat16", "int32", "uint16"
-SB = {
-    "MC": (1280, I), "MCF": (1280, F), "PR": (4096, H), "AD": (4096, H), "GL": (1024, H), "M0": (16, I),
-    "DV": (8, H), "WT": (1, H), "DH": (8, F), "DG": (1024, H), "OU": (256, U), "OF": (256, F), "Z": (256, H), "ZF": (256, F),
-    "KV": (144, F), "BASE": (8, F), "IOTA": (4096, F), "BT": (1280, H), "BTI": (1280, I), "YB": (256, H),
-    "ON": (256, H), "IDN": (128, H), "NID": (128, H), "I128": (128, H), "BLK": (128, H), "BLB": (128, H), "CST": (128, H), "CMB": (256, H),
-    "TH": (128, H), "MSK": (8, F), "PI": (1, I), "PR16": (1, I), "R16": (1, F), "R32": (1, F), "C37": (1, F), "PW": (1, F), "TM": (16, H), "GOB": (16, H),
-    "MI": (16, I), "MI2": (16, I), "MS": (16, U), "XU": (16, U), "UI": (16, I), "UI2": (16, I), "UU": (16, U), "XFU": (16, U),
-    "OG": (256, F), "PP": (256, I), "SS": (256, I), "TT": (256, I), "NW": (256, I), "JK": (256, H), "AC": (1, F), "AI": (1, I), "AP": (1, I), "AT": (1, F),
-}
-for _n in "I16 E16 PWR SX KD GO NN GN T36 BM MF CA CB UM YM XA X DM DVX DA DF XD XF".split(): SB[_n] = (16, F)
+S = np.s_
+SB = {"MCI": (1024, I), "MC": (1040, F), "PR": (4096, H), "AD": (4096, H), "GL": (1024, H), "M0": (16, I), "DV": (8, H), "WT": (1, H),
+      "DVF": (8, F), "WS": (1, F), "W4": (1, F), "OU": (256, U), "NO": (256, F), "O32": (256, F), "Z": (256, H), "ZF": (256, F), "MS": (16, U), "YM": (16, F),
+      "KV": (144, F), "IOTA": (1024, F), "VB": (4128, H), "ON": (2048, H), "NON": (128, H), "IDN": (128, H), "NID": (128, H), "BLK": (128, H), "BLB": (128, H),
+      "BW": (128, H), "BW4": (128, H), "BN": (128, H), "CMB": (256, H), "PM": (128, H), "MSK": (8, F), "PI": (1, I), "PR16": (1, I), "R16": (1, F), "R32": (1, F),
+      "C37": (1, F), "SPR": (1, F), "I16": (128, F), "CI": (8, F), "CL": (8, U), "RS": (128, H), "BN0": (136, H), "BN1": (136, H),
+      "E": (2048, H), "NG": (16, H), "JK": (16, F), "AC": (1, F), "RY": (1, F), "M4": (16, F)}
 for _h in "0123": SB["ZI" + _h], SB["MU" + _h] = (256, H), (16, U)
 for _h in "01":
-    for _n, _w, _d in (("G", 128, H), ("AB", 4112, H), ("PB", 4112, H), ("KB", 4096, H), ("KS", 144, F), ("KU", 8, U), ("VG", 128, H), ("SG", 128, H), ("T2", 128, H), ("R0", 128, H)):
+    for _n, _w, _d in (("AB", 4128, H), ("PB", 4112, H), ("KB", 4096, H), ("KS", 144, F), ("KU", 8, U), ("VG", 128, H), ("DG", 128, H), ("R0", 128, H),
+                       ("Y", 128, H), ("ZT", 128, H), ("Z1", 128, H), ("M37", 264, F), ("MI", 264, I), ("UI", 264, I), ("X", 136, F), ("NE", 128, H), ("SC", 128, H),
+                       ("T2", 8, F), ("XF", 16, U), ("W", 128, F), ("XP", 128, I), ("NW", 128, I), ("D0", 8, F), ("DM", 8, F), ("NN", 8, F), ("TQ", 8, F), ("MN", 8, F)):
         SB[_n + _h] = (_w, _d)
 SCRATCH = {k: ("sbuf", [128, w], d) for k, (w, d) in SB.items()}
-for _h in "01":
-    SCRATCH["C" + _h] = ("sbuf", [128, 8, 16, 18], H)
-    for _x in "01": SCRATCH["BR" + _x + _h] = ("sbuf", [128, 8, 18], H)
-for _n in ("BD", "RM", "RMN", "RMC", "RMW"): SCRATCH[_n] = ("sbuf", [128, 16, 8, 16], H)
-for _b in range(8):
-    SCRATCH["P%d" % _b] = ("psum", [128, 512], F)
-LOADS = {"m0": 2.2, "mc": 4.5, "gl": 6, "z0": 6.5, "pr": 7, "ad": 9, "dv": 3, "wt": 3}
-SEMAPHORES = ["sV", "sA", "sT", "sG", "so0", "so1", "so2"] + ["ld_" + n for n in LOADS] + ["%s%d" % (n, t) for n in ("zi", "mi", "zl", "ml") for t in range(1, 4)]
+for _h in "01": SCRATCH["C" + _h] = ("sbuf", [128, 128, 18], H)
+for _n in ("RMC", "RMN", "RMW"): SCRATCH[_n] = ("sbuf", [128, 16, 8, 16], H)
+SCRATCH["BR"] = ("sbuf", [128, 8, 8, 18], H)
+for _b in range(8): SCRATCH["P%d" % _b] = ("psum", [128, 512], F)
+LOADS = (("S", "m0", "M0", 2.0), ("S", "mc", "MCI", 4.0), ("S", "pr", "PR", 6.5), ("S", "ad", "AD", 8.5), ("S", "gl", "GL", 9.2), ("S", "z0", "ZI0", 9.5),
+         ("A", "wt", "WT", 2.5), ("A", "dv", "DV", 2.5))
+SEMAPHORES = ["sV", "sA", "sT", "sG", "so0", "so1", "so2"] + ["ld_" + x[1] for x in LOADS] + ["%s%d%d" % (n, t, h) for n in ("zi", "mi", "zl", "ml") for t in range(1, 4) for h in range(2)]
 
-CYC, WAKE, CG, PF = 0.00104, 0.12, 1.56, 0.5
-NAS = (0, 8)
-CHS = (4, 4)
-EPS, DV = 0.1, 0.0
-OFF = "GG=-2.8 KD1=-8.8 AB10=-8 MCF=9.2 BASE=-3.2 AP=3 TH=-0.7 C1=-2.8 VG1=-3.6 XD=-5.7 AI=3.2 X10=8.9 MS=-1.8 UI=0.5 BTI=-3.7 BR=-2 RMC=-14.8 JK=-17.1 BLK=1 SS=-19.5 RMN=-18.9 C37=-4.4 AB13=-10.9 SX=-3.6 MU0=-12.1 DG=1.1 OF=1.3 TM=-0.1 G1=4.2 US1=3.9 AB01=-0.8"
-PIN = "VG0=V AB12=A AB11=A PB02=A AB02=A PB13=V PB01=V PB00=V AB03=V AB10=A"
+BIG, TOP, MAGIC = 2.0 ** 25, 2.0 ** 23, 1.5 * 2.0 ** 23
+PAR = {
+    "cyc": 0.00087, "ovV": 0.045, "ovA": 0.06, "ovT": 0.03, "wake": 0.1, "own": 0.06, "cg": 1.56, "cs": 3.8, "pf": 0.5, "far": 2.0, "eps": 0.1,
+    "kind": {(0, 1): "VVAV", (1, 1): "AAAA", (0, 0): "VVVA", (1, 0): "AAAA"},
+    "one": {(0, 1): "V", (1, 1): "A", (0, 0): "A", (1, 0): "V"},
+    "pieces": 2, "dbanks": (0, 1, 2), "period": 20.0,
+}
+TAU = ("send=-1.3 G0=-1.2 a10=-0.7 OU1=-0.5 dma=-0.4 p10=0.1 p11=1 G1=1.2 zt0=1.3 VG10=1.9 PP0=2.2 ZT10=2.3 OU0=2.4 ZT1=2.9 c010=2.9 zt1=3.3 n11=3.4 K1=3.9 c10m=4 p00=4.1 n10=4.3 a11=4.7 P00=4.9 e01=4.9 P01=5.1 c10=5.2 put0=5.2 d010=5.4 ZT0=5.7 x11=5.7 p01=6 KU00=6 Z10=6 a00=6.1 a01=6.1 Y0=6.2 K0=6.5 DG10=6.6 x10=6.8 NO1=7 KU10=7.1 KS00=7.2 Z11=7.5 KS10=7.7 xt1=7.7 n00=7.9 c00m=8.1 x00=8.1 d001=8.3 d000=8.4 ZT11=8.5 Ml1=8.6 us1=8.7 Mb1=8.7 NG1=8.8 T20=8.8 XP0=8.8 W01=9 c00=9.1 d011=9.1 KS11=9.2 VG11=9.2 X0=9.2 OG0=9.4 Y1=9.5 O321=9.6 XF1=9.6 OG1=9.7 ub1=9.8 VG00=10 R01=10.1 xt0=10.1 xb1=10.6 xl1=10.7 M41=10.9 gn1=10.9 UI0=10.9 c11m=11 cg1=11 MI1=11 UI1=11 e00=11 c11=11.1 us0=11.2 Y10=11.3 NW1=11.3 Y11=11.5 c000=11.5 SC0=11.5 Ml0=11.6 X1=11.7 W0=11.7 NE1=11.8 Mb0=11.8 put1=12 KU11=12.1 D01=12.1 O320=12.1 xb0=12.1 DG11=12.2 XP1=12.2 W00=12.2 ub0=12.2 DM1=12.3 xl0=12.3 gn0=12.4 MI0=12.5 DG00=12.6 T21=12.8 M40=12.8 TQ1=13.3 NW0=13.4 W1=13.5 MN1=13.6 NE0=13.6 R00=13.9 cg0=13.9 Z0=14.2 D00=14.3 SC1=14.6 NO0=14.7 c01m=14.7 TQ0=14.7 PP1=14.8 c011=14.9 AC=15.2 Z1=15.3 NN1=15.4 MS1=15.4 n01=15.7 NG0=16.1 c001=16.5 DM0=16.7 VG01=17.2 MS0=17.3 KU01=17.9 DG01=18.4 KS01=19.4 x01=19.6 c01=19.8 PM=19.9 A=20 XF0=20.2 NN0=20.3 MN0=20.5 RY=22.7")
+PIN = "AB0=V G0=VA G1=A Mb0=VA Mb1=VA O320=A O321=A P00=A P01=A PBz=VA RMN=A RMW=A VB=A Y0=VA Y1=A Y10=A Y11=VA ZT0=A ZT1=A a00=VA a01=VA a10=A a11=VA p00=A p01=VA p10=A p11=V"
+PAR["tau"] = {k: float(x) for k, x in (y.split("=") for y in TAU.split())}
+PAR["pin"] = dict(y.split("=") for y in PIN.split())
 
 
-def build(T, topo, core, nxt):
-    ops, wr, rd, bk = [], {}, {}, {}
+def build(T, topo, core, nxt, par):
+    ops, last, readers, step = [], {}, {}, [-1]
+    grid = {k: np.arange(int(np.prod(x[1][1:]))).reshape(x[1][1:]) for k, x in SCRATCH.items()}
+    cyc = par["cyc"]
 
-    def op(eng, fn, reads, writes, cost, banks=(), done=None):
-        i = len(ops)
-        hard, soft = set(), set()
-        for k in reads:
-            if k in wr: hard.add(wr[k])
-        for k in writes:
-            if k in wr: hard.add(wr[k])
-            for r in rd.get(k, ()):
-                if r != i: (soft if ops[r]["eng"] == eng and len(eng) == 1 and ops[r]["done"] is None else hard).add(r)
-        for b in banks:
-            for r in bk.setdefault(b, []):
-                if ops[r]["eng"] != eng: hard.add(r)
-            bk[b].append(i)
-        for k in reads: rd.setdefault(k, []).append(i)
-        for k in writes:
-            wr[k] = i
-            rd[k] = []
-        ops.append({"eng": eng, "fn": fn, "hard": hard, "soft": soft - hard, "cost": cost, "done": done, "w": writes})
-
-    def V(fn, reads, writes, n, banks=(), f=1.0):
-        op("V", fn, reads, writes, max(64, n * f) * CYC + 0.02, banks)
-
-    def G(fn, reads, writes, cost):
-        op("G", fn, reads, writes, cost)
-
-    def copy(o, i, r, w, n, banks=(), f=1.0):
-        V(lambda q: q.tensor_copy(o, i), r, w, n, banks, f)
-
-    def ts(o, i, s1, o1, s2, o2, r, w, n, banks=(), f=1.0):
-        if o2 is None: V(lambda q: q.tensor_scalar(o, i, s1, None, o1), r, w, n, banks, f)
-        else: V(lambda q: q.tensor_scalar(o, i, s1, s2, o1, o2), r, w, n, banks, f)
-
-    def tt(o, a, b, f, r, w, n, banks=(), c=2.0):
-        V(lambda q: q.tensor_tensor(o, a, b, f), r, w, n, banks, c)
-
-    def act(o, i, func, r, w, n, banks=(), gather=False, **kw):
-        op("A", lambda q: q.activation(o, i, func, **kw), r, w, 0.08 + n * CG * CYC if gather else max(64, n) * CYC + 0.05, banks)
-
-    def gath(o, i, neg, r, w, n):
-        def fn(q, e):
-            if e == "A": return q.activation(o, i, AF.Copy, scale=-1.0 if neg else 1.0)
-            return q.tensor_scalar(o, i, -1.0, None, OP.mult) if neg else q.tensor_copy(o, i)
-        op("VA", fn, r, w, 0.08 + n * CG * CYC)
-
-    def fill(o, c, w, n):
-        V(lambda q: q.memset(o, c), [], [w], n, (), 0.5)
-
-    def mm(lst, r, w, n, banks):
-        def fn(q):
-            x = None
-            for (o, l, rr, s, e) in lst: x = q.matmul(o, l, rr, s, e)
-            return x
-        op("T", fn, r, w, n * CYC * PF + 0.05, banks)
-
-    def load(q, name, dst, key):
-        op(q, lambda e: e.dma_start(dst, T[name][:]), [], [key], 0.1, (), ("ld_" + name, 16, LOADS[name]))
-
-    load("S", "m0", T.M0[:], "M0"); load("S", "mc", T.MC[:, 0:1024], "MC"); load("S", "pr", T.PR[:], "PR"); load("S", "ad", T.AD[:], "AD")
-    load("A", "wt", T.WT[:], "WT"); load("A", "dv", T.DV[:], "DV"); load("A", "z0", T.ZI0[:], "ZI0"); load("A", "gl", T.GL[:], "GL")
-    fill(T.ON[:], 1.0, "ON", 256)
-    RM, imp = T.RM[:], {"allow_small_or_imprecise_dtypes": True}
-    G(lambda q: q.iota(T.PI[:], [[0, 1]], 0, 1), [], ["PI"], 0.2)
-    G(lambda q: q.iota(T.I16[:], [[1, 16]], 0, 0, **imp), [], ["I16"], 0.2)
-    G(lambda q: q.affine_select(T.IDN[:], T.ON[:, 0:128], [[-1, 128]], OP.is_equal, 0.0, 0, 1), ["ON"], ["IDN"], 0.5)
-    G(lambda q: q.affine_select(T.BLB[:], T.ON[:, 0:128], [[-16, 8], [0, 16]], OP.is_ge, 0.0, 0, 1), ["ON"], ["BLB"], 0.5)
-    G(lambda q: q.affine_select(T.BLK[:], T.BLB[:], [[16, 8], [0, 16]], OP.is_ge, 0.0, 15, -1), ["BLB"], ["BLK"], 0.5)
-    G(lambda q: q.iota(T.KV[:], [[512, 8], [2, 18]], 14, 0, **imp), [], ["KV"], 0.5)
-    G(lambda q: q.iota(T.SX[:], [[16, 16]], 1024, 0, **imp), [], ["SX"], 0.2)
-    G(lambda q: q.affine_select(T.CMB[:], T.ON[:], [[-1, 16], [1, 16]], OP.is_equal, 0.0, 0, 0), ["ON"], ["CMB"], 0.5)
-    G(lambda q: q.iota(T.IOTA[:], [[1, 4096]], 0, 0, **imp), ["BLK", "CMB", "IDN", "KV", "SX", "I16", "PI"], ["IOTA"], 8.0)
-    copy(T.MSK[:], T.BLK[:, 0:128:16], ["BLK"], ["MSK"], 8)
-    for x in range(8): ts(T.RM[:, :, x, :], T.CMB[:], T.MSK[:, x:x + 1], OP.mult, None, None, ["MSK", "CMB"], [("RM", x)], 256, (), 0.5)
-    RMK = [("RM", x) for x in range(8)]
-    for h in range(2):
-        AB, PB = T["AB%d" % h], T["PB%d" % h]
-        if h: act(AB[:, 15:4112:2], T.AB0[:, 15:4112:2], AF.Copy, ["ABo0"], ["ABo1"], 2049)
+    def v(name, ix=None):
+        if ix is None: ap, el = T[name][:], grid[name]
         else:
-            fill(AB[:, 15:4112:2], 0.0, "ABo0", 2049)
-            fill(AB[:, 15:4112:32], -256.0, "ABo0", 129)
-        act(PB[:, 18:4112:2], T.AB0[:, 15:4108:2], AF.Copy, ["ABo0"], ["PBz%d" % h], 2047, scale=0.0)
-        fill(T["C%d" % h][:, :, :, 0], 1.0, ("C", h, 0), 128)
-    for h in range(2):
-        for x in range(2):
-            if NAS[h]: fill(T["BR%d%d" % (x, h)][:, :, 18 - NAS[h]:18], 2.0 - x, ("BR", h), 144)
-            fill(T["BR%d%d" % (x, h)][:, :, 0:18 - NAS[h]], 1.0 - x, ("BR", h), 144)
-    fill(T.CST[:], 2048.0, "CST", 128)
-    fill(T.TH[:], -1472.0, "TH", 128)
-    ts(T.PR16[:], T.PI[:], 15, OP.bitwise_and, None, None, ["PI"], ["PR16"], 1)
-    copy(T.R16[:], T.PR16[:], ["PR16"], ["R16"], 1)
-    ts(T.R32[:], T.R16[:], 32.0, OP.mult, None, None, ["R16"], ["R32"], 1)
-    ts(T.C37[:], T.R16[:], 37.0, OP.mult, None, None, ["R16"], ["C37"], 1)
-    ts(T.KV[:], T.KV[:], T.R32[:, 0:1], OP.add, None, None, ["R32", "KV"], ["KV"], 144)
-    ts(T.KV[:, 0:144:18], T.KV[:, 0:144:18], 1.0, OP.add, None, None, ["KV"], ["KV"], 8)
-    ts(T.KV[:, 17:144:18], T.KV[:, 17:144:18], -1.0, OP.add, None, None, ["KV"], ["KV"], 8)
-    ts(T.BASE[:], T.KV[:, 0:144:18], 1.0, OP.add, None, None, ["KV"], ["BASE"], 8)
-    ts(T.SX[:], T.SX[:], T.R16[:, 0:1], OP.add, None, None, ["R16", "SX"], ["SX"], 16)
-    ts(T.E16[:], T.I16[:], T.R16[:, 0:1], OP.is_equal, None, None, ["R16", "I16"], ["E16"], 16)
-    ts(T.TM[:], T.I16[:], T.R16[:, 0:1], OP.is_ge, -64.0, OP.mult, ["R16", "I16"], ["TM"], 16)
-    for b in range(16): fill(T.PWR[:, b:b + 1], 2.0 ** -b, ("PWR", b), 1)
-    tt(T.E16[:], T.E16[:], T.PWR[:], OP.mult, ["E16"] + [("PWR", b) for b in range(16)], ["E16"], 16)
-    V(lambda q: q.tensor_reduce(T.PW[:], T.E16[:], AxisListType.X, OP.add), ["E16"], ["PW"], 16)
-    ts(T.BTI[:], T.IOTA[:, 0:1280], T.PW[:, 0:1], OP.mult, -0.5 + 2.0 ** -13, OP.add, ["IOTA", "PW"], ["BTI"], 1280)
-    ts(T.BTI[:], T.BTI[:], 1, OP.bitwise_and, None, None, ["BTI"], ["BTI"], 1280)
-    ts(T.BT[:], T.BTI[:], 2.0, OP.mult, -1.0, OP.add, ["BTI"], ["BT"], 1280)
-    ts(T.NID[:], T.IDN[:], -1.0, OP.mult, None, None, ["IDN"], ["NID"], 128, (), 0.5)
-    ts(T.I128[:], T.IDN[:], 128.0, OP.mult, None, None, ["IDN"], ["I128"], 128, (), 0.5)
-    act(T.RMC[:], RM, AF.Copy, RMK, ["RMC"], 2048, scale=16384.0)
-    act(T.RMN[:], RM, AF.Copy, RMK, ["RMN"], 2048, scale=-1.0)
-    ts(T.RMW[:], RM, T.WT[:, 0:1], OP.mult, None, None, RMK + ["WT"], ["RMW"], 2048, (), 0.5)
-    ts(T.DH[:], T.DV[:], -0.5, OP.mult, None, None, ["DV"], ["DH"], 8)
-    for j in range(8):
-        ts(T.DG[:, 128 * j:128 * j + 128], T.IDN[:], T.DH[:, j:j + 1], OP.mult, None, None, ["IDN", "DH"], [("DG", j)], 128, (), 0.5)
-    copy(T.MU0[:], T.M0[:], ["M0"], ["MU0"], 16)
+            ix = ix if isinstance(ix, tuple) else (ix,)
+            ap, el = T[name][(slice(None),) + ix], grid[name][ix]
+        return {"ap": ap, "el": [(name, np.ravel(el))], "n": int(np.size(el)), "b": 4 if SCRATCH[name][2] in (F, I) else 2, "ps": name[0] == "P" and name[1].isdigit()}
+
+    def ind(win, off):
+        return {"ap": win["ap"].indirect(off["ap"]), "el": win["el"], "off": off["el"], "n": 16 * off["n"], "b": 4, "ps": False}
+
+    def op(name, eng, fn, ins, outs, cost, done=None, after=(), dyn=None):
+        i = len(ops)
+        raw, war, banks = set(after), set(), set()
+        rd = [e for x in ins + outs if isinstance(x, dict) for e in x.get("off", [])] + [e for x in ins if isinstance(x, dict) for e in x["el"]]
+        wr = [e for x in outs for e in x["el"]]
+        for nm, el in rd + wr:
+            if nm not in last: last[nm], readers[nm] = np.full(grid[nm].size, -1), []
+            if nm[0] == "P" and nm[1].isdigit(): banks.add(nm)
+        for nm, el in rd: raw.update(np.unique(last[nm][el]).tolist())
+        for nm, el in wr:
+            (war if eng == "T" else raw).update(np.unique(last[nm][el]).tolist())
+            keep = []
+            for r, m in readers[nm]:
+                if m[el].any():
+                    war.add(r)
+                    m[el] = False
+                if m.any(): keep.append((r, m))
+            readers[nm] = keep
+            last[nm][el] = i
+        for nm, el in rd:
+            m = np.zeros(grid[nm].size, bool)
+            m[el] = True
+            readers[nm].append((i, m))
+        raw -= {-1, i}
+        ops.append({"name": name, "eng": eng, "fn": fn, "raw": raw, "war": war - raw - {-1, i}, "cost": cost, "done": done, "banks": banks, "dyn": dyn, "step": step[0]})
+        return i
+
+    def price(o, ins, both=False, scalar=False):
+        xs = [x for x in ins if isinstance(x, dict)]
+        n = max([o["n"]] + [x["n"] for x in xs])
+        if "off" in o: c = a = par["cs"]
+        elif any("off" in x for x in xs): c = a = par["cg"]
+        elif both: c, a = (1.0 if any(x["ps"] for x in xs) else 2.0), 1.0
+        else: c, a = (0.5 if o["b"] == 2 and all(x["b"] == 2 for x in xs if x["n"] > 1) else 1.0), 1.0
+        return {"V": par["ovV"] + max(30, n * c) * cyc, "A": par["ovA"] + max(30, n * a) * cyc}
+
+    def ap(x): return x["ap"] if isinstance(x, dict) else x
+
+    def copy(nm, o, i): return op(nm, "V", lambda q, e: q.tensor_copy(o["ap"], i["ap"]), [i], [o], price(o, [i]))
+
+    def ts(nm, o, i, s1, o1, s2=None, o2=None):
+        fn = (lambda q, e: q.tensor_scalar(o["ap"], i["ap"], ap(s1), None, o1)) if o2 is None else (lambda q, e: q.tensor_scalar(o["ap"], i["ap"], ap(s1), ap(s2), o1, o2))
+        return op(nm, "V", fn, [i, s1, s2], [o], price(o, [i]))
+
+    def tt(nm, o, a, b, f): return op(nm, "V", lambda q, e: q.tensor_tensor(o["ap"], a["ap"], b["ap"], f), [a, b], [o], price(o, [a, b], True))
+
+    def scan(nm, o, a, b, f0, f1): return op(nm, "V", lambda q, e: q.tensor_tensor_scan(o["ap"], a["ap"], b["ap"], 0.0, f0, f1), [a, b], [o], price(o, [a, b]))
+
+    def act(nm, o, i, func, scale=1.0, bias=0.0, acc=None):
+        kw = {"accum_out": acc["ap"]} if acc else {}
+        return op(nm, "A", lambda q, e: q.activation(o["ap"], i["ap"], func, bias=ap(bias), scale=ap(scale), **kw), [i, scale, bias], [o] + ([acc] if acc else []), price(o, [i]))
+
+    def lin(nm, o, i, scale=1.0, bias=0.0, eng="VA"):
+        def fn(q, e):
+            if e == "A": return q.activation(o["ap"], i["ap"], AF.Identity if bias else AF.Copy, bias=ap(bias), scale=ap(scale))
+            if bias: return q.tensor_scalar(o["ap"], i["ap"], ap(scale), ap(bias), OP.mult, OP.add)
+            return q.tensor_copy(o["ap"], i["ap"]) if scale == 1.0 else q.tensor_scalar(o["ap"], i["ap"], ap(scale), None, OP.mult)
+        return op(nm, par["pin"].get(nm, eng), fn, [i, scale, bias], [o], price(o, [i]))
+
+    def fill(o, c): return op("fill", "V", lambda q, e: q.memset(o["ap"], c), [], [o], price(o, []))
+
+    def mmcost(ns): return {"T": par["ovT"] + sum(max(64, n) for n in ns) * par["pf"] * cyc}
+
+    def mm(nm, lst, first=True, final=True):
+        def fn(q, e):
+            x = None
+            for k, (o, l, r) in enumerate(lst): x = q.matmul(o["ap"], l["ap"], r["ap"], first and k == 0, final and k == len(lst) - 1)
+            return x
+        return op(nm, "T", fn, [x for y in lst for x in y[1:]], [y[0] for y in lst], mmcost([y[2]["n"] for y in lst]))
+
+    def G(o, ins, fn, n): return op("const", "G", lambda q, e: fn(q), ins, [o], {"G": 0.17 + 2 * n * cyc})
+
+    def dma(q, o, i, ins, outs, sem, lat): return op("dma", q, lambda x, e: x.dma_start(o, i), ins, outs, {q: 0.1}, (sem, 16, lat))
+
+    for q, name, dst, lat in LOADS: dma(q, T[dst][:], T[name][:], [], [v(dst)], "ld_" + name, lat)
+    imp = {"allow_small_or_imprecise_dtypes": True}
+    ON, IDN, NID, R16 = v("ON", S[0:128]), v("IDN"), v("NID"), v("R16")
+    fill(v("ON"), 1.0)
+    G(v("PI"), [], lambda q: q.iota(T.PI[:], [[0, 1]], 0, 1), 1)
+    G(v("BLB"), [ON], lambda q: q.affine_select(T.BLB[:], ON["ap"], [[-16, 8], [0, 16]], OP.is_ge, 0.0, 0, 1), 128)
+    G(v("BLK"), [v("BLB")], lambda q: q.affine_select(T.BLK[:], T.BLB[:], [[16, 8], [0, 16]], OP.is_ge, 0.0, 15, -1), 128)
+    G(v("CMB"), [v("ON")], lambda q: q.affine_select(T.CMB[:], T.ON[:, 0:256], [[-1, 16], [1, 16]], OP.is_equal, 0.0, 0, 0), 256)
+    G(IDN, [ON], lambda q: q.affine_select(T.IDN[:], ON["ap"], [[-1, 128]], OP.is_equal, 0.0, 0, 1), 128)
+    G(v("KV"), [], lambda q: q.iota(T.KV[:], [[512, 8], [2, 18]], 14, 0, **imp), 144)
+    G(v("I16"), [], lambda q: q.iota(T.I16[:], [[0, 8], [1, 16]], 0, 0, **imp), 128)
+    G(v("CI"), [], lambda q: q.iota(T.CI[:], [[1, 8]], 0, 0, **imp), 8)
+    G(v("E"), [v("ON")], lambda q: q.affine_select(T.E[:], T.ON[:], [[-1, 128], [0, 16]], OP.is_equal, 0.0, 0, 1), 2048)
+    G(v("IOTA"), [], lambda q: q.iota(T.IOTA[:], [[1, 1024]], 0, 0, **imp), 1024)
+    copy("MU0", v("MU0"), v("M0"))
+    copy("MC", v("MC", S[0:1024]), v("MCI"))
+    fill(v("MC", S[1024:1040]), 0.0)
+    copy("MSK", v("MSK"), v("BLK", S[0:128:16]))
+    for x in range(8): ts("RMC", v("RMC", S[:, x, :]), v("CMB"), v("MSK", S[x:x + 1]), OP.mult, BIG, OP.mult)
+    lin("RMN", v("RMN"), v("RMC"), -1.0)
+    ts("WS", v("WS"), v("WT"), 4.0 / BIG, OP.mult)
+    ts("W4", v("W4"), v("WT"), 4.0, OP.mult)
+    lin("RMW", v("RMW"), v("RMC"), v("WS"))
+    ts("BW", v("BW"), v("BLK"), v("WT"), OP.mult)
+    ts("BW4", v("BW4"), v("BLK"), v("W4"), OP.mult)
+    ts("BN", v("BN"), v("BLK"), -BIG, OP.mult)
+    ts("NID", NID, IDN, -1.0, OP.mult)
+    copy("DVF", v("DVF"), v("DV"))
+    fill(v("AB1", S[0:16]), 0.0), fill(v("AB1", S[4112:4128]), 0.0), fill(v("AB1", S[17:4112:2]), 0.0), fill(v("AB1", S[47:4112:32]), -256.0)
+    fill(v("AB0", S[0:16]), 0.0), fill(v("AB0", S[4112:4128]), 0.0)
+    lin("AB0", v("AB0", S[17:4112:2]), v("AB1", S[17:4112:2]))
+    for h in "10":
+        lin("PBz", v("PB" + h, S[16:4112:2]), v("ON"), 0.0)
+        fill(v("C" + h, S[:, 0]), 0.0), fill(v("M37" + h, S[0:128]), 0.0)
+    fill(v("VB", S[0:16]), 0.0), fill(v("VB", S[4112:4128]), 0.0)
+    lin("VB", v("VB", S[16:4112:2]), v("ON")), lin("VB", v("VB", S[17:4112:2]), v("ON"), 0.0)
+    fill(v("NON"), -1.0), fill(v("PM"), -1.0), fill(v("BN0"), BIG / 256), fill(v("BN1"), 12 * BIG / 128)
+    ts("PR16", v("PR16"), v("PI"), 15, OP.bitwise_and)
+    copy("R16", R16, v("PR16"))
+    ts("R32", v("R32"), R16, 32.0, OP.mult)
+    ts("C37", v("C37"), R16, 1184.0, OP.mult, -393216.0, OP.add)
+    ts("SPR", v("SPR"), R16, 1024.0, OP.add)
+    ts("KV", v("KV"), v("KV"), v("R32"), OP.add)
+    fill(v("KV", S[0:144:18]), 0.0)
+    ts("KV", v("KV", S[17:144:18]), v("KV", S[17:144:18]), 1.0, OP.add)
+    ts("RS", v("RS"), v("I16"), R16, OP.is_equal, TOP, OP.mult)
+    copy("CL", v("CL"), v("CI"))
+    unit = BIG / 128
+    for j in range(2):
+        for h in range(2):
+            x = 4 * j + 2 * h
+            for who, c, k in [(w, S[2 * b:2 * b + 2], S[2:18]) for b, w in enumerate(par["kind"][j, h])] + [(par["one"][j, h], S[:], S[1:2])]:
+                fill(v("BR", (x, c, k)), -unit / 2 if who == "V" else -unit), fill(v("BR", (x + 1, c, k)), -12 * unit if who == "V" else -8 * unit)
+            fill(v("BR", S[x, :, 0:1]), 0.0), fill(v("BR", S[x + 1, :, 0:1]), 32 * unit)
+
+    rid, pid, _ = topo.addr(nxt)
+    mask, ne = topo.mask(core, nxt), len(topo.engines(core, nxt))
+    sent = {}
+
+    def send(kind, t, h, src, ix):
+        o, i = T["%s%d" % ({"z": "ZI", "m": "MU"}[kind], t)][:, ix], v(src, ix)
+        sent[kind, t, h] = op("send", "G", lambda q, e: q.remote_dma(o, i["ap"], T.sem["%si%d%d" % (kind, t, h)], T.sem["%sl%d%d" % (kind, t, h)], pid, rid, mask),
+                              [i], [], {"G": 0.5}, ("%sl%d%d" % (kind, t, h), ne, 1.5))
+
+    def compare(nm, who, out, kk, zt, b):
+        cell, e_ = {}, v("E", S[512 * b:512 * b + 512])
+
+        def fm(q, e):
+            P = T[cell["bank"]][:]
+            if who == "V": return q.matmul(P, zt["ap"], e_["ap"], True, True)
+            q.matmul(P, NID["ap"], kk["ap"], True, False)
+            return q.matmul(P, zt["ap"], e_["ap"], False, True)
+        m = op(nm + "m", "T", fm, [zt, e_] + ([NID, kk] if who == "A" else []), [], mmcost([512] * (1 if who == "V" else 2)), dyn=("take", cell))
+        cost = {"V": par["ovV"] + 512 * cyc, "A": par["ovA"] + 512 * cyc}
+        if who == "V": op(nm, "V", lambda q, e: q.tensor_tensor(out["ap"], kk["ap"], T[cell["bank"]][:], OP.is_le), [kk], [out], cost, after=[m], dyn=("give", cell))
+        else: op(nm, "A", lambda q, e: q.activation(out["ap"], T[cell["bank"]][:], AF.Sign, bias=0.5), [], [out], cost, after=[m], dyn=("give", cell))
 
     for t in range(4):
-        ZI, MU = T["ZI%d" % t], T["MU%d" % t]
-        zk, mk = "ZI%d" % t, "MU%d" % t
-        if t:
-            nw = len(topo.engines(core, nxt))
-            op("", None, [zk + "s"], [zk], 0, (), ("zi%d" % t, nw, 3.0))
-            op("", None, [mk + "s"], [mk], 0, (), ("mi%d" % t, nw, 3.0))
-        for h in range(2):
-            a = 128 * h
-            copy(T.OU[:, a:a + 128], T.MC[:, 0:1024].indirect(MU[:, 8 * h:8 * h + 8]), ["MC", mk], [("OU", h)], 128, (), CG)
-            act(T["G%d" % h][:], T.GL[:].indirect(MU[:, 8 * h:8 * h + 8]), AF.Copy, ["GL", mk], ["G%d" % h], 128, gather=True)
-        copy(T.MF[:], MU[:], [mk], ["MF"], 16)
-        for h in range(2):
-            Zb, Xb, Eb = T["P%d" % h], T["P%d" % (2 + h)], T["P%d" % (6 + h)]
-            AB, PB, KB, C = T["AB%d" % h], T["PB%d" % h], T["KB%d" % h], T["C%d" % h]
-            KS, KU, vg, sg, T2, R0, G_ = [T[n + str(h)] for n in ("KS", "KU", "VG", "SG", "T2", "R0", "G")]
-            a, b, ch, NA = 128 * h, 128 * h + 128, CHS[h], NAS[h]
-            mm([(Zb[:, 0:128], T.IDN[:], ZI[:, a:b], True, True)], [zk, "IDN"], ["ZP%d" % h], 128, [h])
-            n = 128 // ch
-            for c in range(ch):
-                lo, s0 = 32 * n * c, a + n * c
-                gath(PB[:, 15 + lo:15 + lo + 32 * n:2], T.PR[:].indirect(T.OU[:, s0:s0 + n]), False, ["PR", ("OU", h)], [("PB", h, c)], 16 * n)
-                gath(AB[:, 16 + lo:16 + lo + 32 * n:2], T.AD[:].indirect(T.OU[:, s0:s0 + n]), True, ["AD", ("OU", h)], [("AB", h, c)], 16 * n)
-            pk, ak = [("PB", h, c) for c in range(ch)], [("AB", h, c) for c in range(ch)]
-            copy(PB[:, 16:4112:32], PB[:, 15:4111:32], pk + ["PBz%d" % h], ["P0%d" % h], 128, (), 0.5)
-            copy(PB[:, 47:4112:32], G_[:], ["G%d" % h, "P0%d" % h], pk, 128, (), 0.5)
-            V(lambda q, KB=KB, AB=AB, PB=PB: q.tensor_tensor_scan(KB[:, ::-1], AB[:, 4111:15:-1], PB[:, 4111:15:-1], 0.0, OP.add, OP.max),
-              pk + ak + ["P0%d" % h, "PBz%d" % h, "ABo%d" % h], ["KB%d" % h], 4096, (), 0.5)
-            mm([(Eb[:, 0:128], T.IDN[:], KB[:, 1:4096:32], True, False), (Eb[:, 0:128], T.IDN[:], AB[:, 16:4112:32], False, True)],
-               ["IDN", "KB%d" % h] + ak, ["E0%d" % h], 256, [6 + h])
-            act(R0[:], Eb[:, 0:128], AF.Relu, ["E0%d" % h], ["R0%d" % h], 128, [6 + h])
-            us = T["P%d" % (4 + h)][:, 384 * h:384 * h + 128]
-            for k in range(16):
-                if k % 4 == 0: lst = []
-                lst.append((us, T.RM[:, k, :, :], KB[:, 2 * k + 1:4096:32], k == 0, False))
-                lst.append((us, T.RMN[:, k, :, :], KB[:, 2 * k:4096:32] if k else R0[:], False, k == 15))
-                if k % 4 == 3: mm(lst, RMK + ["RMN", "KB%d" % h, "R0%d" % h, ("UO", h, k)], [("US", h, k), ("UO", h, k - 4)], 8 * 128, [4 + h])
-            zsrc, zkey = ZI[:, a:b], zk
-            kpos = [2 * k - 1 if k else 0 for k in range(17)]
+        ZI, MU, step[0] = "ZI%d" % t, "MU%d" % t, t
+        for h in (1, 0):
+            a, s = 128 * h, str(h)
+            mu = v(MU, S[8 * h:8 * h + 8])
+            if t:
+                op("m in", "", None, [], [mu], {}, ("mi%d%d" % (t, h), ne, par["far"]), [sent["m", t, h]])
+                op("z in", "", None, [], [v(ZI, S[a:a + 128])], {}, ("zi%d%d" % (t, h), ne, par["far"]), [sent["z", t, h]])
+            copy("OU" + s, v("OU", S[a:a + 128]), ind(v("MC", S[0:1024]) if t else v("MCI"), mu))
+            ts("NO" + s, v("NO", S[a:a + 128]), v("OU", S[a:a + 128]), -1.0, OP.mult)
+            lin("O32" + s, v("O32", S[a:a + 128]), v("NO", S[a:a + 128]), -32.0)
+        for h in (1, 0):
+            a, s = 128 * h, str(h)
+            AB, PB, KB, C, XB = "AB" + s, "PB" + s, "KB" + s, "C" + s, "P%d" % (3 + h)
+            mu, z0 = v(MU, S[8 * h:8 * h + 8]), v(ZI, S[a:a + 128])
+            xs, xt, cp = v(XB, S[144:272]), v("P7", S[256 + a:384 + a]), v(XB, S[0:144])
+            zt, y, z1, vg, dg, ks = v("ZT" + s), v("Y" + s), v("Z1" + s), v("VG" + s), v("DG" + s), v("KS" + s, S[17:144:18])
+            n = 128 // par["pieces"]
+            for c in range(par["pieces"]):
+                lin("p%d%d" % (h, c), v(PB, S[15 + 32 * n * c:15 + 32 * n * (c + 1):2]), ind(v("PR"), v("OU", S[a + n * c:a + n * (c + 1)])))
+            for c in range(par["pieces"]):
+                lin("a%d%d" % (h, c), v(AB, S[16 + 32 * n * c:16 + 32 * n * (c + 1):2]), ind(v("AD"), v("OU", S[a + n * c:a + n * (c + 1)])), -1.0)
+            lin("P0" + s, v(PB, S[16:4112:32]), v(PB, S[15:4111:32]))
+            lin("G" + s, v(PB, S[47:4112:32]), ind(v("GL"), mu))
+            scan("K" + s, v(KB, S[::-1]), v(AB, S[4111:15:-1]), v(PB, S[4111:15:-1]), OP.add, OP.max)
+            mm("zt" + s, [(xt, z0, IDN)])
+            lin("ZT" + s, zt, xt)
+            lin("Y" + s, y, z0, 1.0, -255.0)
+            lin("Mb" + s, v("M37" + s, S[128:256]), ind(v("IOTA"), mu), 148.0, TOP)
+            ts("Ml" + s, v("M37" + s, S[256:264]), mu, 148.0, OP.mult, TOP, OP.add)
+            ts("M4" + s, v("M4", S[8 * h:8 * h + 8]), mu, 4.0, OP.mult, TOP, OP.add)
+            mm("e0" + s, [(xs, IDN, v(KB, S[1:4096:32])), (xs, IDN, v(AB, S[16:4112:32]))])
+            act("R0" + s, v("R0" + s), xs, AF.Relu)
+            us, w0, og = v("P5", S[0:128]), v("P5", S[128:256]), v("P5", S[256 + a:384 + a])
+            for k4 in range(3, -1, -1):
+                lst = []
+                for k in range(4 * k4, 4 * k4 + 4):
+                    lst += [(us, v("RMC", S[k]), v(KB, S[2 * k + 1:4096:32])), (us, v("RMN", S[k]), v(KB, S[2 * k:4096:32]) if k else v("R0" + s))]
+                mm("us" + s, lst, k4 == 3, k4 == 0)
+            ts("W0" + s, w0, us, 253.5 * BIG, OP.is_lt, v("C37"), OP.mult)
+            tt("OG" + s, og, v("NO", S[a:a + 128]), w0, OP.max)
+            tt("W" + s, v("W" + s), v("O32", S[a:a + 128]), w0, OP.add)
+            z = z0
             for j in range(2):
-                for B, bank, ks in ((T.P7, 7, range(17 - NA, 17 - NA + min(4, NA))), (T.P6, 6, range(17 - NA + min(4, NA), 17))):
-                    if not ks: continue
-                    lst = []
-                    for i, k in enumerate(ks):
-                        lst.append((B[:, 128 * i:128 * i + 128], T.IDN[:], zsrc, True, False))
-                        lst.append((B[:, 128 * i:128 * i + 128], T.NID[:], KB[:, kpos[k]:4096:32], False, True))
-                    mm(lst, ["IDN", "NID", zkey, "KB%d" % h], [("D", h, bank)], 128 * len(lst), [bank])
-                    for i, k in enumerate(ks):
-                        act(C[:, :, :, k + 1], B[:, 128 * i:128 * i + 128], AF.Sign, [("D", h, bank)], [("C", h, k + 1)], 128, [bank], bias=0.5)
-                for k in range(17 - NA):
-                    tt(C[:, :, :, k + 1], KB[:, kpos[k]:4096:32], Zb[:, 0:128], OP.is_le, ["KB%d" % h, "ZP%d" % h], [("C", h, k + 1)], 128, [h], 1.0)
-                cp = Xb[:, 0:144]
-                lst = [(cp, T.TH[:], T["BR0%d" % h][:], True, False)] + ([(cp, T.CST[:], T["BR1%d" % h][:], False, False)] if NA else [])
-                lst += [(cp, T.RMC[:, r, :, :], C[:, :, r, :], False, r == 15) for r in range(16)]
-                mm(lst, [("C", h, k) for k in range(18)] + [("BR", h)] + ["RMC", "CST", "TH"], ["CP%d" % h], 18 * 144, [2 + h])
-                V(lambda q, KS=KS, cp=cp: q.tensor_tensor_scan(KS[:], cp, T.KV[:], 0.0, OP.max, OP.min), ["CP%d" % h, "KV"], ["KS%d" % h], 144, [2 + h])
-                copy(KU[:], KS[:, 17:144:18], ["KS%d" % h], ["KU%d" % h], 8)
-                abk = ak + ["ABo%d" % h, "KU%d" % h]
-                act(sg[:], AB[:].indirect(KU[:]), AF.Sign, abk, ["SG%d" % h], 128, gather=True, bias=192.0)
-                gath(vg[:], AB[:].indirect(KU[:]), False, abk, ["VG%d" % h], 128)
-                xs, dj = Xb[:, 144:272], 2 * t + j
-                mm([(xs, T.IDN[:], zsrc, True, False), (xs, T.NID[:], vg[:], False, False), (xs, T.I128[:], sg[:], False, True)],
-                   [zkey, "IDN", "NID", "I128", "VG%d" % h, "SG%d" % h], ["X1%d" % h], 384, [2 + h])
-                ts(T2[:], xs, 383.0, OP.min, 128.0, OP.subtract, ["X1%d" % h], ["T2%d" % h], 128, [2 + h])
-                mm([(xs, T.IDN[:], T2[:], True, False), (xs, T.DG[:, 128 * dj:128 * dj + 128], sg[:], False, True)],
-                   ["IDN", ("DG", dj), "T2%d" % h, "SG%d" % h], ["X1%d" % h], 256, [2 + h])
-                bias, xr = T.DH[:, dj:dj + 1], ["X1%d" % h, "DH"]
-                if j == 0: act(Zb[:, 0:128], xs, AF.Abs, xr, ["ZP%d" % h], 128, [h, 2 + h], bias=bias)
-                act(T.Z[:, a:b], xs, AF.Abs, xr, ["Z%d" % h], 128, [2 + h], bias=bias)
-                if t == 3 and j == 1: act(T.ZF[:, a:b], xs, AF.Abs, xr, ["ZF%d" % h], 128, [2 + h], bias=bias)
-                zsrc, zkey = T.Z[:, a:b], "Z%d" % h
-            ul = T.P2[:, 400 + 8 * h:408 + 8 * h]
-            mm([(ul, T.RMW[:, r, :, :], T.Z[:, a + r:b:16], r == 0, r == 15) for r in range(16)], ["RMW", "Z%d" % h], [("UL", h)], 1024, [2])
-            tt(T.KD[:, 8 * h:8 * h + 8], KS[:, 17:144:18], T.BASE[:], OP.subtract, ["KS%d" % h, "BASE"], [("KD", h)], 8)
-
-        def send(q, src, name, sem):
-            rid, pid, _ = topo.addr(nxt)
-            q.remote_dma(T[name][:], src[:], T.sem[sem % "i"], T.sem[sem % "l"], pid, rid, topo.mask(core, nxt))
-        n1, ne = t + 1, len(topo.engines(core, nxt))
+                js = "%d%d" % (h, j)
+                if par["one"][j, h] == "V": tt("c0" + js, v(C, S[:, 1]), v(KB, S[0:4096:32]), z, OP.is_le)
+                else:
+                    mm("d0" + js, [(xs, IDN, z), (xs, NID, v(KB, S[0:4096:32]))])
+                    act("c0" + js, v(C, S[:, 1]), xs, AF.Sign, 1.0, 0.5)
+                for b in range(4):
+                    compare("c" + js, par["kind"][j, h][b], v(C, S[32 * b:32 * b + 32, 2:18]), v(KB, S[1024 * b + 1:1024 * b + 1024:2]), zt, b)
+                    if b % 2:
+                        c4 = 2 * b - 2
+                        o = v(XB, S[18 * c4:18 * c4 + 72])
+                        x = 4 * j + 2 * h
+                        mm("n" + js, [(o, v("PM"), v("BR", S[x, c4:c4 + 4])), (o, ON, v("BR", S[x + 1, c4:c4 + 4]))]
+                           + [(o, v("RMC", S[r]), v(C, S[16 * c4 + r:16 * c4 + 64:16])) for r in range(16)])
+                scan("KS" + js, v("KS" + s), cp, v("KV"), OP.max, OP.min)
+                copy("KU" + js, v("KU" + s), ks)
+                tt("VG" + js, vg, ind(v(AB), v("KU" + s)), y, OP.max)
+                lin("DG" + js, dg, ind(v("VB"), v("KU" + s)), v("DVF", S[2 * t + j:2 * t + j + 1]), 0.0, "A")
+                mm("x" + js, [(xs, IDN, z), (xs, NID, vg), (xs, NID, dg)])
+                if j == 0:
+                    mm("xt" + s, [(xt, z, IDN), (xt, vg, NID), (xt, dg, NID)])
+                    act("Z1" + s, z1, xs, AF.Abs)
+                    act("ZT1" + s, zt, xt, AF.Abs)
+                    lin("Y1" + s, y, z1, 1.0, -255.0)
+                    z = z1
+                    tb, tc = v("P6", S[0:264]), v("P7", S[0:136])
+                    mm("ub" + s, [(v("P6", S[0:128]), v("BW"), z1)])
+                    mm("xb" + s, [(v("P6", S[128:256]), v("BW4"), z1)])
+                    mm("xl" + s, [(v("P6", S[256:264]), v("RMW", S[r]), v("Z1" + s, S[r:128:16])) for r in range(16)])
+                    tt("cg" + s, v(C, S[:, 0]), v(KB, S[31:4096:32]), z1, OP.is_le)
+                    gb, gl = v("P7", S[0:128]), v("P7", S[128:136])
+                    mm("gn" + s, [(tc, v("PM"), v("BN0")), (tc, ON, v("BN1")), (gb, v("BN"), v(C, S[:, 0]))]
+                       + [(gl, v("RMN", S[r]), v(C, S[r:128:16, 0])) for r in range(16)])
+                    tt("MI" + s, v("MI" + s), tb, v("M37" + s), OP.add)
+                    ts("UI" + s, v("UI" + s), v("MI" + s), int(TOP) + 4095, OP.bitwise_and)
+                    tt("X" + s, v("X" + s), v("UI" + s, S[128:264]), tc, OP.max)
+                    xl, ml = v("X" + s, S[128:136]), v("UI" + s, S[256:264])
+                    tt("NE" + s, v("NE" + s), ind(xl, v("CL")), v("X" + s, S[0:128]), OP.not_equal)
+                    scan("SC" + s, v("SC" + s, S[::-1]), v("NE" + s, S[::-1]), v("RS", S[::-1]), OP.mult, OP.max)
+                    tt("T2" + s, v("T2" + s), xl, v("SC" + s, S[0:128:16]), OP.subtract)
+                    ts("XF" + s, v("XF" + s, S[0:16:2]), v("T2" + s), 0.25, OP.mult, v("SPR"), OP.min)
+                    tt("PP" + s, og, v("UI" + s, S[0:128]), og, OP.mult)
+                    tt("XP" + s, v("XP" + s), v("W" + s), og, OP.subtract)
+                    ts("NW" + s, v("NW" + s), v("XP" + s), 5, OP.arith_shift_right, 4095, OP.bitwise_and)
+                    for c in range(7, -1, -1):
+                        copy("put" + s, ind(v("MC"), v("XF" + s, S[2 * c:2 * c + 1])), v("NW" + s, S[16 * c:16 * c + 16]))
+                    ng = v("NG", S[8 * h:8 * h + 8])
+                    ts("NG" + s, ng, xl, TOP + 8192.0, OP.is_ge)
+                    tt("D0" + s, v("D0" + s), v("M4", S[8 * h:8 * h + 8]), ml, OP.subtract)
+                    tt("DM" + s, v("DM" + s), v("D0" + s), ng, OP.mult)
+                else:
+                    act("Z" + s, v("Z" if t < 3 else "ZF", S[a:a + 128]), xs, AF.Abs)
+                    act("NN" + s, v("NN" + s), ks, AF.Sign)
+                    tt("TQ" + s, v("TQ" + s), v("NN" + s), v("DM" + s), OP.mult)
+                    tt("MN" + s, v("MN" + s), v("TQ" + s), v("UI" + s, S[256:264]), OP.add)
+                    ts("MS" + s, v("MS" if t < 3 else "YM", S[8 * h:8 * h + 8]), v("MN" + s), -TOP, OP.add, 0.25, OP.mult)
+                    if t < 3:
+                        send("m", t + 1, h, "MS", S[8 * h:8 * h + 8])
+                        send("z", t + 1, h, "Z", S[a:a + 128])
         if t < 3:
-            op("G", lambda q, n1=n1: send(q, T.Z, "ZI%d" % n1, "z%%s%d" % n1), ["Z0", "Z1"], ["ZI%ds" % n1], 0.5, (), ("zl%d" % n1, ne, 2.0))
-        KDK, ULK = [("KD", 0), ("KD", 1)], [("UL", 0), ("UL", 1)]
-        copy(T.OF[:], T.OU[:], [("OU", 0), ("OU", 1)], ["OF"], 256)
-        for h in range(2):
-            us, a, uk = T["P%d" % (4 + h)][:, 384 * h:384 * h + 128], 128 * h, [("US", h, k) for k in (3, 7, 11, 15)]
-            ts(T.P4[:, 128 + a:256 + a], us, 254.0, OP.is_lt, None, None, uk, [("GG", h)], 128, [4, 5])
-            ts(T.P5[:, a:a + 128], us, 254.0, OP.is_lt, T.C37[:, 0:1], OP.mult, uk + ["C37"], [("W0", h)], 128, [4, 5])
-        tt(T.OG[:], T.OF[:], T.P4[:, 128:384], OP.mult, ["OF", ("GG", 0), ("GG", 1)], ["OG"], 256, [4], 1.0)
-        tt(T.P5[:, 0:256], T.OF[:], T.P5[:, 0:256], OP.add, ["OF", ("W0", 0), ("W0", 1)], ["W1"], 256, [5], 1.0)
-        ts(T.GO[:], T.KD[:], 31.0, OP.is_equal, None, None, KDK, ["GO"], 16)
-        ts(T.NN[:], T.KD[:], 0.0, OP.is_lt, None, None, KDK, ["NN"], 16)
-        tt(T.GN[:], T.GO[:], T.NN[:], OP.add, ["GO", "NN"], ["GN"], 16)
-        ts(T.T36[:], T.GN[:], 36.0, OP.mult, 1.0, OP.add, ["GN"], ["T36"], 16)
-        tt(T.BM[:], T.T36[:], T.MF[:], OP.mult, ["T36", "MF"], ["BM"], 16)
-        ts(T.CA[:], T.GO[:], -1.0, OP.mult, 1.0, OP.add, ["GO"], ["CA"], 16)
-        tt(T.CB[:], T.CA[:], T.SX[:], OP.mult, ["CA", "SX"], ["CB"], 16)
-        UL = T.P2[:, 400:416]
-        tt(T.UM[:], T.GN[:], UL, OP.mult, ULK + ["GN"], ["UM"], 16, [2])
-        copy(T.UI[:], UL, ULK, ["UI"], 16, [2])
-        tt(T.MI[:], T.UM[:], T.BM[:], OP.add, ["UM", "BM"], ["MI"], 16)
-        ts(T.MI2[:], T.MI[:], 1023, OP.bitwise_and, None, None, ["MI"], ["MI2"], 16)
-        if t < 3:
-            copy(T.MS[:], T.MI2[:], ["MI2"], ["MS"], 16)
-            op("G", lambda q, n1=n1: send(q, T.MS, "MU%d" % n1, "m%%s%d" % n1), ["MS"], ["MU%ds" % n1], 0.5, (), ("ml%d" % n1, ne, 2.0))
-        else:
-            copy(T.YM[:], T.MI2[:], ["MI2"], ["YM"], 16)
-        tt(T.XA[:], T.MI2[:], T.GO[:], OP.mult, ["MI2", "GO"], ["XA"], 16)
-        tt(T.X[:], T.XA[:], T.CB[:], OP.add, ["XA", "CB"], ["X"], 16)
-        copy(T.XU[:], T.X[:], ["X"], ["XU"], 16)
-        ts(T.UI2[:], T.UI[:], 4095, OP.bitwise_and, None, None, ["UI"], ["UI2"], 16)
-        copy(T.UU[:], T.UI2[:], ["UI2"], ["UU"], 16)
-        tt(T.DM[:], T.SX[:], T.X[:], OP.subtract, ["SX", "X"], ["DM"], 16)
-        act(T.YB[:], T.BT[:].indirect(T.XU[:]), AF.Copy, ["BT", "XU"], ["YB"], 256, gather=True)
-        for gg in range(8):
-            if gg in (1, 4, 7): act(T.BD[:, :, gg, :], T.YB[:], AF.Copy, ["YB", "MSK"], [("BD", gg)], 256, scale=T.MSK[:, gg:gg + 1])
-            else: ts(T.BD[:, :, gg, :], T.YB[:], T.MSK[:, gg:gg + 1], OP.mult, None, None, ["YB", "MSK"], [("BD", gg)], 256, (), 0.5)
-        for cs, bank in (((14, 15), 1), ((12, 13), 3), ((10, 11), 0), ((7, 8, 9), 7), ((0, 1, 2, 3, 4, 5, 6), 6)):
-            off, P, lst, red = 0, T["P%d" % bank], [], []
-            for c in cs:
-                lh, nn = T.BD[:, c, :, :], 16 * c + 16
-                if c: lst.append((P[:, off:off + 16 * c], lh, T.YB[:, 0:16 * c], True, True))
-                lst.append((P[:, off + 16 * c:off + nn], lh, T.YB[:, 16 * c:nn], True, False))
-                lst.append((P[:, off + 16 * c:off + nn], T.IDN[:], T.TM[:], False, True))
-                red.append((c, off, nn))
-                off += nn
-            mm(lst, [("BD", gg) for gg in range(8)] + ["YB", "IDN", "TM"], [("E", bank)], off + 100 * len(cs), [bank])
-            for c, o, nn in red:
-                if c < 10: V(lambda q, c=c, o=o, nn=nn, P=P: q.tensor_reduce(T.DVX[:, c:c + 1], P[:, o:o + nn], AxisListType.X, OP.max), [("E", bank)], [("DF", c)], nn, [bank])
-                else: act(T.JK[:, 0:nn], P[:, o:o + nn], AF.Relu, [("E", bank)], ["JK", ("DF", c)], nn, [bank], bias=-15.0, accum_out=T.DA[:, c:c + 1])
-        ts(T.DF[:, 0:10], T.DVX[:, 0:10], 15.5, OP.is_ge, None, None, [("DF", c) for c in range(10)], ["DF0"], 10)
-        ts(T.DF[:, 10:16], T.DA[:, 10:16], 0.5, OP.is_ge, None, None, [("DF", c) for c in range(10, 16)], ["DF1"], 6)
-        tt(T.XD[:], T.DF[:], T.DM[:], OP.mult, ["DF0", "DF1", "DM"], ["XD"], 16)
-        tt(T.XF[:], T.XD[:], T.X[:], OP.add, ["XD", "X"], ["XF"], 16)
-        copy(T.XFU[:], T.XF[:], ["XF"], ["XFU"], 16)
-        V(lambda q: q.tensor_tensor(T.PP[:], T.IOTA[:].indirect(T.UU[:]), T.OG[:], OP.mult), ["IOTA", "UU", "OG"], ["PP"], 256, (), CG)
-        ts(T.SS[:], T.PP[:], 5, OP.arith_shift_right, None, None, ["PP"], ["SS"], 256)
-        tt(T.TT[:], T.SS[:], T.P5[:, 0:256], OP.add, ["SS", "W1"], ["TT"], 256, [5], 1.0)
-        ts(T.NW[:], T.TT[:], 4095, OP.bitwise_and, None, None, ["TT"], ["NW"], 256)
-        if t < 3:
-            copy(T.MC[:].indirect(T.XFU[:]), T.NW[:], ["NW", "XFU"], ["MC"], 256, (), 3.8)
-            ts(T.GOB[:], T.KD[:], 31.0, OP.is_equal, None, None, KDK, ["GOB"], 16)
-            mm([(T.P7[:, 496:512], T.ON[:, 0:128], T.GOB[:], True, True)], ["ON", "GOB"], ["APS"], 64, [7])
-            V(lambda q: q.tensor_reduce(T.AC[:], T.P7[:, 496:512], AxisListType.X, OP.add), ["APS"], ["AC"], 16, [7])
-            copy(T.AI[:], T.AC[:], ["AC"], ["AI"], 1)
-            ts(T.AP[:], T.AI[:], 1, OP.bitwise_and, None, None, ["AI"], ["AP"], 1)
-            ts(T.AT[:], T.AP[:], -128.0, OP.mult, -1472.0, OP.add, ["AP"], ["AT"], 1)
-            ts(T.TH[:], T.ON[:, 0:128], T.AT[:, 0:1], OP.mult, None, None, ["ON", "AT"], ["TH"], 128, (), 0.5)
-        else:
-            copy(T.MCF[:, 0:1024], T.MC[:, 0:1024], ["MC"], ["MCF"], 1024)
-            copy(T.MCF[:].indirect(T.XFU[:]), T.NW[:], ["NW", "XFU"], ["MCF"], 256, (), 3.8)
-            op("S", lambda q: q.dma_start(T.yz[:], T.ZF[:]), ["ZF0", "ZF1"], [], 0.1, (), ("so0", 16, 2))
-            op("S", lambda q: q.dma_start(T.ym[:], T.YM[:]), ["YM"], [], 0.1, (), ("so1", 16, 2))
-            op("S", lambda q: q.dma_start(T.ymc[:], T.MCF[:, 0:1024]), ["MCF"], [], 0.1, (), ("so2", 16, 4))
+            pa = v("P6", S[300:316])
+            mm("A", [(pa, ON, v("NG"))])
+            act("AC", v("JK"), pa, AF.Identity, -0.5, 1.0 / 64, v("AC"))
+            ts("RY", v("RY"), v("AC"), MAGIC, OP.add, MAGIC, OP.subtract)
+            act("PM", v("PM"), v("NON"), AF.Sign, v("AC"), v("RY"))
+    dma("S", T.ymc[:], T.MC[:, 0:1024], [v("MC")], [], "so2", 3.5)
+    dma("S", T.yz[:], T.ZF[:], [v("ZF")], [], "so0", 2.5)
+    dma("S", T.ym[:], T.YM[:], [v("YM")], [], "so1", 2.0)
     return ops
 
 
-def name_of(o):
-    w = o["w"][0] if o["w"] else "out"
-    if not isinstance(w, tuple): return w
-    piece = w[0] in ("PB", "AB")
-    return w[0] + (str(w[1]) if piece or w[0] in ("C", "OU", "US", "UL", "KD", "D") else "") + (str(w[2]) if piece else "")
-
-
-def schedule(ops):
-    off = {k: float(v) for k, v in (x.split("=") for x in OFF.split())}
-    pin = dict(x.split("=") for x in PIN.split())
+def schedule(ops, par):
     n = len(ops)
-    kids = [[] for _ in ops]
-    need = [0] * n
+    kids, need = [[] for _ in ops], [0] * n
     for i, o in enumerate(ops):
-        for d in o["hard"] | o["soft"]:
+        for d in o["raw"] | o["war"]:
             kids[d].append(i)
             need[i] += 1
-    lat = [o["done"][2] if o["done"] else o["cost"] for o in ops]
-    prio = [0.0] * n
+    lat = [o["done"][2] if o["done"] else min(o["cost"][e] for e in o["eng"]) for o in ops]
+    due = [0.0] * n
     for i in range(n - 1, -1, -1):
-        prio[i] = lat[i] + 0.08 + max([prio[k] for k in kids[i]] + [0.0])
-    prio = [p + off.get(name_of(o), 0.0) for p, o in zip(prio, ops)]
-    for o in ops:
-        if len(o["eng"]) > 1: o["cand"] = pin.get(name_of(o), o["eng"])
-        else: o["cand"] = o["eng"]
-    free, fin, start, est = dict.fromkeys("VATGS", 0.0), [0.0] * n, [0.0] * n, [0.0] * n
-    ready = [i for i in range(n) if need[i] == 0]
-    order = []
+        o = ops[i]
+        due[i] = par["period"] * o["step"] + par["tau"].get(o["name"], 0.0) if o["step"] >= 0 else min([due[k] for k in kids[i]] + [99.0]) - lat[i] - par["wake"]
+    prio = [-x for x in due]
+    free, start, fin = dict.fromkeys("VATGS", 0.0), [0.0] * n, [0.0] * n
+    user = {"P%d" % b: {} for b in range(8)}
+    idle = ["P%d" % b for b in par["dbanks"]]
+    ready, order = [i for i in range(n) if need[i] == 0], []
+
+    def plan(i, e):
+        o = ops[i]
+        hard = set(o["raw"]) | {d for d in o["war"] if ops[d]["eng"] != "T" or e != "T"}
+        banks = set(o["banks"])
+        if o["dyn"]: banks.add(idle[0] if o["dyn"][0] == "take" else o["dyn"][1]["bank"])
+        hard |= {d for b in banks for x, d in user[b].items() if x != e}
+        b = max([fin[d] + (par["own"] if ops[d]["eng"] == e else par["wake"]) for d in hard] + [free[e] if e else 0.0])
+        return b, e, hard, banks
+
     while ready:
-        beg = []
+        cand = []
         for i in ready:
-            e = ops[i]["cand"]
-            beg.append(est[i] if not e else max(est[i], free[e]) if len(e) == 1 else max(est[i], min(free["V"] + DV, free["A"])))
-        m = min(beg) + EPS
-        best = None
-        for i, b in zip(ready, beg):
-            if b <= m and (best is None or prio[i] > prio[best[0]]): best = (i, b)
-        i, b = best
+            o = ops[i]
+            if o["dyn"] and o["dyn"][0] == "take" and not idle: continue
+            cand.append((i, min((plan(i, e) for e in (o["eng"] or [""])), key=lambda p: p[0] + o["cost"].get(p[1], 0.0))))
+        m = min(c[1][0] for c in cand) + par["eps"]
+        i, (b, e, hard, banks) = max((c for c in cand if c[1][0] <= m), key=lambda c: prio[c[0]])
         o = ops[i]
         ready.remove(i)
-        e = o["cand"]
-        if len(e) > 1: e = "V" if free["V"] + DV <= free["A"] else "A"
-        if len(o["eng"]) > 1: o["fn"] = (lambda f, e: lambda q: f(q, e))(o["fn"], e)
-        o["eng"] = o["cand"] = e
-        if e:
-            b = max(est[i], free[e])
-            free[e] = b + o["cost"]
-        start[i], fin[i] = b, b + lat[i]
+        o["eng"], o["hard"] = e, hard
+        if o["dyn"]:
+            if o["dyn"][0] == "take": o["dyn"][1]["bank"] = idle.pop(0)
+            else: idle.append(o["dyn"][1]["bank"])
+        for x in banks: user[x][e] = i
+        if e: free[e] = b + o["cost"][e]
+        start[i], fin[i] = b, b + (o["done"][2] if o["done"] else o["cost"][e])
         order.append(i)
         for k in kids[i]:
             need[k] -= 1
-            w = 0.06 if ops[k]["cand"] == e else WAKE
-            est[k] = max(est[k], fin[i] + w if i in ops[k]["hard"] else start[i])
             if need[k] == 0: ready.append(k)
     return order, start, fin
 
@@ -367,9 +372,8 @@ def rank_program(g, core, T, topo):
     rank = T.rank_of(core)
     if rank is None:
         return
-    nxt = T.cores[(rank + 1) % len(T.cores)]
-    ops = build(T, topo, core, nxt)
-    order, _, _ = schedule(ops)
+    ops = build(T, topo, core, T.cores[(rank + 1) % len(T.cores)], PAR)
+    order, _, _ = schedule(ops, PAR)
     Q = {"V": g.vector, "A": g.scalar, "T": g.tensor, "G": g, "S": g.sync}
     cnt = {e: 0 for e in Q}
     done, know = {}, {}
@@ -384,18 +388,18 @@ def rank_program(g, core, T, topo):
         kn = known[e]
         wants = {}
         for d in o["hard"]:
-            s, v = done[d]
-            if kn.get(s, 0) < v and wants.get(s, (0, 0))[0] < v: wants[s] = (v, d)
+            s, c = done[d]
+            if kn.get(s, 0) < c and wants.get(s, (0, 0))[0] < c: wants[s] = (c, d)
         for s in sorted(wants, key=lambda s: -wants[s][1]):
-            v, d = wants[s]
-            if kn.get(s, 0) >= v: continue
-            Q[e].wait_ge(T.sem[s], v)
+            c, d = wants[s]
+            if kn.get(s, 0) >= c: continue
+            Q[e].wait_ge(T.sem[s], c)
             for a, b in know[d].items():
                 if kn.get(a, 0) < b: kn[a] = b
-        x = o["fn"](Q[e])
+        x = o["fn"](Q[e], e)
         if o["done"]:
             done[i] = o["done"][:2]
-            if x is not None: x.then_inc(T.sem[done[i][0]], done[i][1])
+            if x is not None and o["name"] == "dma": x.then_inc(T.sem[done[i][0]], done[i][1])
         else:
             cnt[e] += 1
             done[i] = ("s" + e, cnt[e])
@@ -404,7 +408,7 @@ def rank_program(g, core, T, topo):
         know[i][done[i][0]] = done[i][1]
     kn = known["S"]
     for i in reversed(order):
-        s, v = done[i]
-        if kn.get(s, 0) < v:
-            g.sync.wait_ge(T.sem[s], v)
-            kn[s] = v
+        s, c = done[i]
+        if kn.get(s, 0) < c:
+            g.sync.wait_ge(T.sem[s], c)
+            kn[s] = c

@@ -26,13 +26,16 @@ SEMAPHORES = ["sV", "sA", "sT", "sG", "so0", "so1", "so2"] + ["ld_" + x[1] for x
 
 BIG, TOP, MAGIC = 2.0 ** 25, 2.0 ** 23, 1.5 * 2.0 ** 23
 PAR = {
-    "cyc": 0.00087, "ovV": 0.045, "ovA": 0.06, "ovT": 0.03, "wake": 0.1, "own": 0.06, "cg": 1.56, "cs": 3.8, "pf": 0.5, "far": 2.0, "eps": 0.1,
+    "cyc": 0.00087, "ovV": 0.045, "ovA": 0.06, "ovT": 0.03, "ovM": 0.0, "wake": 0.1, "own": 0.06, "cg": 1.56, "cs": 3.8, "pf": 0.5, "far": 2.0, "eps": 0.1,
     "kind": {(0, 1): "VVAV", (1, 1): "AAAA", (0, 0): "VVVA", (1, 0): "AAAA"},
     "one": {(0, 1): "V", (1, 1): "A", (0, 0): "A", (1, 0): "V"},
     "pieces": 2, "dbanks": (0, 1, 2), "period": 20.0,
 }
 TAU = ("send=-1.3 G0=-1.2 a10=-0.7 OU1=-0.5 dma=-0.4 p10=0.1 p11=1 G1=1.2 zt0=1.3 VG10=1.9 PP0=2.2 ZT10=2.3 OU0=2.4 ZT1=2.9 c010=2.9 zt1=3.3 n11=3.4 K1=3.9 c10m=4 p00=4.1 n10=4.3 a11=4.7 P00=4.9 e01=4.9 P01=5.1 c10=5.2 put0=5.2 d010=5.4 ZT0=5.7 x11=5.7 p01=6 KU00=6 Z10=6 a00=6.1 a01=6.1 Y0=6.2 K0=6.5 DG10=6.6 x10=6.8 NO1=7 KU10=7.1 KS00=7.2 Z11=7.5 KS10=7.7 xt1=7.7 n00=7.9 c00m=8.1 x00=8.1 d001=8.3 d000=8.4 ZT11=8.5 Ml1=8.6 us1=8.7 Mb1=8.7 NG1=8.8 T20=8.8 XP0=8.8 W01=9 c00=9.1 d011=9.1 KS11=9.2 VG11=9.2 X0=9.2 OG0=9.4 Y1=9.5 O321=9.6 XF1=9.6 OG1=9.7 ub1=9.8 VG00=10 R01=10.1 xt0=10.1 xb1=10.6 xl1=10.7 M41=10.9 gn1=10.9 UI0=10.9 c11m=11 cg1=11 MI1=11 UI1=11 e00=11 c11=11.1 us0=11.2 Y10=11.3 NW1=11.3 Y11=11.5 c000=11.5 SC0=11.5 Ml0=11.6 X1=11.7 W0=11.7 NE1=11.8 Mb0=11.8 put1=12 KU11=12.1 D01=12.1 O320=12.1 xb0=12.1 DG11=12.2 XP1=12.2 W00=12.2 ub0=12.2 DM1=12.3 xl0=12.3 gn0=12.4 MI0=12.5 DG00=12.6 T21=12.8 M40=12.8 TQ1=13.3 NW0=13.4 W1=13.5 MN1=13.6 NE0=13.6 R00=13.9 cg0=13.9 Z0=14.2 D00=14.3 SC1=14.6 NO0=14.7 c01m=14.7 TQ0=14.7 PP1=14.8 c011=14.9 AC=15.2 Z1=15.3 NN1=15.4 MS1=15.4 n01=15.7 NG0=16.1 c001=16.5 DM0=16.7 VG01=17.2 MS0=17.3 KU01=17.9 DG01=18.4 KS01=19.4 x01=19.6 c01=19.8 PM=19.9 A=20 XF0=20.2 NN0=20.3 MN0=20.5 RY=22.7")
 PIN = "AB0=V G0=VA G1=A Mb0=VA Mb1=VA O320=A O321=A P00=A P01=A PBz=VA RMN=A RMW=A VB=A Y0=VA Y1=A Y10=A Y11=VA ZT0=A ZT1=A a00=VA a01=VA a10=A a11=VA p00=A p01=VA p10=A p11=V"
+TAU = "Y10=-17.7 n11=-6.3 zt0=-6.2 OG0=-4.3 OU1=-2.5 ZT10=-2.4 G1=-2 p00=-1.6 XP0=-1.1 a10=-1 PP0=0 put0=0 xt1=-0 G0=0.1 OU0=0.2 c010=0.3 send=0.5 P01=1.2 x01=1.5 K1=1.7 dma=1.9 p11=2 zt1=2.4 ZT1=2.8 x10=3.6 VG10=3.7 p10=4.2 c10=4.2 X0=4.3 e01=4.7 a11=4.9 c10m=5 NG1=5 x11=5.2 d010=5.4 KS10=5.4 d000=5.5 Y0=5.7 Y1=5.7 p01=6.1 P00=6.2 ZT0=6.2 KS00=6.3 X1=6.6 us1=6.7 n10=7.4 DG10=7.6 x00=7.7 TQ0=7.7 ZT11=7.9 c00m=8.1 Z11=8.2 a00=8.3 d001=8.3 KS11=8.3 n00=8.4 c11m=8.6 Z10=8.9 KU10=8.9 W01=9 cg0=9 c00=9.1 K0=9.3 UI0=9.4 O320=9.4 Ml1=9.5 Mb1=9.6 d011=9.6 ub1=9.8 M40=9.8 a01=9.9 XF1=10.1 xt0=10.1 Mb0=10.5 xb1=10.6 XP1=10.6 xl1=10.7 gn1=10.7 NE1=10.7 us0=10.8 VG11=11 cg1=11 Y11=11 T20=11.5 M41=11.6 W0=11.6 W1=11.6 xb0=11.7 NW1=11.9 KU11=11.9 ub0=11.9 xl0=11.9 VG00=12.2 put1=12.2 DG11=12.2 DM1=12.3 DM0=12.3 R01=12.6 NE0=12.7 Ml0=12.9 SC0=13.3 NN1=13.5 c11=13.7 MI0=13.8 KU00=13.9 D01=13.9 NO0=13.9 c011=13.9 gn0=14 TQ1=14.1 D00=14.2 W00=14.3 DG00=14.3 n01=14.7 c01=14.8 AC=14.9 R00=15 NG0=15 MN0=15.4 O321=15.5 MI1=15.6 NO1=15.7 c01m=15.7 VG01=16 T21=16.3 NW0=16.5 SC1=16.7 c001=16.7 e00=16.8 MS1=16.8 UI1=17 MS0=17 OG1=17.7 Z1=17.8 MN1=18.6 KU01=18.7 Z0=18.9 NN0=19.1 A=19.4 c000=20 XF0=20.2 KS01=21 PP1=22.5 RY=23.5 PM=24.6 DG01=24.8"
+PIN = "AB0=A G0=VA G1=V Mb0=VA Mb1=V O320=A O321=V P00=VA P01=A PBz=VA RMN=A RMW=VA VB=A Y0=V Y1=A Y10=A Y11=A ZT0=A ZT1=A a00=A a01=VA a10=VA a11=VA p00=V p01=A p10=A p11=V"
+PAR.update(dict(cyc=.00083, ovV=.01, ovA=.02, wake=.24, own=.24, eps=0.15))
 PAR["tau"] = {k: float(x) for k, x in (y.split("=") for y in TAU.split())}
 PAR["pin"] = dict(y.split("=") for y in PIN.split())
 
@@ -113,7 +116,7 @@ def build(T, topo, core, nxt, par):
 
     def fill(o, c): return op("fill", "V", lambda q, e: q.memset(o["ap"], c), [], [o], price(o, []))
 
-    def mmcost(ns): return {"T": par["ovT"] + sum(max(64, n) for n in ns) * par["pf"] * cyc}
+    def mmcost(ns): return {"T": par["ovT"] + sum(max(64, n) * par["pf"] * cyc + par["ovM"] for n in ns)}
 
     def mm(nm, lst, first=True, final=True):
         def fn(q, e):

@@ -3,69 +3,76 @@ from concourse.mybir import AluOpType as OP, ActivationFunctionType as AF
 
 F, H, I, U = "float32", "bfloat16", "int32", "uint16"
 S = np.s_
-SB = {"MCI": (1024, I), "MC": (1040, F), "PR": (4096, H), "AD": (4096, H), "GL": (1024, H), "M0": (16, I), "DV": (8, H), "WT": (1, H),
+SB = {"MCI": (1024, I), "MC": (1280, F), "PR": (4096, H), "AD": (4096, H), "GL": (1024, H), "M0": (16, I), "DV": (8, H), "WT": (1, H),
       "DVF": (8, F), "WS": (1, F), "W4": (1, F), "OU": (256, U), "NO": (256, F), "O32": (256, F), "Z": (256, H), "ZF": (256, F), "MS": (16, U), "YM": (16, F),
-      "KV": (144, F), "IOTA": (1024, F), "VB": (4128, H), "ON": (2048, H), "NON": (128, H), "IDN": (128, H), "NID": (128, H), "BLK": (128, H), "BLB": (128, H),
+      "KV": (288, F), "IOTA": (1024, F), "VB": (8224, H), "ON": (2048, H), "NON": (128, H), "IDN": (128, H), "NID": (128, H), "BLK": (128, H), "BLB": (128, H),
       "BW": (128, H), "BW4": (128, H), "BN": (128, H), "CMB": (256, H), "PM": (128, H), "MSK": (8, F), "PI": (1, I), "PR16": (1, I), "R16": (1, F), "R32": (1, F),
-      "C37": (1, F), "SPR": (1, F), "I16": (128, F), "CI": (8, F), "CL": (8, U), "RS": (128, H), "BN0": (136, H), "BN1": (136, H),
-      "E": (2048, H), "NG": (16, H), "JK": (16, F), "AC": (1, F), "RY": (1, F), "M4": (16, F)}
-for _h in "0123": SB["ZI" + _h], SB["MU" + _h] = (256, H), (16, U)
-for _h in "01":
-    for _n, _w, _d in (("AB", 4128, H), ("PB", 4112, H), ("KB", 4096, H), ("KS", 144, F), ("KU", 8, U), ("VG", 128, H), ("DG", 128, H), ("R0", 128, H),
-                       ("Y", 128, H), ("ZT", 128, H), ("Z1", 128, H), ("M37", 264, F), ("MI", 264, I), ("UI", 264, I), ("X", 136, F), ("NE", 128, H), ("SC", 128, H),
-                       ("T2", 8, F), ("XF", 16, U), ("W", 128, F), ("XP", 128, I), ("NW", 128, I), ("D0", 8, F), ("DM", 8, F), ("NN", 8, F), ("TQ", 8, F), ("MN", 8, F)):
-        SB[_n + _h] = (_w, _d)
+      "C37": (1, F), "I17": (17, F), "DI": (17, F), "DJ": (17, F), "SP": (16, F), "SPT": (16, F), "BT": (272, H), "KI": (288, F), "GO": (16, H), "JK": (16, F), "AC": (1, F), "RY": (1, F),
+      "AB": (8320, H), "PB": (8320, H), "KB": (8192, H), "KS": (288, F), "KU": (16, U), "VG": (256, H), "DG": (256, H), "R0": (256, H), "Y": (256, H), "Z1": (256, H),
+      "M37": (528, F), "MI": (528, I), "UI": (528, I), "X": (272, F), "NE": (2200, F), "SC": (2200, F), "RS": (2200, F), "XF": (32, U), "W": (256, F), "XP": (256, I), "NW": (256, I)}
+for _n in ("M4", "D0", "VF", "NN", "TQ", "MN"): SB[_n] = (16, F)
+for _t in "0123": SB["ZI" + _t], SB["MU" + _t] = (256, H), (16, U)
 SCRATCH = {k: ("sbuf", [128, w], d) for k, (w, d) in SB.items()}
-for _h in "01": SCRATCH["C" + _h] = ("sbuf", [128, 128, 18], H)
+SCRATCH["C"] = ("sbuf", [128, 256, 18], H)
 for _n in ("RMC", "RMN", "RMW"): SCRATCH[_n] = ("sbuf", [128, 16, 8, 16], H)
-SCRATCH["BR"] = ("sbuf", [128, 8, 8, 18], H)
+SCRATCH["BR"] = ("sbuf", [128, 12, 16, 18], H)
 for _b in range(8): SCRATCH["P%d" % _b] = ("psum", [128, 512], F)
-LOADS = (("S", "m0", "M0", 2.0), ("S", "mc", "MCI", 4.0), ("S", "pr", "PR", 6.5), ("S", "ad", "AD", 8.5), ("S", "gl", "GL", 9.2), ("S", "z0", "ZI0", 9.5),
-         ("A", "wt", "WT", 2.5), ("A", "dv", "DV", 2.5))
-SEMAPHORES = ["sV", "sA", "sT", "sG", "so0", "so1", "so2"] + ["ld_" + x[1] for x in LOADS] + ["%s%d%d" % (n, t, h) for n in ("zi", "mi", "zl", "ml") for t in range(1, 4) for h in range(2)]
+SEMAPHORES = ["sV", "sA", "sT", "sG", "so0", "so1", "so2"] + ["ld_" + n for n in ("m0", "mc", "pr", "ad", "gl", "z0", "wt", "dv")]
+SEMAPHORES += ["%s%d%d" % (n, t, h) for n in ("zi", "mi", "zl", "ml") for t in range(1, 4) for h in range(3)]
 
 BIG, TOP, MAGIC = 2.0 ** 25, 2.0 ** 23, 1.5 * 2.0 ** 23
 PAR = {
-    "cyc": 0.00087, "ovV": 0.045, "ovA": 0.06, "ovT": 0.03, "ovM": 0.0, "wake": 0.1, "own": 0.06, "cg": 1.56, "cs": 3.8, "pf": 0.5, "far": 2.0, "eps": 0.1,
-    "kind": {(0, 1): "VVAV", (1, 1): "AAAA", (0, 0): "VVVA", (1, 0): "AAAA"},
-    "one": {(0, 1): "V", (1, 1): "A", (0, 0): "A", (1, 0): "V"},
-    "pieces": 2, "dbanks": (0, 1, 2), "period": 20.0,
+    "cyc": 0.00083, "ovV": 0.0, "ovA": 0.0, "ovT": 0.03, "ovI": 0.05, "min": 64, "wake": 0.22, "cg": 1.56, "cs": 3.8, "pf": 0.5, "far": 2.0,
+    "loads": (("S", "m0", "M0", 2.0), ("S", "mc", "MCI", 4.0), ("S", "pr", "PR", 6.5), ("S", "ad", "AD", 8.5), ("S", "gl", "GL", 9.2), ("S", "z0", "ZI0", 9.5),
+              ("A", "wt", "WT", 2.5), ("A", "dv", "DV", 2.5)),
+    "chunks": ((8, 8), (0, 8)),
+    "passes": ((0, 0), (1, 0), (0, 1), (1, 1)),
+    "scalar": {(0, 0): 0, (1, 0): 8, (0, 1): 12, (1, 1): 12},
+    "split": (2, 2), "group": (8, 8), "zp": "", "pieces": 2, "pin": {}, "bias": 0.0, "no": "01", "period": 20.0, "due": {},
 }
-TAU = ("send=-1.3 G0=-1.2 a10=-0.7 OU1=-0.5 dma=-0.4 p10=0.1 p11=1 G1=1.2 zt0=1.3 VG10=1.9 PP0=2.2 ZT10=2.3 OU0=2.4 ZT1=2.9 c010=2.9 zt1=3.3 n11=3.4 K1=3.9 c10m=4 p00=4.1 n10=4.3 a11=4.7 P00=4.9 e01=4.9 P01=5.1 c10=5.2 put0=5.2 d010=5.4 ZT0=5.7 x11=5.7 p01=6 KU00=6 Z10=6 a00=6.1 a01=6.1 Y0=6.2 K0=6.5 DG10=6.6 x10=6.8 NO1=7 KU10=7.1 KS00=7.2 Z11=7.5 KS10=7.7 xt1=7.7 n00=7.9 c00m=8.1 x00=8.1 d001=8.3 d000=8.4 ZT11=8.5 Ml1=8.6 us1=8.7 Mb1=8.7 NG1=8.8 T20=8.8 XP0=8.8 W01=9 c00=9.1 d011=9.1 KS11=9.2 VG11=9.2 X0=9.2 OG0=9.4 Y1=9.5 O321=9.6 XF1=9.6 OG1=9.7 ub1=9.8 VG00=10 R01=10.1 xt0=10.1 xb1=10.6 xl1=10.7 M41=10.9 gn1=10.9 UI0=10.9 c11m=11 cg1=11 MI1=11 UI1=11 e00=11 c11=11.1 us0=11.2 Y10=11.3 NW1=11.3 Y11=11.5 c000=11.5 SC0=11.5 Ml0=11.6 X1=11.7 W0=11.7 NE1=11.8 Mb0=11.8 put1=12 KU11=12.1 D01=12.1 O320=12.1 xb0=12.1 DG11=12.2 XP1=12.2 W00=12.2 ub0=12.2 DM1=12.3 xl0=12.3 gn0=12.4 MI0=12.5 DG00=12.6 T21=12.8 M40=12.8 TQ1=13.3 NW0=13.4 W1=13.5 MN1=13.6 NE0=13.6 R00=13.9 cg0=13.9 Z0=14.2 D00=14.3 SC1=14.6 NO0=14.7 c01m=14.7 TQ0=14.7 PP1=14.8 c011=14.9 AC=15.2 Z1=15.3 NN1=15.4 MS1=15.4 n01=15.7 NG0=16.1 c001=16.5 DM0=16.7 VG01=17.2 MS0=17.3 KU01=17.9 DG01=18.4 KS01=19.4 x01=19.6 c01=19.8 PM=19.9 A=20 XF0=20.2 NN0=20.3 MN0=20.5 RY=22.7")
-PIN = "AB0=V G0=VA G1=A Mb0=VA Mb1=VA O320=A O321=A P00=A P01=A PBz=VA RMN=A RMW=A VB=A Y0=VA Y1=A Y10=A Y11=VA ZT0=A ZT1=A a00=VA a01=VA a10=A a11=VA p00=A p01=VA p10=A p11=V"
-TAU = "Y10=-17.7 n11=-6.3 zt0=-6.2 OG0=-4.3 OU1=-2.5 ZT10=-2.4 G1=-2 p00=-1.6 XP0=-1.1 a10=-1 PP0=0 put0=0 xt1=-0 G0=0.1 OU0=0.2 c010=0.3 send=0.5 P01=1.2 x01=1.5 K1=1.7 dma=1.9 p11=2 zt1=2.4 ZT1=2.8 x10=3.6 VG10=3.7 p10=4.2 c10=4.2 X0=4.3 e01=4.7 a11=4.9 c10m=5 NG1=5 x11=5.2 d010=5.4 KS10=5.4 d000=5.5 Y0=5.7 Y1=5.7 p01=6.1 P00=6.2 ZT0=6.2 KS00=6.3 X1=6.6 us1=6.7 n10=7.4 DG10=7.6 x00=7.7 TQ0=7.7 ZT11=7.9 c00m=8.1 Z11=8.2 a00=8.3 d001=8.3 KS11=8.3 n00=8.4 c11m=8.6 Z10=8.9 KU10=8.9 W01=9 cg0=9 c00=9.1 K0=9.3 UI0=9.4 O320=9.4 Ml1=9.5 Mb1=9.6 d011=9.6 ub1=9.8 M40=9.8 a01=9.9 XF1=10.1 xt0=10.1 Mb0=10.5 xb1=10.6 XP1=10.6 xl1=10.7 gn1=10.7 NE1=10.7 us0=10.8 VG11=11 cg1=11 Y11=11 T20=11.5 M41=11.6 W0=11.6 W1=11.6 xb0=11.7 NW1=11.9 KU11=11.9 ub0=11.9 xl0=11.9 VG00=12.2 put1=12.2 DG11=12.2 DM1=12.3 DM0=12.3 R01=12.6 NE0=12.7 Ml0=12.9 SC0=13.3 NN1=13.5 c11=13.7 MI0=13.8 KU00=13.9 D01=13.9 NO0=13.9 c011=13.9 gn0=14 TQ1=14.1 D00=14.2 W00=14.3 DG00=14.3 n01=14.7 c01=14.8 AC=14.9 R00=15 NG0=15 MN0=15.4 O321=15.5 MI1=15.6 NO1=15.7 c01m=15.7 VG01=16 T21=16.3 NW0=16.5 SC1=16.7 c001=16.7 e00=16.8 MS1=16.8 UI1=17 MS0=17 OG1=17.7 Z1=17.8 MN1=18.6 KU01=18.7 Z0=18.9 NN0=19.1 A=19.4 c000=20 XF0=20.2 KS01=21 PP1=22.5 RY=23.5 PM=24.6 DG01=24.8"
-PIN = "AB0=A G0=VA G1=V Mb0=VA Mb1=V O320=A O321=V P00=VA P01=A PBz=VA RMN=A RMW=VA VB=A Y0=V Y1=A Y10=A Y11=A ZT0=A ZT1=A a00=A a01=VA a10=VA a11=VA p00=V p01=A p10=A p11=V"
-PAR.update(dict(cyc=.00083, ovV=.01, ovA=.02, wake=.24, own=.24, eps=0.15))
-PAR["tau"] = {k: float(x) for k, x in (y.split("=") for y in TAU.split())}
-PAR["pin"] = dict(y.split("=") for y in PIN.split())
+
+
+DUE = "KU00=-6.6 p10=-3.4 p00=-3.1 p01=-2.6 OU0=-1.7 dma=-1.7 NE0=0.2 K0=0.8 a01=0.9 a00=1.2 G0=1.2 P00=1.3 p11=1.3 OU1=1.5 P01=1.5 a10=1.7 zp0=2.3 a11=2.5 c00=3.4 K1=3.4 VG10=3.4 zp1=3.5 G1=3.6 KS00=3.6 VG00=4.1 c10=4.4 cg1=4.4 x10=4.6 d00=4.9 n10=5 R00=5.1 n00=5.2 x00=5.2 Ml0=5.2 ZP0=5.4 Y0=5.6 M40=5.7 DG00=5.8 OG1=6.1 d10=6.4 us0=6.5 O320=6.5 D00=6.8 Z10=6.9 Z0=7.1 R01=7.6 KU10=7.7 M41=7.7 DG10=7.9 ZP1=7.9 VG01=7.9 e00=8 TQ0=8 PP0=8.1 xl1=8.2 Z11=8.3 W0=8.5 TQ1=8.6 gn0=8.9 ub1=8.9 Mb1=9 W1=9 Mb0=9.1 put1=9.2 NO0=9.2 DG01=9.2 GP1=9.2 SC1=9.2 NF1=9.3 Y1=9.5 O321=9.5 KS10=9.6 NE1=9.6 XF1=9.6 X0=9.9 W00=10.1 DM0=10.2 n11=10.2 cg0=10.3 NF0=10.4 PP1=10.5 KS11=10.5 xl0=10.6 OG0=10.6 ub0=10.8 NW0=10.8 MI0=10.9 X1=11 GP0=11.1 SC0=11.4 us1=11.5 XF0=11.5 UI1=11.5 NG1=11.5 W01=12 UI0=12 put0=12 d01=12 NG0=12.1 Ml1=12.2 c01=12.2 n01=12.3 sz0=12.6 D01=12.6 MI1=12.7 NN0=12.7 KS01=12.8 KU01=12.9 XP1=13 c11=13 GO0=13 VF0=13.1 NW1=13.4 Y11=13.4 e01=13.4 NO1=13.6 XP0=13.7 MS0=13.8 DM1=14 DG11=14.2 gn1=14.2 d11=14.5 MS1=14.8 GO1=15 VF1=15.1 AC=15.6 Y10=15.8 RY=16.3 VG11=16.5 NN1=16.5 sm1=16.8 sm0=17.8 Z1=18.6 MN0=19 MN1=19.3 A=20.3 KU11=20.3 PM=21.7 x11=23.4 x01=25.7 sz1=27"
+PIN = "G0=A G1=V Mb0=A Mb1=A O320=A O321=VA P00=A P01=A RMN=VA RMW=A Y0=A Y1=VA Y10=VA Y11=A a00=A a01=V a10=A a11=A p00=VA p01=A p10=A p11=VA"
+PAR.update({"due": {k: float(x) for k, x in (y.split("=") for y in DUE.split())}, "pin": dict(y.split("=") for y in PIN.split())})
+PAR.update({"scalar": {(0, 0): 0, (1, 0): 8, (0, 1): 8, (1, 1): 8}, "group": (2, 4), "zp": "01", "far": 1.5})
+
+
+def cost(w, e, par):
+    kind, n = w
+    if kind == "fix": return n
+    if kind == "mm": return par["ovT"] + sum(max(64, x) for x in n) * par["pf"] * par["cyc"]
+    if kind == "G": return 0.17 + 2 * n * par["cyc"]
+    if kind in ("cg", "cs"): return par["ov" + e] + par["ovI"] * (1.3 if e == "A" else 1.0) + n * par[kind] * par["cyc"]
+    return par["ov" + e] + max(par["min"], n * (1.0 if e == "A" else kind)) * par["cyc"]
 
 
 def build(T, topo, core, nxt, par):
     ops, last, readers, step = [], {}, {}, [-1]
     grid = {k: np.arange(int(np.prod(x[1][1:]))).reshape(x[1][1:]) for k, x in SCRATCH.items()}
-    cyc = par["cyc"]
 
-    def v(name, ix=None):
-        if ix is None: ap, el = T[name][:], grid[name]
+    def v(name, ix=None, rows=S[:]):
+        if ix is None: ap, el = T[name][rows], grid[name]
         else:
             ix = ix if isinstance(ix, tuple) else (ix,)
-            ap, el = T[name][(slice(None),) + ix], grid[name][ix]
-        return {"ap": ap, "el": [(name, np.ravel(el))], "n": int(np.size(el)), "b": 4 if SCRATCH[name][2] in (F, I) else 2, "ps": name[0] == "P" and name[1].isdigit()}
+            ap, el = T[name][(rows,) + ix], grid[name][ix]
+        return {"ap": ap, "el": [(name, np.ravel(el))], "n": int(np.size(el)), "b": 4 if SCRATCH[name][2] in (F, I) else 2, "ps": SCRATCH[name][0] == "psum"}
+
+    def w(name, a, n, step=1): return v(name, S[a:a + (n - 1) * step + 1:step])
 
     def ind(win, off):
         return {"ap": win["ap"].indirect(off["ap"]), "el": win["el"], "off": off["el"], "n": 16 * off["n"], "b": 4, "ps": False}
 
-    def op(name, eng, fn, ins, outs, cost, done=None, after=(), dyn=None):
+    def op(name, eng, fn, ins, outs, work, done=None, after=()):
         i = len(ops)
-        raw, war, banks = set(after), set(), set()
+        raw, war = set(after), set()
         rd = [e for x in ins + outs if isinstance(x, dict) for e in x.get("off", [])] + [e for x in ins if isinstance(x, dict) for e in x["el"]]
         wr = [e for x in outs for e in x["el"]]
         for nm, el in rd + wr:
             if nm not in last: last[nm], readers[nm] = np.full(grid[nm].size, -1), []
-            if nm[0] == "P" and nm[1].isdigit(): banks.add(nm)
         for nm, el in rd: raw.update(np.unique(last[nm][el]).tolist())
         for nm, el in wr:
-            (war if eng == "T" else raw).update(np.unique(last[nm][el]).tolist())
+            war.update(np.unique(last[nm][el]).tolist())
             keep = []
             for r, m in readers[nm]:
                 if m[el].any():
@@ -78,18 +85,19 @@ def build(T, topo, core, nxt, par):
             m = np.zeros(grid[nm].size, bool)
             m[el] = True
             readers[nm].append((i, m))
-        raw -= {-1, i}
-        ops.append({"name": name, "eng": eng, "fn": fn, "raw": raw, "war": war - raw - {-1, i}, "cost": cost, "done": done, "banks": banks, "dyn": dyn, "step": step[0]})
+        deps = (raw | war) - {-1, i}
+        soft = {d for d in deps if eng == "T" and ops[d]["eng"] == "T"}
+        ops.append({"name": name, "eng": eng, "fn": fn, "hard": deps - soft, "soft": soft, "work": work, "done": done, "step": step[0],
+                    "banks": sorted({nm for nm, el in rd + wr if SCRATCH[nm][0] == "psum"})})
         return i
 
-    def price(o, ins, both=False, scalar=False):
+    def price(o, ins, both=False):
         xs = [x for x in ins if isinstance(x, dict)]
         n = max([o["n"]] + [x["n"] for x in xs])
-        if "off" in o: c = a = par["cs"]
-        elif any("off" in x for x in xs): c = a = par["cg"]
-        elif both: c, a = (1.0 if any(x["ps"] for x in xs) else 2.0), 1.0
-        else: c, a = (0.5 if o["b"] == 2 and all(x["b"] == 2 for x in xs if x["n"] > 1) else 1.0), 1.0
-        return {"V": par["ovV"] + max(30, n * c) * cyc, "A": par["ovA"] + max(30, n * a) * cyc}
+        if "off" in o: return ("cs", n)
+        if any("off" in x for x in xs): return ("cg", n)
+        if both: return (1.0 if any(x["ps"] for x in xs) else 2.0, n)
+        return (0.5 if o["b"] == 2 and all(x["b"] == 2 for x in xs if x["n"] > 1) else 1.0, n)
 
     def ap(x): return x["ap"] if isinstance(x, dict) else x
 
@@ -112,42 +120,43 @@ def build(T, topo, core, nxt, par):
             if e == "A": return q.activation(o["ap"], i["ap"], AF.Identity if bias else AF.Copy, bias=ap(bias), scale=ap(scale))
             if bias: return q.tensor_scalar(o["ap"], i["ap"], ap(scale), ap(bias), OP.mult, OP.add)
             return q.tensor_copy(o["ap"], i["ap"]) if scale == 1.0 else q.tensor_scalar(o["ap"], i["ap"], ap(scale), None, OP.mult)
-        return op(nm, par["pin"].get(nm, eng), fn, [i, scale, bias], [o], price(o, [i]))
+        return op(nm, eng, fn, [i, scale, bias], [o], price(o, [i]))
 
     def fill(o, c): return op("fill", "V", lambda q, e: q.memset(o["ap"], c), [], [o], price(o, []))
 
-    def mmcost(ns): return {"T": par["ovT"] + sum(max(64, n) * par["pf"] * cyc + par["ovM"] for n in ns)}
+    def mm(nm, lst, first=True, final=True, size=None):
+        size = size or len(lst)
 
-    def mm(nm, lst, first=True, final=True):
         def fn(q, e):
             x = None
-            for k, (o, l, r) in enumerate(lst): x = q.matmul(o["ap"], l["ap"], r["ap"], first and k == 0, final and k == len(lst) - 1)
+            for k, (o, l, r) in enumerate(lst): x = q.matmul(o["ap"], l["ap"], r["ap"], first and k % size == 0, final and k % size == size - 1)
             return x
-        return op(nm, "T", fn, [x for y in lst for x in y[1:]], [y[0] for y in lst], mmcost([y[2]["n"] for y in lst]))
+        return op(nm, "T", fn, [x for y in lst for x in y[1:]], [y[0] for y in lst], ("mm", [y[2]["n"] for y in lst]))
 
-    def G(o, ins, fn, n): return op("const", "G", lambda q, e: fn(q), ins, [o], {"G": 0.17 + 2 * n * cyc})
+    def G(o, ins, fn): return op("const", "G", lambda q, e: fn(q), ins, [o], ("G", o["n"]))
 
-    def dma(q, o, i, ins, outs, sem, lat): return op("dma", q, lambda x, e: x.dma_start(o, i), ins, outs, {q: 0.1}, (sem, 16, lat))
+    def dma(q, o, i, ins, outs, sem, lat): return op("dma", q, lambda x, e: x.dma_start(o, i), ins, outs, ("fix", 0.1), (sem, 16, lat))
 
-    for q, name, dst, lat in LOADS: dma(q, T[dst][:], T[name][:], [], [v(dst)], "ld_" + name, lat)
+    chunks = par["chunks"]
+    ncm = max(nc for _, nc in chunks)
+    for q, name, dst, lat in par["loads"]: dma(q, T[dst][:], T[name][:], [], [v(dst)], "ld_" + name, lat)
     imp = {"allow_small_or_imprecise_dtypes": True}
-    ON, IDN, NID, R16 = v("ON", S[0:128]), v("IDN"), v("NID"), v("R16")
-    fill(v("ON"), 1.0)
-    G(v("PI"), [], lambda q: q.iota(T.PI[:], [[0, 1]], 0, 1), 1)
-    G(v("BLB"), [ON], lambda q: q.affine_select(T.BLB[:], ON["ap"], [[-16, 8], [0, 16]], OP.is_ge, 0.0, 0, 1), 128)
-    G(v("BLK"), [v("BLB")], lambda q: q.affine_select(T.BLK[:], T.BLB[:], [[16, 8], [0, 16]], OP.is_ge, 0.0, 15, -1), 128)
-    G(v("CMB"), [v("ON")], lambda q: q.affine_select(T.CMB[:], T.ON[:, 0:256], [[-1, 16], [1, 16]], OP.is_equal, 0.0, 0, 0), 256)
-    G(IDN, [ON], lambda q: q.affine_select(T.IDN[:], ON["ap"], [[-1, 128]], OP.is_equal, 0.0, 0, 1), 128)
-    G(v("KV"), [], lambda q: q.iota(T.KV[:], [[512, 8], [2, 18]], 14, 0, **imp), 144)
-    G(v("I16"), [], lambda q: q.iota(T.I16[:], [[0, 8], [1, 16]], 0, 0, **imp), 128)
-    G(v("CI"), [], lambda q: q.iota(T.CI[:], [[1, 8]], 0, 0, **imp), 8)
-    G(v("E"), [v("ON")], lambda q: q.affine_select(T.E[:], T.ON[:], [[-1, 128], [0, 16]], OP.is_equal, 0.0, 0, 1), 2048)
-    G(v("IOTA"), [], lambda q: q.iota(T.IOTA[:], [[1, 1024]], 0, 0, **imp), 1024)
+    ON, IDN, NID, R16 = w("ON", 0, 128), v("IDN"), v("NID"), v("R16")
+    fill(w("ON", 0, 256), 1.0)
+    G(v("PI"), [], lambda q: q.iota(T.PI[:], [[0, 1]], 0, 1))
+    G(v("BLB"), [ON], lambda q: q.affine_select(T.BLB[:], ON["ap"], [[-16, 8], [0, 16]], OP.is_ge, 0.0, 0, 1))
+    G(v("BLK"), [v("BLB")], lambda q: q.affine_select(T.BLK[:], T.BLB[:], [[16, 8], [0, 16]], OP.is_ge, 0.0, 15, -1))
+    G(v("CMB"), [w("ON", 0, 256)], lambda q: q.affine_select(T.CMB[:], T.ON[:, 0:256], [[-1, 16], [1, 16]], OP.is_equal, 0.0, 0, 0))
+    G(IDN, [ON], lambda q: q.affine_select(T.IDN[:], ON["ap"], [[-1, 128]], OP.is_equal, 0.0, 0, 1))
+    KI = w("KI", 0, 18 * ncm)
+    G(KI, [], lambda q: q.iota(KI["ap"], [[512, ncm], [2, 18]], 14, 0, **imp))
+    G(v("I17"), [], lambda q: q.iota(T.I17[:], [[1, 17]], 0, 0, **imp))
+    G(v("IOTA"), [], lambda q: q.iota(T.IOTA[:], [[1, 1024]], 0, 0, **imp))
     copy("MU0", v("MU0"), v("M0"))
-    copy("MC", v("MC", S[0:1024]), v("MCI"))
-    fill(v("MC", S[1024:1040]), 0.0)
-    copy("MSK", v("MSK"), v("BLK", S[0:128:16]))
-    for x in range(8): ts("RMC", v("RMC", S[:, x, :]), v("CMB"), v("MSK", S[x:x + 1]), OP.mult, BIG, OP.mult)
+    copy("MC", w("MC", 0, 1024), v("MCI"))
+    fill(w("MC", 1024, 16 * ncm), 0.0)
+    copy("MSK", v("MSK"), w("BLK", 0, 8, 16))
+    for x in range(8): ts("RMC", v("RMC", S[:, x, :]), v("CMB"), w("MSK", x, 1), OP.mult, BIG, OP.mult)
     lin("RMN", v("RMN"), v("RMC"), -1.0)
     ts("WS", v("WS"), v("WT"), 4.0 / BIG, OP.mult)
     ts("W4", v("W4"), v("WT"), 4.0, OP.mult)
@@ -157,218 +166,239 @@ def build(T, topo, core, nxt, par):
     ts("BN", v("BN"), v("BLK"), -BIG, OP.mult)
     ts("NID", NID, IDN, -1.0, OP.mult)
     copy("DVF", v("DVF"), v("DV"))
-    fill(v("AB1", S[0:16]), 0.0), fill(v("AB1", S[4112:4128]), 0.0), fill(v("AB1", S[17:4112:2]), 0.0), fill(v("AB1", S[47:4112:32]), -256.0)
-    fill(v("AB0", S[0:16]), 0.0), fill(v("AB0", S[4112:4128]), 0.0)
-    lin("AB0", v("AB0", S[17:4112:2]), v("AB1", S[17:4112:2]))
-    for h in "10":
-        lin("PBz", v("PB" + h, S[16:4112:2]), v("ON"), 0.0)
-        fill(v("C" + h, S[:, 0]), 0.0), fill(v("M37" + h, S[0:128]), 0.0)
-    fill(v("VB", S[0:16]), 0.0), fill(v("VB", S[4112:4128]), 0.0)
-    lin("VB", v("VB", S[16:4112:2]), v("ON")), lin("VB", v("VB", S[17:4112:2]), v("ON"), 0.0)
-    fill(v("NON"), -1.0), fill(v("PM"), -1.0), fill(v("BN0"), BIG / 256), fill(v("BN1"), 12 * BIG / 128)
+    for h, (c0, nc) in enumerate(chunks):
+        b, n = 32 * (16 * c0 + 2 - h), 16 * nc
+        fill(w("AB", b, 16), 0.0), fill(w("AB", b + 16 + 32 * n, 16), 0.0), fill(w("AB", b + 17, 16 * n, 2), 0.0), fill(w("AB", b + 47, n, 32), -256.0)
+        fill(w("PB", b + 16, 16 * n, 2), 0.0), fill(w("M37", 33 * c0, n), 0.0)
+    fill(v("C", S[:, 0]), 0.0)
+    fill(w("VB", 0, 16), 0.0), fill(w("VB", 16, 256 * ncm + 8, 2), 1.0), fill(w("VB", 17, 256 * ncm + 8, 2), 0.0)
+    LO, HI = S[0:64], S[64:128]
+    fill(v("NON"), -1.0), fill(v("PM", None, LO), -1.0), fill(v("PM", None, HI), 1.0), fill(v("BT", S[0:256], LO), BIG / 128), fill(v("BT", S[0:256], HI), 12 * BIG / 64), fill(v("BT", S[256:272]), 0.0)
     ts("PR16", v("PR16"), v("PI"), 15, OP.bitwise_and)
     copy("R16", R16, v("PR16"))
     ts("R32", v("R32"), R16, 32.0, OP.mult)
     ts("C37", v("C37"), R16, 1184.0, OP.mult, -393216.0, OP.add)
-    ts("SPR", v("SPR"), R16, 1024.0, OP.add)
-    ts("KV", v("KV"), v("KV"), v("R32"), OP.add)
-    fill(v("KV", S[0:144:18]), 0.0)
-    ts("KV", v("KV", S[17:144:18]), v("KV", S[17:144:18]), 1.0, OP.add)
-    ts("RS", v("RS"), v("I16"), R16, OP.is_equal, TOP, OP.mult)
-    copy("CL", v("CL"), v("CI"))
-    unit = BIG / 128
-    for j in range(2):
-        for h in range(2):
-            x = 4 * j + 2 * h
-            for who, c, k in [(w, S[2 * b:2 * b + 2], S[2:18]) for b, w in enumerate(par["kind"][j, h])] + [(par["one"][j, h], S[:], S[1:2])]:
-                fill(v("BR", (x, c, k)), -unit / 2 if who == "V" else -unit), fill(v("BR", (x + 1, c, k)), -12 * unit if who == "V" else -8 * unit)
-            fill(v("BR", S[x, :, 0:1]), 0.0), fill(v("BR", S[x + 1, :, 0:1]), 32 * unit)
+    for c0, nc in chunks:
+        ts("KV", w("KV", 18 * c0, 18 * nc), w("KI", 0, 18 * nc), v("R32"), OP.add)
+        fill(w("KV", 18 * c0, nc, 18), 0.0), fill(w("KV", 18 * c0 + 17, nc, 18), 512.0 * nc + 17)
+    ts("SP", v("SP"), w("I17", 0, 16), 16.0, OP.mult, R16, OP.add)
+    ts("SP", v("SP"), v("SP"), 1024.0, OP.add)
+    ts("DI", v("DI", S[::-1]), v("I17"), R16, OP.is_equal, 0.25, OP.mult)
+    tt("DJ", w("DJ", 0, 16), w("DI", 0, 16), w("DI", 1, 16), OP.subtract)
+    copy("DJ", w("DJ", 16, 1), w("DI", 16, 1))
+    seg, runs, pos = {}, {}, 0
+    for h, (c0, nc) in enumerate(chunks):
+        gr, at = par["group"][h], {}
+        for g0 in range(0, nc, gr):
+            for i in range(gr):
+                c = g0 + (i // 2 if i % 2 == 0 else gr - 1 - i // 2)
+                at[c], pos = pos, pos + 16 * (c - g0 + 1) + 2
+        seg[h] = [(at[c], 16 * (c % gr + 1)) for c in range(nc)]
+        hf = (gr + 1) // 2
+        runs[h] = [range(i, nc, gr) for i in range(gr)] if gr <= 2 else [range(c, c + hf) for c in range(0, nc, hf)]
+        fill(w("RS", min(at.values()), pos - min(at.values())), 0.0)
+        for c in range(nc):
+            copy("RS", w("RS", at[c], 17), v("DJ")), fill(w("NE", at[c], 1), 0.0), copy("RS", w("RS", at[c] + seg[h][c][1] + 1, 1), w("SP", c % gr, 1))
+            ts("SPT", w("SPT", c0 + c, 1), w("SP", c % gr, 1), 4.0, OP.mult, TOP, OP.add)
+
+    def ends(name, h, run):
+        p = [seg[h][c][0] + seg[h][c][1] + 1 for c in run]
+        d = p[1] - p[0] if len(p) > 1 else 1
+        return v(name, S[p[0]:p[-1] + (1 if d > 0 else -1):d])
+    unit, br = BIG / 64, {}
+    for na in sorted(set(par["scalar"].values())):
+        x = br[na] = len(br)
+        for k, a0, a1 in ((S[0:1], 0.0, 32 * unit), (S[1:1 + na], -unit, -8 * unit), (S[1 + na:18], -unit / 2, -12 * unit)):
+            if k.start < k.stop: fill(v("BR", (x, S[0:ncm], k), LO), a0), fill(v("BR", (x, S[0:ncm], k), HI), a1)
 
     rid, pid, _ = topo.addr(nxt)
     mask, ne = topo.mask(core, nxt), len(topo.engines(core, nxt))
-    sent = {}
+    sent, turn = {}, [0]
 
-    def send(kind, t, h, src, ix):
-        o, i = T["%s%d" % ({"z": "ZI", "m": "MU"}[kind], t)][:, ix], v(src, ix)
-        sent[kind, t, h] = op("send", "G", lambda q, e: q.remote_dma(o, i["ap"], T.sem["%si%d%d" % (kind, t, h)], T.sem["%sl%d%d" % (kind, t, h)], pid, rid, mask),
-                              [i], [], {"G": 0.5}, ("%sl%d%d" % (kind, t, h), ne, 1.5))
+    def send(kind, t, h, src, a, n):
+        o, i = T["%s%d" % ({"z": "ZI", "m": "MU"}[kind], t)][:, a:a + n], w(src, a, n)
+        sent[kind, t, h] = op("s%s%d" % (kind, h), "G", lambda q, e: q.remote_dma(o, i["ap"], T.sem["%si%d%d" % (kind, t, h)], T.sem["%sl%d%d" % (kind, t, h)], pid, rid, mask),
+                              [i], [], ("fix", 0.5), ("%sl%d%d" % (kind, t, h), ne, 1.5))
 
-    def compare(nm, who, out, kk, zt, b):
-        cell, e_ = {}, v("E", S[512 * b:512 * b + 512])
+    def head(t, h):
+        (c0, nc), s = chunks[h], str(h)
+        a, n, b = 16 * c0, 16 * nc, 32 * (16 * c0 + 2 - h)
+        mu, z0, xs = w("MU%d" % t, c0, nc), w("ZI%d" % t, a, n), w("P%d" % (3 + h % 2), 288, n)
+        m = n // par["pieces"]
+        for c in range(par["pieces"]): lin("p%d%d" % (h, c), w("PB", b + 15 + 32 * m * c, 16 * m, 2), ind(v("PR"), w("OU", a + m * c, m)))
+        for c in range(par["pieces"]): lin("a%d%d" % (h, c), w("AB", b + 16 + 32 * m * c, 16 * m, 2), ind(v("AD"), w("OU", a + m * c, m)), -1.0)
+        lin("P0" + s, w("PB", b + 16, n, 32), w("PB", b + 15, n, 32))
+        lin("G" + s, w("PB", b + 47, n, 32), ind(v("GL"), mu))
+        back = S[b + 15 + 32 * n:b + 15:-1]
+        scan("K" + s, v("KB", S[32 * (a + n) - 1:(32 * a - 1 if a else None):-1]), v("AB", back), v("PB", back), OP.add, OP.max)
+        if par["scalar"][h, 0] < 17: mm("zp" + s, [(w("P2", a, n), IDN, z0)])
+        lin("Y" + s, w("Y", a, n), z0, 1.0, -255.0)
+        lin("Mb" + s, w("M37", 33 * c0 + n, n), ind(v("IOTA"), mu), 148.0, TOP)
+        ts("Ml" + s, w("M37", 33 * c0 + 2 * n, nc), mu, 148.0, OP.mult, TOP, OP.add)
+        ts("M4" + s, w("M4", c0, nc), mu, 4.0, OP.mult, TOP, OP.add)
+        mm("e0" + s, [(xs, IDN, w("KB", 32 * a + 1, n, 32)), (xs, IDN, w("AB", b + 16, n, 32))])
+        act("R0" + s, w("R0", a, n), xs, AF.Relu)
+        us, w0, og = w("P5", 0, n), w("P5", 0, n), w("P5", 256 + a, n)
+        for k4 in range(3, -1, -1):
+            lst = []
+            for k in range(4 * k4, 4 * k4 + 4):
+                lst += [(us, v("RMC", S[k]), w("KB", 32 * a + 2 * k + 1, n, 32)), (us, v("RMN", S[k]), w("KB", 32 * a + 2 * k, n, 32) if k else w("R0", a, n))]
+            mm("us" + s, lst, k4 == 3, k4 == 0)
+        ts("W0" + s, w0, us, 253.5 * BIG, OP.is_lt, v("C37"), OP.mult)
+        tt("OG" + s, og, w("NO", a, n), w0, OP.max)
+        tt("W" + s, w("W", a, n), w("O32", a, n), w0, OP.add)
 
-        def fm(q, e):
-            P = T[cell["bank"]][:]
-            if who == "V": return q.matmul(P, zt["ap"], e_["ap"], True, True)
-            q.matmul(P, NID["ap"], kk["ap"], True, False)
-            return q.matmul(P, zt["ap"], e_["ap"], False, True)
-        m = op(nm + "m", "T", fm, [zt, e_] + ([NID, kk] if who == "A" else []), [], mmcost([512] * (1 if who == "V" else 2)), dyn=("take", cell))
-        cost = {"V": par["ovV"] + 512 * cyc, "A": par["ovA"] + 512 * cyc}
-        if who == "V": op(nm, "V", lambda q, e: q.tensor_tensor(out["ap"], kk["ap"], T[cell["bank"]][:], OP.is_le), [kk], [out], cost, after=[m], dyn=("give", cell))
-        else: op(nm, "A", lambda q, e: q.activation(out["ap"], T[cell["bank"]][:], AF.Sign, bias=0.5), [], [out], cost, after=[m], dyn=("give", cell))
+    def one_pass(t, h, j):
+        (c0, nc), s, js = chunks[h], str(h), "%d%d" % (h, j)
+        a, n, b, XB = 16 * c0, 16 * nc, 32 * (16 * c0 + 2 - h), "P%d" % (3 + h % 2)
+        z, y, z1, vg, dg, xs = w("Z1" if j else "ZI%d" % t, a, n), w("Y", a, n), w("Z1", a, n), w("VG", a, n), w("DG", a, n), w(XB, 288, n)
+        ks, ku, na = w("KS", 18 * c0 + 17, nc, 18), w("KU", c0, nc), par["scalar"][h, j]
+        cs = nc // par["split"][h]
+        for c1 in range(0, nc, cs):
+            m, a1 = 16 * cs, a + 16 * c1
+            def kk(k): return w("KB", 32 * a1 + (2 * k - 1 if k else 0), m, 32)
+            per = 512 // m
+            for k0 in range(0, na, per):
+                bank = "P%d" % (turn[0] % 2)
+                turn[0] += 1
+                ks_ = range(k0, min(na, k0 + per))
+                mm("d" + js, [x for k in ks_ for x in ((w(bank, m * (k - k0), m), NID, kk(k)), (w(bank, m * (k - k0), m), IDN, w(z["el"][0][0], a1, m)))], size=2)
+                for k in ks_: act("c" + js, v("C", S[a1:a1 + m, k + 1]), w(bank, m * (k - k0), m), AF.Sign, 1.0, 0.5)
+            for k in range(16 - j, na - 1, -1): tt("c" + js, v("C", S[a1:a1 + m, k + 1]), kk(k), w("P2", a1, m), OP.is_le)
+            o = w(XB, 18 * c1, 18 * cs)
+            mm("n" + js, [(o, v("PM"), v("BR", S[br[na], 0:cs]))] + [(o, v("RMC", S[r]), v("C", S[a1 + r:a1 + m:16])) for r in range(16)])
+        scan("KS" + js, w("KS", 18 * c0, 18 * nc), w(XB, 0, 18 * nc), w("KV", 0, 18 * nc), OP.max, OP.min)
+        copy("KU" + js, ku, ks)
+        tt("VG" + js, vg, ind(w("AB", b, 32 * n + 32), ku), y, OP.max)
+        lin("DG" + js, dg, ind(w("VB", 0, 32 * n + 32), ku), w("DVF", 2 * t + j, 1), 0.0, "A")
+        mm("x" + js, [(xs, IDN, z), (xs, NID, vg), (xs, NID, dg)])
+        ml = w("UI", 33 * c0 + 2 * n, nc)
+        if j:
+            act("Z" + s, w("Z" if t < 3 else "ZF", a, n), xs, AF.Abs)
+            act("NN" + s, w("NN", c0, nc), ks, AF.Sign)
+            ts("GO" + s, w("GO", c0, nc), ks, 512.0 * nc + 17, OP.is_equal)
+            tt("VF" + s, w("VF", c0, nc), w("NN", c0, nc), w("GO", c0, nc), OP.subtract)
+            tt("TQ" + s, w("TQ", c0, nc), w("VF", c0, nc), w("D0", c0, nc), OP.mult)
+            tt("MN" + s, w("MN", c0, nc), w("TQ", c0, nc), ml, OP.add)
+            ts("MS" + s, w("MS" if t < 3 else "YM", c0, nc), w("MN", c0, nc), -TOP, OP.add, 0.25, OP.mult)
+            if t < 3: send("m", t + 1, h, "MS", c0, nc), send("z", t + 1, h, "Z", a, n)
+            return
+        act("Z1" + s, z1, xs, AF.Abs)
+        if par["scalar"][h, 1] < 16: act("ZP" + s, w("P2", a, n), xs, AF.Abs)
+        lin("Y1" + s, y, z1, 1.0, -255.0)
+        mm("ub" + s, [(w("P6", 0, n), v("BW"), z1), (w("P6", n, n), v("BW4"), z1)], size=1)
+        mm("xl" + s, [(w("P6", 2 * n, nc), v("RMW", S[r]), w("Z1", a + r, nc, 16)) for r in range(16)])
+        tt("cg" + s, v("C", S[a:a + n, 17]), w("KB", 32 * a + 31, n, 32), w("P2", a, n) if s in par["zp"] else z1, OP.is_le)
+        tc = w("P7", 0, n + nc)
+        mm("gn" + s, [(tc, v("PM"), w("BT", 256 - n, n + nc)), (w("P7", 0, n), v("BN"), v("C", S[a:a + n, 17]))])
+        tt("MI" + s, w("MI", 33 * c0, 33 * nc), w("P6", 0, 33 * nc), w("M37", 33 * c0, 33 * nc), OP.add)
+        ts("UI" + s, w("UI", 33 * c0, 33 * nc), w("MI", 33 * c0, 33 * nc), int(TOP) + 4095, OP.bitwise_and)
+        tt("X" + s, w("X", 17 * c0, 17 * nc), w("UI", 33 * c0 + n, 17 * nc), tc, OP.max)
+        og, gr = w("P5", 256 + a, n), par["group"][h]
+        sb, xw = min(seg[h])[0], 2 if gr == 1 else 1
+        sl = max(seg[h])[0] + max(seg[h])[1] + 2 - sb
+        for run in runs[h]: tt("NF" + s, ends("NE", h, run), w("UI", 33 * c0 + 2 * n + run[0], len(run), run.step), w("SPT", c0 + run[0], len(run), run.step), OP.subtract)
+        for c in range(nc - 1, -1, -1):
+            hi = 17 * c0 + 16 * c + 15
+            lo = hi - seg[h][c][1]
+            ts("NE" + s, w("NE", seg[h][c][0] + 1, hi - lo), v("X", S[hi:(lo if lo >= 0 else None):-1]), w("X", 17 * c0 + n + c, 1), OP.not_equal)
+        scan("SC" + s, w("SC", sb, sl), w("NE", sb, sl), w("RS", sb, sl), OP.mult, OP.add)
+        for run in runs[h]: copy("XF" + s, w("XF", 2 * c0 + xw * run[0], len(run), xw * run.step), ends("SC", h, run))
+        tt("PP" + s, og, w("UI", 33 * c0, n), og, OP.mult)
+        tt("XP" + s, w("XP", a, n), w("W", a, n), og, OP.subtract)
+        ts("NW" + s, w("NW", a, n), w("XP", a, n), 5, OP.arith_shift_right, 4095, OP.bitwise_and)
+        for c in range(nc - gr, -1, -gr): copy("put" + s, ind(w("MC", 0, 1024 + 16 * ncm), w("XF", 2 * c0 + xw * c, gr)), w("NW", a + 16 * c, 16 * gr))
+        tt("D0" + s, w("D0", c0, nc), w("M4", c0, nc), ml, OP.subtract)
 
     for t in range(4):
-        ZI, MU, step[0] = "ZI%d" % t, "MU%d" % t, t
-        for h in (1, 0):
-            a, s = 128 * h, str(h)
-            mu = v(MU, S[8 * h:8 * h + 8])
+        step[0] = t
+        for h, (c0, nc) in enumerate(chunks):
+            a, n, s, mu = 16 * c0, 16 * nc, str(h), w("MU%d" % t, c0, nc)
             if t:
-                op("m in", "", None, [], [mu], {}, ("mi%d%d" % (t, h), ne, par["far"]), [sent["m", t, h]])
-                op("z in", "", None, [], [v(ZI, S[a:a + 128])], {}, ("zi%d%d" % (t, h), ne, par["far"]), [sent["z", t, h]])
-            copy("OU" + s, v("OU", S[a:a + 128]), ind(v("MC", S[0:1024]) if t else v("MCI"), mu))
-            ts("NO" + s, v("NO", S[a:a + 128]), v("OU", S[a:a + 128]), -1.0, OP.mult)
-            lin("O32" + s, v("O32", S[a:a + 128]), v("NO", S[a:a + 128]), -32.0)
-        for h in (1, 0):
-            a, s = 128 * h, str(h)
-            AB, PB, KB, C, XB = "AB" + s, "PB" + s, "KB" + s, "C" + s, "P%d" % (3 + h)
-            mu, z0 = v(MU, S[8 * h:8 * h + 8]), v(ZI, S[a:a + 128])
-            xs, xt, cp = v(XB, S[144:272]), v("P7", S[256 + a:384 + a]), v(XB, S[0:144])
-            zt, y, z1, vg, dg, ks = v("ZT" + s), v("Y" + s), v("Z1" + s), v("VG" + s), v("DG" + s), v("KS" + s, S[17:144:18])
-            n = 128 // par["pieces"]
-            for c in range(par["pieces"]):
-                lin("p%d%d" % (h, c), v(PB, S[15 + 32 * n * c:15 + 32 * n * (c + 1):2]), ind(v("PR"), v("OU", S[a + n * c:a + n * (c + 1)])))
-            for c in range(par["pieces"]):
-                lin("a%d%d" % (h, c), v(AB, S[16 + 32 * n * c:16 + 32 * n * (c + 1):2]), ind(v("AD"), v("OU", S[a + n * c:a + n * (c + 1)])), -1.0)
-            lin("P0" + s, v(PB, S[16:4112:32]), v(PB, S[15:4111:32]))
-            lin("G" + s, v(PB, S[47:4112:32]), ind(v("GL"), mu))
-            scan("K" + s, v(KB, S[::-1]), v(AB, S[4111:15:-1]), v(PB, S[4111:15:-1]), OP.add, OP.max)
-            mm("zt" + s, [(xt, z0, IDN)])
-            lin("ZT" + s, zt, xt)
-            lin("Y" + s, y, z0, 1.0, -255.0)
-            lin("Mb" + s, v("M37" + s, S[128:256]), ind(v("IOTA"), mu), 148.0, TOP)
-            ts("Ml" + s, v("M37" + s, S[256:264]), mu, 148.0, OP.mult, TOP, OP.add)
-            ts("M4" + s, v("M4", S[8 * h:8 * h + 8]), mu, 4.0, OP.mult, TOP, OP.add)
-            mm("e0" + s, [(xs, IDN, v(KB, S[1:4096:32])), (xs, IDN, v(AB, S[16:4112:32]))])
-            act("R0" + s, v("R0" + s), xs, AF.Relu)
-            us, w0, og = v("P5", S[0:128]), v("P5", S[128:256]), v("P5", S[256 + a:384 + a])
-            for k4 in range(3, -1, -1):
-                lst = []
-                for k in range(4 * k4, 4 * k4 + 4):
-                    lst += [(us, v("RMC", S[k]), v(KB, S[2 * k + 1:4096:32])), (us, v("RMN", S[k]), v(KB, S[2 * k:4096:32]) if k else v("R0" + s))]
-                mm("us" + s, lst, k4 == 3, k4 == 0)
-            ts("W0" + s, w0, us, 253.5 * BIG, OP.is_lt, v("C37"), OP.mult)
-            tt("OG" + s, og, v("NO", S[a:a + 128]), w0, OP.max)
-            tt("W" + s, v("W" + s), v("O32", S[a:a + 128]), w0, OP.add)
-            z = z0
-            for j in range(2):
-                js = "%d%d" % (h, j)
-                if par["one"][j, h] == "V": tt("c0" + js, v(C, S[:, 1]), v(KB, S[0:4096:32]), z, OP.is_le)
-                else:
-                    mm("d0" + js, [(xs, IDN, z), (xs, NID, v(KB, S[0:4096:32]))])
-                    act("c0" + js, v(C, S[:, 1]), xs, AF.Sign, 1.0, 0.5)
-                for b in range(4):
-                    compare("c" + js, par["kind"][j, h][b], v(C, S[32 * b:32 * b + 32, 2:18]), v(KB, S[1024 * b + 1:1024 * b + 1024:2]), zt, b)
-                    if b % 2:
-                        c4 = 2 * b - 2
-                        o = v(XB, S[18 * c4:18 * c4 + 72])
-                        x = 4 * j + 2 * h
-                        mm("n" + js, [(o, v("PM"), v("BR", S[x, c4:c4 + 4])), (o, ON, v("BR", S[x + 1, c4:c4 + 4]))]
-                           + [(o, v("RMC", S[r]), v(C, S[16 * c4 + r:16 * c4 + 64:16])) for r in range(16)])
-                scan("KS" + js, v("KS" + s), cp, v("KV"), OP.max, OP.min)
-                copy("KU" + js, v("KU" + s), ks)
-                tt("VG" + js, vg, ind(v(AB), v("KU" + s)), y, OP.max)
-                lin("DG" + js, dg, ind(v("VB"), v("KU" + s)), v("DVF", S[2 * t + j:2 * t + j + 1]), 0.0, "A")
-                mm("x" + js, [(xs, IDN, z), (xs, NID, vg), (xs, NID, dg)])
-                if j == 0:
-                    mm("xt" + s, [(xt, z, IDN), (xt, vg, NID), (xt, dg, NID)])
-                    act("Z1" + s, z1, xs, AF.Abs)
-                    act("ZT1" + s, zt, xt, AF.Abs)
-                    lin("Y1" + s, y, z1, 1.0, -255.0)
-                    z = z1
-                    tb, tc = v("P6", S[0:264]), v("P7", S[0:136])
-                    mm("ub" + s, [(v("P6", S[0:128]), v("BW"), z1)])
-                    mm("xb" + s, [(v("P6", S[128:256]), v("BW4"), z1)])
-                    mm("xl" + s, [(v("P6", S[256:264]), v("RMW", S[r]), v("Z1" + s, S[r:128:16])) for r in range(16)])
-                    tt("cg" + s, v(C, S[:, 0]), v(KB, S[31:4096:32]), z1, OP.is_le)
-                    gb, gl = v("P7", S[0:128]), v("P7", S[128:136])
-                    mm("gn" + s, [(tc, v("PM"), v("BN0")), (tc, ON, v("BN1")), (gb, v("BN"), v(C, S[:, 0]))]
-                       + [(gl, v("RMN", S[r]), v(C, S[r:128:16, 0])) for r in range(16)])
-                    tt("MI" + s, v("MI" + s), tb, v("M37" + s), OP.add)
-                    ts("UI" + s, v("UI" + s), v("MI" + s), int(TOP) + 4095, OP.bitwise_and)
-                    tt("X" + s, v("X" + s), v("UI" + s, S[128:264]), tc, OP.max)
-                    xl, ml = v("X" + s, S[128:136]), v("UI" + s, S[256:264])
-                    tt("NE" + s, v("NE" + s), ind(xl, v("CL")), v("X" + s, S[0:128]), OP.not_equal)
-                    scan("SC" + s, v("SC" + s, S[::-1]), v("NE" + s, S[::-1]), v("RS", S[::-1]), OP.mult, OP.max)
-                    tt("T2" + s, v("T2" + s), xl, v("SC" + s, S[0:128:16]), OP.subtract)
-                    ts("XF" + s, v("XF" + s, S[0:16:2]), v("T2" + s), 0.25, OP.mult, v("SPR"), OP.min)
-                    tt("PP" + s, og, v("UI" + s, S[0:128]), og, OP.mult)
-                    tt("XP" + s, v("XP" + s), v("W" + s), og, OP.subtract)
-                    ts("NW" + s, v("NW" + s), v("XP" + s), 5, OP.arith_shift_right, 4095, OP.bitwise_and)
-                    for c in range(7, -1, -1):
-                        copy("put" + s, ind(v("MC"), v("XF" + s, S[2 * c:2 * c + 1])), v("NW" + s, S[16 * c:16 * c + 16]))
-                    ng = v("NG", S[8 * h:8 * h + 8])
-                    ts("NG" + s, ng, xl, TOP + 8192.0, OP.is_ge)
-                    tt("D0" + s, v("D0" + s), v("M4", S[8 * h:8 * h + 8]), ml, OP.subtract)
-                    tt("DM" + s, v("DM" + s), v("D0" + s), ng, OP.mult)
-                else:
-                    act("Z" + s, v("Z" if t < 3 else "ZF", S[a:a + 128]), xs, AF.Abs)
-                    act("NN" + s, v("NN" + s), ks, AF.Sign)
-                    tt("TQ" + s, v("TQ" + s), v("NN" + s), v("DM" + s), OP.mult)
-                    tt("MN" + s, v("MN" + s), v("TQ" + s), v("UI" + s, S[256:264]), OP.add)
-                    ts("MS" + s, v("MS" if t < 3 else "YM", S[8 * h:8 * h + 8]), v("MN" + s), -TOP, OP.add, 0.25, OP.mult)
-                    if t < 3:
-                        send("m", t + 1, h, "MS", S[8 * h:8 * h + 8])
-                        send("z", t + 1, h, "Z", S[a:a + 128])
+                op("m in", "", None, [], [mu], ("fix", 0.0), ("mi%d%d" % (t, h), ne, par["far"]), [sent["m", t, h]])
+                op("z in", "", None, [], [w("ZI%d" % t, a, n)], ("fix", 0.0), ("zi%d%d" % (t, h), ne, par["far"]), [sent["z", t, h]])
+            copy("OU" + s, w("OU", a, n), ind(w("MC", 0, 1024) if t else v("MCI"), mu))
+            if s in par["no"]: lin("NO" + s, w("NO", a, n), ind(w("MC", 0, 1024), mu), -1.0, 0.0, "A")
+            else: ts("NO" + s, w("NO", a, n), w("OU", a, n), -1.0, OP.mult)
+            lin("O32" + s, w("O32", a, n), w("NO", a, n), -32.0)
+        for h, j in par["passes"]:
+            if j == 0: head(t, h)
+            one_pass(t, h, j)
         if t < 3:
-            pa = v("P6", S[300:316])
-            mm("A", [(pa, ON, v("NG"))])
+            pa = w("P6", 496, 16)
+            mm("A", [(pa, ON, v("GO"))])
             act("AC", v("JK"), pa, AF.Identity, -0.5, 1.0 / 64, v("AC"))
             ts("RY", v("RY"), v("AC"), MAGIC, OP.add, MAGIC, OP.subtract)
-            act("PM", v("PM"), v("NON"), AF.Sign, v("AC"), v("RY"))
-    dma("S", T.ymc[:], T.MC[:, 0:1024], [v("MC")], [], "so2", 3.5)
+            act("PM", v("PM", None, LO), v("NON", None, LO), AF.Sign, v("AC", None, LO), v("RY", None, LO))
+    dma("S", T.ymc[:], T.MC[:, 0:1024], [v("MC", S[0:1024 + 16 * ncm])], [], "so2", 3.5)
     dma("S", T.yz[:], T.ZF[:], [v("ZF")], [], "so0", 2.5)
     dma("S", T.ym[:], T.YM[:], [v("YM")], [], "so1", 2.0)
     return ops
 
 
-def schedule(ops, par):
-    n = len(ops)
-    kids, need = [[] for _ in ops], [0] * n
-    for i, o in enumerate(ops):
-        for d in o["raw"] | o["war"]:
-            kids[d].append(i)
-            need[i] += 1
-    lat = [o["done"][2] if o["done"] else min(o["cost"][e] for e in o["eng"]) for o in ops]
-    due = [0.0] * n
-    for i in range(n - 1, -1, -1):
-        o = ops[i]
-        due[i] = par["period"] * o["step"] + par["tau"].get(o["name"], 0.0) if o["step"] >= 0 else min([due[k] for k in kids[i]] + [99.0]) - lat[i] - par["wake"]
-    prio = [-x for x in due]
-    free, start, fin = dict.fromkeys("VATGS", 0.0), [0.0] * n, [0.0] * n
-    user = {"P%d" % b: {} for b in range(8)}
-    idle = ["P%d" % b for b in par["dbanks"]]
-    ready, order = [i for i in range(n) if need[i] == 0], []
+def first(lst, t):
+    lo, hi = 0, len(lst)
+    while lo < hi:
+        mid = (lo + hi) // 2
+        if lst[mid][1] > t: hi = mid
+        else: lo = mid + 1
+    return lo
 
-    def plan(i, e):
-        o = ops[i]
-        hard = set(o["raw"]) | {d for d in o["war"] if ops[d]["eng"] != "T" or e != "T"}
-        banks = set(o["banks"])
-        if o["dyn"]: banks.add(idle[0] if o["dyn"][0] == "take" else o["dyn"][1]["bank"])
-        hard |= {d for b in banks for x, d in user[b].items() if x != e}
-        b = max([fin[d] + (par["own"] if ops[d]["eng"] == e else par["wake"]) for d in hard] + [free[e] if e else 0.0])
-        return b, e, hard, banks
 
+def place(ops, par, links, prio):
+    n, wake = len(ops), par["wake"]
+    kids, need = [[] for _ in ops], [len(x) for x in links]
+    for i in range(n):
+        for d, _ in links[i]: kids[d].append(i)
+    busy = {k: [] for k in list("VATGS") + ["P%d" % b for b in range(8)]}
+    start, dur, eng = [0.0] * n, [0.0] * n, [""] * n
+    ready = [i for i in range(n) if need[i] == 0]
     while ready:
-        cand = []
-        for i in ready:
-            o = ops[i]
-            if o["dyn"] and o["dyn"][0] == "take" and not idle: continue
-            cand.append((i, min((plan(i, e) for e in (o["eng"] or [""])), key=lambda p: p[0] + o["cost"].get(p[1], 0.0))))
-        m = min(c[1][0] for c in cand) + par["eps"]
-        i, (b, e, hard, banks) = max((c for c in cand if c[1][0] <= m), key=lambda c: prio[c[0]])
-        o = ops[i]
+        i = max(ready, key=lambda x: (prio[x], -x))
         ready.remove(i)
-        o["eng"], o["hard"] = e, hard
-        if o["dyn"]:
-            if o["dyn"][0] == "take": o["dyn"][1]["bank"] = idle.pop(0)
-            else: idle.append(o["dyn"][1]["bank"])
-        for x in banks: user[x][e] = i
-        if e: free[e] = b + o["cost"][e]
-        start[i], fin[i] = b, b + (o["done"][2] if o["done"] else o["cost"][e])
-        order.append(i)
+        o = ops[i]
+        est, best = max([start[d] + dur[d] + gap for d, gap in links[i]] + [0.0]), None
+        for e in par["pin"].get(o["name"], o["eng"]) if len(o["eng"]) > 1 else o["eng"] or [""]:
+            c, t0, moved = cost(o["work"], e, par), est, True
+            while moved and e:
+                moved = False
+                for k in [e] + o["banks"]:
+                    lst = busy[k]
+                    for x in range(first(lst, t0 - wake), len(lst)):
+                        a, b, who = lst[x]
+                        gap = wake if who != e else 0.0
+                        if a >= t0 + c + wake: break
+                        if a < t0 + c + gap and t0 < b + gap: t0, moved = b + gap, True
+            key = t0 + c + (par["bias"] if e == "V" else 0.0)
+            if best is None or key < best[0]: best = (key, e, t0, c)
+        _, e, t0, c = best
+        start[i], dur[i], eng[i] = t0, c, e
+        for k in ([e] if e else []) + o["banks"]: busy[k].insert(first(busy[k], t0), (t0, t0 + c, e))
         for k in kids[i]:
             need[k] -= 1
             if need[k] == 0: ready.append(k)
-    return order, start, fin
+    return start, dur, eng
+
+
+def schedule(ops, par):
+    n, wake = len(ops), par["wake"]
+    late = [o["done"][2] - o["work"][1] if o["done"] else 0.0 for o in ops]
+    links = [[(d, late[d] + wake if ops[d]["eng"] and o["eng"] else late[d] * bool(o["eng"]) + wake) for d in o["hard"]] + [(d, 0.0) for d in o["soft"]] for o in ops]
+    due = [par["period"] * o["step"] + par["due"].get(o["name"], 0.0) + 1e-6 * i if o["step"] >= 0 else 999.0 for i, o in enumerate(ops)]
+    for i in range(n - 1, -1, -1):
+        for d, gap in links[i]:
+            if ops[d]["step"] < 0: due[d] = min(due[d], due[i] - gap - cost(ops[d]["work"], ops[d]["eng"][0], par))
+    start, dur, eng = place(ops, par, links, [-x for x in due])
+    order = sorted(range(n), key=lambda i: (start[i], i))
+    user, waits = {}, [set(o["hard"]) for o in ops]
+    for i in order:
+        for k in ops[i]["banks"]:
+            waits[i] |= {d for x, d in user.setdefault(k, {}).items() if x != eng[i]}
+            user[k][eng[i]] = i
+    return order, eng, waits, start, dur
+
+
+PLAN = {}
 
 
 def rank_program(g, core, T, topo):
@@ -376,21 +406,21 @@ def rank_program(g, core, T, topo):
     if rank is None:
         return
     ops = build(T, topo, core, T.cores[(rank + 1) % len(T.cores)], PAR)
-    order, _, _ = schedule(ops, PAR)
+    if not PLAN: PLAN["all"] = schedule(ops, PAR)
+    order, eng, waits, _, _ = PLAN["all"]
     Q = {"V": g.vector, "A": g.scalar, "T": g.tensor, "G": g, "S": g.sync}
     cnt = {e: 0 for e in Q}
     done, know = {}, {}
     known = {e: {} for e in Q}
     for i in order:
-        o = ops[i]
-        e = o["eng"]
+        o, e = ops[i], eng[i]
         if not e:
             done[i] = o["done"][:2]
             know[i] = {done[i][0]: done[i][1]}
             continue
         kn = known[e]
         wants = {}
-        for d in o["hard"]:
+        for d in waits[i]:
             s, c = done[d]
             if kn.get(s, 0) < c and wants.get(s, (0, 0))[0] < c: wants[s] = (c, d)
         for s in sorted(wants, key=lambda s: -wants[s][1]):
@@ -402,7 +432,7 @@ def rank_program(g, core, T, topo):
         x = o["fn"](Q[e], e)
         if o["done"]:
             done[i] = o["done"][:2]
-            if x is not None and o["name"] == "dma": x.then_inc(T.sem[done[i][0]], done[i][1])
+            if o["name"] == "dma": x.then_inc(T.sem[done[i][0]], done[i][1])
         else:
             cnt[e] += 1
             done[i] = ("s" + e, cnt[e])

@@ -7,14 +7,14 @@ SB = {"MCI": (1024, I), "MC": (1280, F), "PR": (4096, H), "AD": (4096, H), "GL":
       "DVF": (8, F), "WS": (1, F), "W4": (1, F), "OU": (256, U), "NO": (256, F), "O32": (256, F), "Z": (256, H), "ZF": (256, F), "MS": (16, U), "YM": (16, F),
       "KV": (288, F), "IOTA": (1024, F), "VB": (8224, H), "ON": (2048, H), "NON": (128, H), "IDN": (128, H), "NID": (128, H), "BLK": (128, H), "BLB": (128, H),
       "BW": (128, H), "BW4": (128, H), "BN": (128, H), "CMB": (256, H), "PM": (128, H), "MSK": (8, F), "PI": (1, I), "PR16": (1, I), "R16": (1, F), "R32": (1, F),
-      "C37": (1, F), "I17": (17, F), "DI": (17, F), "DJ": (17, F), "SP": (16, F), "SPT": (16, F), "BT": (272, H), "KI": (288, F), "GO": (16, H), "JK": (16, F), "AC": (1, F), "RY": (1, F),
+      "C37": (1, F), "B8": (16, H), "FT": (128, H), "SP": (16, F), "SPT": (16, F), "BT": (272, H), "KI": (288, F), "GO": (16, H), "JK": (16, F), "AC": (1, F), "RY": (1, F),
       "AB": (8320, H), "PB": (8320, H), "KB": (8192, H), "KS": (288, F), "KU": (16, U), "VG": (256, H), "DG": (256, H), "R0": (256, H), "Y": (256, H), "Z1": (256, H),
       "M37": (528, F), "MI": (528, I), "UI": (528, I), "X": (272, F), "NE": (2200, F), "SC": (2200, F), "RS": (2200, F), "XF": (32, U), "W": (256, F), "XP": (256, I), "NW": (256, I)}
 for _n in ("M4", "D0", "VF", "NN", "TQ", "MN"): SB[_n] = (16, F)
 for _t in "0123": SB["ZI" + _t], SB["MU" + _t] = (256, H), (16, U)
 SCRATCH = {k: ("sbuf", [128, w], d) for k, (w, d) in SB.items()}
 SCRATCH["C"] = ("sbuf", [128, 256, 18], H)
-for _n in ("RMC", "RMN", "RMW"): SCRATCH[_n] = ("sbuf", [128, 16, 8, 16], H)
+for _n in ("RMC", "RMW"): SCRATCH[_n] = ("sbuf", [128, 16, 8, 16], H)
 SCRATCH["BR"] = ("sbuf", [128, 12, 16, 18], H)
 for _b in range(8): SCRATCH["P%d" % _b] = ("psum", [128, 512], F)
 SEMAPHORES = ["sV", "sA", "sT", "sG", "so0", "so1", "so2"] + ["ld_" + n for n in ("m0", "mc", "pr", "ad", "gl", "z0", "wt", "dv")]
@@ -34,6 +34,8 @@ PAR = {
 
 DUE = "KU00=-6.6 p10=-3.4 p00=-3.1 p01=-2.6 OU0=-1.7 dma=-1.7 NE0=0.2 K0=0.8 a01=0.9 a00=1.2 G0=1.2 P00=1.3 p11=1.3 OU1=1.5 P01=1.5 a10=1.7 zp0=2.3 a11=2.5 c00=3.4 K1=3.4 VG10=3.4 zp1=3.5 G1=3.6 KS00=3.6 VG00=4.1 c10=4.4 cg1=4.4 x10=4.6 d00=4.9 n10=5 R00=5.1 n00=5.2 x00=5.2 Ml0=5.2 ZP0=5.4 Y0=5.6 M40=5.7 DG00=5.8 OG1=6.1 d10=6.4 us0=6.5 O320=6.5 D00=6.8 Z10=6.9 Z0=7.1 R01=7.6 KU10=7.7 M41=7.7 DG10=7.9 ZP1=7.9 VG01=7.9 e00=8 TQ0=8 PP0=8.1 xl1=8.2 Z11=8.3 W0=8.5 TQ1=8.6 gn0=8.9 ub1=8.9 Mb1=9 W1=9 Mb0=9.1 put1=9.2 NO0=9.2 DG01=9.2 GP1=9.2 SC1=9.2 NF1=9.3 Y1=9.5 O321=9.5 KS10=9.6 NE1=9.6 XF1=9.6 X0=9.9 W00=10.1 DM0=10.2 n11=10.2 cg0=10.3 NF0=10.4 PP1=10.5 KS11=10.5 xl0=10.6 OG0=10.6 ub0=10.8 NW0=10.8 MI0=10.9 X1=11 GP0=11.1 SC0=11.4 us1=11.5 XF0=11.5 UI1=11.5 NG1=11.5 W01=12 UI0=12 put0=12 d01=12 NG0=12.1 Ml1=12.2 c01=12.2 n01=12.3 sz0=12.6 D01=12.6 MI1=12.7 NN0=12.7 KS01=12.8 KU01=12.9 XP1=13 c11=13 GO0=13 VF0=13.1 NW1=13.4 Y11=13.4 e01=13.4 NO1=13.6 XP0=13.7 MS0=13.8 DM1=14 DG11=14.2 gn1=14.2 d11=14.5 MS1=14.8 GO1=15 VF1=15.1 AC=15.6 Y10=15.8 RY=16.3 VG11=16.5 NN1=16.5 sm1=16.8 sm0=17.8 Z1=18.6 MN0=19 MN1=19.3 A=20.3 KU11=20.3 PM=21.7 x11=23.4 x01=25.7 sz1=27"
 PIN = "G0=A G1=V Mb0=A Mb1=A O320=A O321=VA P00=A P01=A RMN=VA RMW=A Y0=A Y1=VA Y10=VA Y11=A a00=A a01=V a10=A a11=A p00=VA p01=A p10=A p11=VA"
+DUE = "K0=-10.8 dma=-7.1 Z1=-6.3 P01=-5.6 O320=-5.6 a01=-5.4 KU00=-5.3 p00=-4.9 gn0=-3.9 Y0=-2.3 X0=-2.2 GO0=-2.2 OU0=-2 DG00=-1.3 O321=-1 ZP0=-0.9 DG10=-0.5 a00=-0.1 G0=-0 NW0=0.2 p01=0.7 OU1=0.7 c00=1.5 KU10=1.6 KS00=1.8 VG00=2.1 P00=2.2 R00=2.2 c10=2.4 MS0=2.4 W00=2.6 p10=3.1 M40=3.1 p11=3.3 R01=3.4 cg1=3.5 a10=4.1 zp0=4.2 ub1=4.2 X1=4.2 Y1=4.3 M41=4.5 W0=4.9 KS10=4.9 us1=5 Ml1=5 a11=5.4 xl0=5.9 Ml0=6.4 VG10=6.6 xl1=6.6 Z11=6.8 Mb1=7 ub0=7.2 G1=7.3 n01=7.5 zp1=7.8 n00=7.8 ZP1=7.8 MN1=8.1 K1=8.5 us0=8.6 D01=8.6 NE0=8.8 sz0=8.8 W1=8.9 n10=9 Z0=9.1 cg0=9.1 PP1=9.1 NF1=9.2 NO0=9.4 SC1=9.4 OG0=9.5 TQ0=9.6 D00=9.8 Mb0=10 VF1=10 KS11=10.1 e00=10.4 n11=10.5 x10=10.6 UI0=10.9 NF0=11 put0=11.2 MI0=11.4 OG1=11.6 Z10=11.6 MI1=11.7 KU01=11.8 x00=12 XF1=12 VF0=12.1 UI1=12.3 NE1=12.4 c01=12.4 SC0=12.5 c11=12.8 XF0=12.9 XP1=13 PP0=13.1 KS01=13.2 NW1=13.2 VG11=13.2 e01=13.4 TQ1=13.5 W01=13.5 NO1=13.6 MS1=13.7 gn1=14 put1=14.4 VG01=14.9 XP0=15 DG11=15.1 RY=15.5 NN1=15.7 Y10=15.8 NN0=16.4 A=17.4 MN0=17.7 DG01=18.1 Y11=18.5 GO1=18.6 sm0=19.3 x11=19.9 KU11=21 sm1=21.5 x01=21.8 AC=22 sz1=24.7 PM=28.2"
+PIN = "G0=VA G1=VA Mb0=VA Mb1=A O320=VA O321=A P00=VA P01=VA RMN=A RMW=VA Y0=VA Y1=VA Y10=VA Y11=A a00=A a01=VA a10=A a11=A p00=A p01=V p10=A p11=A zp0=V zp1=A"
 PAR.update({"due": {k: float(x) for k, x in (y.split("=") for y in DUE.split())}, "pin": dict(y.split("=") for y in PIN.split())})
 PAR.update({"scalar": {(0, 0): 0, (1, 0): 8, (0, 1): 8, (1, 1): 8}, "group": (2, 4), "zp": "01", "far": 1.5})
 
@@ -142,7 +144,7 @@ def build(T, topo, core, nxt, par):
     for q, name, dst, lat in par["loads"]: dma(q, T[dst][:], T[name][:], [], [v(dst)], "ld_" + name, lat)
     imp = {"allow_small_or_imprecise_dtypes": True}
     ON, IDN, NID, R16 = w("ON", 0, 128), v("IDN"), v("NID"), v("R16")
-    fill(w("ON", 0, 256), 1.0)
+    fill(w("ON", 0, 256), 1.0), fill(w("ON", 256, 768), 1.0)
     G(v("PI"), [], lambda q: q.iota(T.PI[:], [[0, 1]], 0, 1))
     G(v("BLB"), [ON], lambda q: q.affine_select(T.BLB[:], ON["ap"], [[-16, 8], [0, 16]], OP.is_ge, 0.0, 0, 1))
     G(v("BLK"), [v("BLB")], lambda q: q.affine_select(T.BLK[:], T.BLB[:], [[16, 8], [0, 16]], OP.is_ge, 0.0, 15, -1))
@@ -150,14 +152,16 @@ def build(T, topo, core, nxt, par):
     G(IDN, [ON], lambda q: q.affine_select(T.IDN[:], ON["ap"], [[-1, 128]], OP.is_equal, 0.0, 0, 1))
     KI = w("KI", 0, 18 * ncm)
     G(KI, [], lambda q: q.iota(KI["ap"], [[512, ncm], [2, 18]], 14, 0, **imp))
-    G(v("I17"), [], lambda q: q.iota(T.I17[:], [[1, 17]], 0, 0, **imp))
     G(v("IOTA"), [], lambda q: q.iota(T.IOTA[:], [[1, 1024]], 0, 0, **imp))
+    VB = w("VB", 0, 512 * ncm + 32)
+    G(VB, [], lambda q: q.iota(VB["ap"], [[0, 256 * ncm + 16], [-1, 2]], 1, 0, **imp))
     copy("MU0", v("MU0"), v("M0"))
     copy("MC", w("MC", 0, 1024), v("MCI"))
     fill(w("MC", 1024, 16 * ncm), 0.0)
     copy("MSK", v("MSK"), w("BLK", 0, 8, 16))
     for x in range(8): ts("RMC", v("RMC", S[:, x, :]), v("CMB"), w("MSK", x, 1), OP.mult, BIG, OP.mult)
-    lin("RMN", v("RMN"), v("RMC"), -1.0)
+    copy("B8", w("B8", 0, 8), w("BLK", 0, 8, 16))
+    ts("B8", w("B8", 8, 8), w("BLK", 0, 8, 16), -1.0, OP.mult)
     ts("WS", v("WS"), v("WT"), 4.0 / BIG, OP.mult)
     ts("W4", v("W4"), v("WT"), 4.0, OP.mult)
     lin("RMW", v("RMW"), v("RMC"), v("WS"))
@@ -168,43 +172,34 @@ def build(T, topo, core, nxt, par):
     copy("DVF", v("DVF"), v("DV"))
     for h, (c0, nc) in enumerate(chunks):
         b, n = 32 * (16 * c0 + 2 - h), 16 * nc
-        fill(w("AB", b, 16), 0.0), fill(w("AB", b + 16 + 32 * n, 16), 0.0), fill(w("AB", b + 17, 16 * n, 2), 0.0), fill(w("AB", b + 47, n, 32), -256.0)
-        fill(w("PB", b + 16, 16 * n, 2), 0.0), fill(w("M37", 33 * c0, n), 0.0)
+        fill(w("AB", b, 16), 0.0), fill(w("AB", b + 16 + 32 * n, 16), 0.0), fill(w("M37", 33 * c0, n), 0.0)
+        for x in range(0, 16 * n, 1024):
+            lin("AB%d" % h, w("AB", b + 17 + 2 * x, min(1024, 16 * n - x), 2), w("ON", 0, min(1024, 16 * n - x)), 0.0)
+            lin("PB%d" % h, w("PB", b + 16 + 2 * x, min(1024, 16 * n - x), 2), w("ON", 0, min(1024, 16 * n - x)), 0.0)
+        fill(w("AB", b + 47, n, 32), -256.0)
     fill(v("C", S[:, 0]), 0.0)
-    fill(w("VB", 0, 16), 0.0), fill(w("VB", 16, 256 * ncm + 8, 2), 1.0), fill(w("VB", 17, 256 * ncm + 8, 2), 0.0)
     LO, HI = S[0:64], S[64:128]
     fill(v("NON"), -1.0), fill(v("PM", None, LO), -1.0), fill(v("PM", None, HI), 1.0), fill(v("BT", S[0:256], LO), BIG / 128), fill(v("BT", S[0:256], HI), 12 * BIG / 64), fill(v("BT", S[256:272]), 0.0)
     ts("PR16", v("PR16"), v("PI"), 15, OP.bitwise_and)
     copy("R16", R16, v("PR16"))
     ts("R32", v("R32"), R16, 32.0, OP.mult)
-    ts("C37", v("C37"), R16, 1184.0, OP.mult, -393216.0, OP.add)
+    ts("C37", v("C37"), R16, 592.0, OP.mult, -196608.0, OP.add)
     for c0, nc in chunks:
         ts("KV", w("KV", 18 * c0, 18 * nc), w("KI", 0, 18 * nc), v("R32"), OP.add)
-        fill(w("KV", 18 * c0, nc, 18), 0.0), fill(w("KV", 18 * c0 + 17, nc, 18), 512.0 * nc + 17)
-    ts("SP", v("SP"), w("I17", 0, 16), 16.0, OP.mult, R16, OP.add)
-    ts("SP", v("SP"), v("SP"), 1024.0, OP.add)
-    ts("DI", v("DI", S[::-1]), v("I17"), R16, OP.is_equal, 0.25, OP.mult)
-    tt("DJ", w("DJ", 0, 16), w("DI", 0, 16), w("DI", 1, 16), OP.subtract)
-    copy("DJ", w("DJ", 16, 1), w("DI", 16, 1))
-    seg, runs, pos = {}, {}, 0
+        fill(w("KV", 18 * c0, nc, 18), 1.0), fill(w("KV", 18 * c0 + 17, nc, 18), 512.0 * nc + 17)
+    seg, pos = {}, 0
     for h, (c0, nc) in enumerate(chunks):
-        gr, at = par["group"][h], {}
-        for g0 in range(0, nc, gr):
-            for i in range(gr):
-                c = g0 + (i // 2 if i % 2 == 0 else gr - 1 - i // 2)
-                at[c], pos = pos, pos + 16 * (c - g0 + 1) + 2
-        seg[h] = [(at[c], 16 * (c % gr + 1)) for c in range(nc)]
-        hf = (gr + 1) // 2
-        runs[h] = [range(i, nc, gr) for i in range(gr)] if gr <= 2 else [range(c, c + hf) for c in range(0, nc, hf)]
-        fill(w("RS", min(at.values()), pos - min(at.values())), 0.0)
-        for c in range(nc):
-            copy("RS", w("RS", at[c], 17), v("DJ")), fill(w("NE", at[c], 1), 0.0), copy("RS", w("RS", at[c] + seg[h][c][1] + 1, 1), w("SP", c % gr, 1))
-            ts("SPT", w("SPT", c0 + c, 1), w("SP", c % gr, 1), 4.0, OP.mult, TOP, OP.add)
-
-    def ends(name, h, run):
-        p = [seg[h][c][0] + seg[h][c][1] + 1 for c in run]
-        d = p[1] - p[0] if len(p) > 1 else 1
-        return v(name, S[p[0]:p[-1] + (1 if d > 0 else -1):d])
+        gr = par["group"][h]
+        ln = 16 * gr + 2
+        seg[h], pos = (pos, ln), pos + nc * ln
+        sb, sc, sp = seg[h][0], w("SC", seg[h][0], nc * ln), w("SP", c0, nc)
+        G(sc, [], lambda q, sc=sc, nc=nc, ln=ln: q.iota(sc["ap"], [[0, nc], [-1, ln]], 16, 0, **imp))
+        G(sp, [], lambda q, sp=sp, nc=nc, gr=gr: q.iota(sp["ap"], [[0, nc // gr], [16, gr]], 1024, 0, **imp))
+        ts("RS", sc, sc, R16, OP.is_equal, 0.25, OP.mult)
+        tt("RS", w("RS", sb, nc * ln - 1), w("SC", sb, nc * ln - 1), w("SC", sb + 1, nc * ln - 1), OP.subtract)
+        ts("RS", w("RS", sb + ln - 1, nc, ln), sp, R16, OP.add)
+        ts("SPT", w("SPT", c0, nc), w("RS", sb + ln - 1, nc, ln), 4.0, OP.mult, TOP, OP.add)
+        fill(w("NE", sb, nc * ln), 1.0), fill(w("NE", sb, nc, ln), 0.0)
     unit, br = BIG / 64, {}
     for na in sorted(set(par["scalar"].values())):
         x = br[na] = len(br)
@@ -238,13 +233,16 @@ def build(T, topo, core, nxt, par):
         ts("M4" + s, w("M4", c0, nc), mu, 4.0, OP.mult, TOP, OP.add)
         mm("e0" + s, [(xs, IDN, w("KB", 32 * a + 1, n, 32)), (xs, IDN, w("AB", b + 16, n, 32))])
         act("R0" + s, w("R0", a, n), xs, AF.Relu)
-        us, w0, og = w("P5", 0, n), w("P5", 0, n), w("P5", 256 + a, n)
-        for k4 in range(3, -1, -1):
+        rows, w0, og = S[0:n], w("P5", 128, n), w("P5", 256 + a, n)
+        for k4 in range(1, -1, -1):
             lst = []
-            for k in range(4 * k4, 4 * k4 + 4):
-                lst += [(us, v("RMC", S[k]), w("KB", 32 * a + 2 * k + 1, n, 32)), (us, v("RMN", S[k]), w("KB", 32 * a + 2 * k, n, 32) if k else w("R0", a, n))]
-            mm("us" + s, lst, k4 == 3, k4 == 0)
-        ts("W0" + s, w0, us, 253.5 * BIG, OP.is_lt, v("C37"), OP.mult)
+            for k in range(8 * k4, 8 * k4 + 8):
+                o = v("P5", S[k:113 + k:16], rows)
+                lst += [(o, w("KB", 32 * a + 2 * k + 1, n, 32), w("B8", 0, 8)), (o, w("KB", 32 * a + 2 * k, n, 32) if k else w("R0", a, n), w("B8", 8, 8))]
+            mm("us" + s, lst, size=2)
+        act("FT" + s, v("FT", None, rows), v("P5", S[0:128], rows), AF.Sign, -1.0, 253.5)
+        mm("ft" + s, [(w0, v("FT", None, rows), v("IDN", S[0:n], rows))])
+        lin("W0" + s, w0, w0, v("C37"), v("C37"))
         tt("OG" + s, og, w("NO", a, n), w0, OP.max)
         tt("W" + s, w("W", a, n), w("O32", a, n), w0, OP.add)
 
@@ -267,7 +265,7 @@ def build(T, topo, core, nxt, par):
             for k in range(16 - j, na - 1, -1): tt("c" + js, v("C", S[a1:a1 + m, k + 1]), kk(k), w("P2", a1, m), OP.is_le)
             o = w(XB, 18 * c1, 18 * cs)
             mm("n" + js, [(o, v("PM"), v("BR", S[br[na], 0:cs]))] + [(o, v("RMC", S[r]), v("C", S[a1 + r:a1 + m:16])) for r in range(16)])
-        scan("KS" + js, w("KS", 18 * c0, 18 * nc), w(XB, 0, 18 * nc), w("KV", 0, 18 * nc), OP.max, OP.min)
+        scan("KS" + js, w("KS", 18 * c0, 18 * nc), w(XB, 0, 18 * nc), w("KV", 18 * c0, 18 * nc), OP.max, OP.min)
         copy("KU" + js, ku, ks)
         tt("VG" + js, vg, ind(w("AB", b, 32 * n + 32), ku), y, OP.max)
         lin("DG" + js, dg, ind(w("VB", 0, 32 * n + 32), ku), w("DVF", 2 * t + j, 1), 0.0, "A")
@@ -275,7 +273,7 @@ def build(T, topo, core, nxt, par):
         ml = w("UI", 33 * c0 + 2 * n, nc)
         if j:
             act("Z" + s, w("Z" if t < 3 else "ZF", a, n), xs, AF.Abs)
-            act("NN" + s, w("NN", c0, nc), ks, AF.Sign)
+            act("NN" + s, w("NN", c0, nc), ks, AF.Sign, 1.0, -1.0)
             ts("GO" + s, w("GO", c0, nc), ks, 512.0 * nc + 17, OP.is_equal)
             tt("VF" + s, w("VF", c0, nc), w("NN", c0, nc), w("GO", c0, nc), OP.subtract)
             tt("TQ" + s, w("TQ", c0, nc), w("VF", c0, nc), w("D0", c0, nc), OP.mult)
@@ -284,7 +282,7 @@ def build(T, topo, core, nxt, par):
             if t < 3: send("m", t + 1, h, "MS", c0, nc), send("z", t + 1, h, "Z", a, n)
             return
         act("Z1" + s, z1, xs, AF.Abs)
-        if par["scalar"][h, 1] < 16: act("ZP" + s, w("P2", a, n), xs, AF.Abs)
+        if par["scalar"][h, 1] < 16 or s in par["zp"]: act("ZP" + s, w("P2", a, n), xs, AF.Abs)
         lin("Y1" + s, y, z1, 1.0, -255.0)
         mm("ub" + s, [(w("P6", 0, n), v("BW"), z1), (w("P6", n, n), v("BW4"), z1)], size=1)
         mm("xl" + s, [(w("P6", 2 * n, nc), v("RMW", S[r]), w("Z1", a + r, nc, 16)) for r in range(16)])
@@ -295,15 +293,14 @@ def build(T, topo, core, nxt, par):
         ts("UI" + s, w("UI", 33 * c0, 33 * nc), w("MI", 33 * c0, 33 * nc), int(TOP) + 4095, OP.bitwise_and)
         tt("X" + s, w("X", 17 * c0, 17 * nc), w("UI", 33 * c0 + n, 17 * nc), tc, OP.max)
         og, gr = w("P5", 256 + a, n), par["group"][h]
-        sb, xw = min(seg[h])[0], 2 if gr == 1 else 1
-        sl = max(seg[h])[0] + max(seg[h])[1] + 2 - sb
-        for run in runs[h]: tt("NF" + s, ends("NE", h, run), w("UI", 33 * c0 + 2 * n + run[0], len(run), run.step), w("SPT", c0 + run[0], len(run), run.step), OP.subtract)
+        (sb, ln), xw = seg[h], 2 if gr == 1 else 1
+        tt("NF" + s, w("NE", sb + ln - 1, nc, ln), ml, w("SPT", c0, nc), OP.subtract)
         for c in range(nc - 1, -1, -1):
             hi = 17 * c0 + 16 * c + 15
-            lo = hi - seg[h][c][1]
-            ts("NE" + s, w("NE", seg[h][c][0] + 1, hi - lo), v("X", S[hi:(lo if lo >= 0 else None):-1]), w("X", 17 * c0 + n + c, 1), OP.not_equal)
-        scan("SC" + s, w("SC", sb, sl), w("NE", sb, sl), w("RS", sb, sl), OP.mult, OP.add)
-        for run in runs[h]: copy("XF" + s, w("XF", 2 * c0 + xw * run[0], len(run), xw * run.step), ends("SC", h, run))
+            lo = hi - 16 * (c % gr + 1)
+            ts("NE" + s, w("NE", sb + ln * c + 1, hi - lo), v("X", S[hi:(lo if lo >= 0 else None):-1]), w("X", 17 * c0 + n + c, 1), OP.not_equal)
+        scan("SC" + s, w("SC", sb, nc * ln), w("NE", sb, nc * ln), w("RS", sb, nc * ln), OP.mult, OP.add)
+        copy("XF" + s, w("XF", 2 * c0, nc, xw), w("SC", sb + ln - 1, nc, ln))
         tt("PP" + s, og, w("UI", 33 * c0, n), og, OP.mult)
         tt("XP" + s, w("XP", a, n), w("W", a, n), og, OP.subtract)
         ts("NW" + s, w("NW", a, n), w("XP", a, n), 5, OP.arith_shift_right, 4095, OP.bitwise_and)
@@ -399,6 +396,14 @@ def schedule(ops, par):
 
 
 PLAN = {}
+CODE = "hmfmfyg3cxdxedhbdaewbgbcexe4bvaw8ncfdyg37qf3dygj9qcgcuc2h7ggbsgedbdu9tewb4agdjdge8ftbvf2c7foczezbpeh9obtaabib6akeodiajfzenf0bbcke9bna1eed0flawdycvadcffjbyebe8ftepedbsdoftffc8fgcjetceeabba4cjas8yea9tdqdzefefcufz9gaqepd1bqdvfccse9dcd47raa8z91bgeaezeqf7j2cte5cnelcehucjiid6drb8bf_BVBBAAAAAABAAAAVABBVAAABBAA"
+
+
+def unpack(ops, par):
+    al, (d, f) = "0123456789abcdefghijklmnopqrstuvwxyz", CODE.split("_")
+    names, flex = sorted({o["name"] for o in ops if o["step"] >= 0 and o["eng"]}), sorted({o["name"] for o in ops if len(o["eng"]) > 1})
+    due = {n: round((al.index(d[2 * i]) * 36 + al.index(d[2 * i + 1])) / 10 - 40, 1) for i, n in enumerate(names)}
+    return dict(par, due=due, pin={n: {"B": "VA"}.get(c, c) for n, c in zip(flex, f)})
 
 
 def rank_program(g, core, T, topo):
@@ -406,7 +411,7 @@ def rank_program(g, core, T, topo):
     if rank is None:
         return
     ops = build(T, topo, core, T.cores[(rank + 1) % len(T.cores)], PAR)
-    if not PLAN: PLAN["all"] = schedule(ops, PAR)
+    if not PLAN: PLAN["all"] = schedule(ops, unpack(ops, PAR))
     order, eng, waits, _, _ = PLAN["all"]
     Q = {"V": g.vector, "A": g.scalar, "T": g.tensor, "G": g, "S": g.sync}
     cnt = {e: 0 for e in Q}

@@ -7,10 +7,10 @@ SB = {"MCI": (1024, I), "MC": (1280, F), "PR": (4096, H), "AD": (4096, H), "GL":
       "DVF": (8, F), "WS": (1, F), "W4": (1, F), "OU": (256, U), "NO": (256, F), "O32": (256, F), "Z": (256, H), "ZF": (256, F), "MS": (16, U), "YM": (16, F),
       "KV": (288, F), "IOTA": (1024, F), "VB": (8224, H), "ON": (2048, H), "NON": (128, H), "IDN": (128, H), "NID": (128, H), "BLK": (128, H), "BLB": (128, H),
       "BW": (128, H), "BW4": (128, H), "BN": (128, H), "CMB": (256, H), "PM": (128, H), "MSK": (8, F), "PI": (1, I), "PR16": (1, I), "R16": (1, F), "R32": (1, F),
-      "C37": (1, F), "B8": (16, H), "FT": (128, H), "SP": (16, F), "SPT": (16, F), "BT": (272, H), "KI": (288, F), "GO": (16, H), "JK": (16, F), "AC": (1, F), "RY": (1, F),
+      "C37": (1, F), "B8": (16, H), "FT": (128, H), "SP": (16, F), "SPT": (16, F), "BT": (128, H), "KI": (288, F), "GO": (16, H), "JK": (16, F), "AC": (1, F), "RY": (1, F),
       "AB": (8320, H), "PB": (8320, H), "KB": (8192, H), "KS": (288, F), "KU": (16, U), "VG": (256, H), "DG": (256, H), "R0": (256, H), "Y": (256, H), "Z1": (256, H),
-      "M37": (528, F), "MI": (528, I), "UI": (528, I), "X": (272, F), "NE": (2200, F), "SC": (2200, F), "RS": (2200, F), "XF": (32, U), "W": (256, F), "XP": (256, I), "NW": (256, I)}
-for _n in ("M4", "D0", "VF", "NN", "TQ", "MN"): SB[_n] = (16, F)
+      "M37": (272, F), "QX": (272, F), "QU": (256, F), "X": (272, F), "OG": (256, F), "CU": (392, H), "HF": (136, H), "IDF": (128, F), "NE": (2200, F), "SC": (2200, F), "RS": (2200, F), "XF": (32, U), "W": (256, F), "XP": (256, I), "NW": (256, I)}
+for _n in ("M4", "ML", "D0", "VF", "NN", "TQ", "MN"): SB[_n] = (16, F)
 for _t in "0123": SB["ZI" + _t], SB["MU" + _t] = (256, H), (16, U)
 SCRATCH = {k: ("sbuf", [128, w], d) for k, (w, d) in SB.items()}
 SCRATCH["C"] = ("sbuf", [128, 256, 18], H)
@@ -20,7 +20,7 @@ for _b in range(8): SCRATCH["P%d" % _b] = ("psum", [128, 512], F)
 SEMAPHORES = ["sV", "sA", "sT", "sG", "so0", "so1", "so2"] + ["ld_" + n for n in ("m0", "mc", "pr", "ad", "gl", "z0", "wt", "dv")]
 SEMAPHORES += ["%s%d%d" % (n, t, h) for n in ("zi", "mi", "zl", "ml") for t in range(1, 4) for h in range(3)]
 
-BIG, TOP, MAGIC = 2.0 ** 25, 2.0 ** 23, 1.5 * 2.0 ** 23
+BIG, OFF, STEP, MAGIC = 2.0 ** 25, 511.5 - 2.0 ** 19, 5 * 2.0 ** 18, 1.5 * 2.0 ** 23
 PAR = {
     "cyc": 0.00083, "ovV": 0.0, "ovA": 0.0, "ovT": 0.03, "ovI": 0.05, "min": 64, "wake": 0.22, "cg": 1.56, "cs": 3.8, "pf": 0.5, "far": 2.0,
     "loads": (("S", "m0", "M0", 2.0), ("S", "mc", "MCI", 4.0), ("S", "pr", "PR", 6.5), ("S", "ad", "AD", 8.5), ("S", "gl", "GL", 9.2), ("S", "z0", "ZI0", 9.5),
@@ -28,7 +28,7 @@ PAR = {
     "chunks": ((8, 8), (0, 8)),
     "passes": ((0, 0), (1, 0), (0, 1), (1, 1)),
     "scalar": {(0, 0): 0, (1, 0): 8, (0, 1): 12, (1, 1): 12},
-    "split": (2, 2), "group": (8, 8), "zp": "", "pieces": 2, "pin": {}, "bias": 0.0, "no": "01", "period": 20.0, "due": {},
+    "split": (2, 2), "group": (8, 8), "dbanks": (0, 1), "act2": "01", "sp": {}, "spin": {}, "just": 1, "zp": "", "pieces": 2, "pin": {}, "bias": 0.0, "no": "01", "period": 20.0, "due": {},
 }
 
 
@@ -37,12 +37,16 @@ PIN = "G0=A G1=V Mb0=A Mb1=A O320=A O321=VA P00=A P01=A RMN=VA RMW=A Y0=A Y1=VA 
 DUE = "K0=-10.8 dma=-7.1 Z1=-6.3 P01=-5.6 O320=-5.6 a01=-5.4 KU00=-5.3 p00=-4.9 gn0=-3.9 Y0=-2.3 X0=-2.2 GO0=-2.2 OU0=-2 DG00=-1.3 O321=-1 ZP0=-0.9 DG10=-0.5 a00=-0.1 G0=-0 NW0=0.2 p01=0.7 OU1=0.7 c00=1.5 KU10=1.6 KS00=1.8 VG00=2.1 P00=2.2 R00=2.2 c10=2.4 MS0=2.4 W00=2.6 p10=3.1 M40=3.1 p11=3.3 R01=3.4 cg1=3.5 a10=4.1 zp0=4.2 ub1=4.2 X1=4.2 Y1=4.3 M41=4.5 W0=4.9 KS10=4.9 us1=5 Ml1=5 a11=5.4 xl0=5.9 Ml0=6.4 VG10=6.6 xl1=6.6 Z11=6.8 Mb1=7 ub0=7.2 G1=7.3 n01=7.5 zp1=7.8 n00=7.8 ZP1=7.8 MN1=8.1 K1=8.5 us0=8.6 D01=8.6 NE0=8.8 sz0=8.8 W1=8.9 n10=9 Z0=9.1 cg0=9.1 PP1=9.1 NF1=9.2 NO0=9.4 SC1=9.4 OG0=9.5 TQ0=9.6 D00=9.8 Mb0=10 VF1=10 KS11=10.1 e00=10.4 n11=10.5 x10=10.6 UI0=10.9 NF0=11 put0=11.2 MI0=11.4 OG1=11.6 Z10=11.6 MI1=11.7 KU01=11.8 x00=12 XF1=12 VF0=12.1 UI1=12.3 NE1=12.4 c01=12.4 SC0=12.5 c11=12.8 XF0=12.9 XP1=13 PP0=13.1 KS01=13.2 NW1=13.2 VG11=13.2 e01=13.4 TQ1=13.5 W01=13.5 NO1=13.6 MS1=13.7 gn1=14 put1=14.4 VG01=14.9 XP0=15 DG11=15.1 RY=15.5 NN1=15.7 Y10=15.8 NN0=16.4 A=17.4 MN0=17.7 DG01=18.1 Y11=18.5 GO1=18.6 sm0=19.3 x11=19.9 KU11=21 sm1=21.5 x01=21.8 AC=22 sz1=24.7 PM=28.2"
 PIN = "G0=VA G1=VA Mb0=VA Mb1=A O320=VA O321=A P00=VA P01=VA RMN=A RMW=VA Y0=VA Y1=VA Y10=VA Y11=A a00=A a01=VA a10=A a11=A p00=A p01=V p10=A p11=A zp0=V zp1=A"
 PAR.update({"due": {k: float(x) for k, x in (y.split("=") for y in DUE.split())}, "pin": dict(y.split("=") for y in PIN.split())})
-PAR.update({"scalar": {(0, 0): 0, (1, 0): 8, (0, 1): 8, (1, 1): 8}, "group": (2, 4), "zp": "01", "far": 1.5})
+PAR.update({"scalar": {(0, 0): 8, (1, 0): 8, (0, 1): 0, (1, 1): 8}, "group": (2, 4), "zp": "01", "far": 1.5})
+
+
+SECOND = [x + h + "1" for h in "01" for x in "d s c n KS KU VG DG x".split()] + [x + h for h in "01" for x in "NN GO VF TQ MN MS Z Y1 D0 M4".split()]
 
 
 def cost(w, e, par):
     kind, n = w
     if kind == "fix": return n
+    if kind == "sum": return sum(cost(x, e, par) for x in n)
     if kind == "mm": return par["ovT"] + sum(max(64, x) for x in n) * par["pf"] * par["cyc"]
     if kind == "G": return 0.17 + 2 * n * par["cyc"]
     if kind in ("cg", "cs"): return par["ov" + e] + par["ovI"] * (1.3 if e == "A" else 1.0) + n * par[kind] * par["cyc"]
@@ -93,6 +97,20 @@ def build(T, topo, core, nxt, par):
                     "banks": sorted({nm for nm, el in rd + wr if SCRATCH[nm][0] == "psum"})})
         return i
 
+    def join(count, size):
+        first_, made = len(ops) - count, ops[len(ops) - count:]
+        del ops[first_:]
+        runs = -(-count // size) if count else 0
+        new = [first_ + x * runs // count for x in range(count)]
+        for r in range(runs):
+            part = [o for o, x in zip(made, new) if x == first_ + r]
+            ops.append(dict(part[0], fn=lambda q, e, part=part: [o["fn"](q, e) for o in part][-1], hard=set().union(*[o["hard"] for o in part]),
+                            work=("sum", [o["work"] for o in part]), banks=sorted({b for o in part for b in o["banks"]})))
+        for nm in last:
+            m = last[nm] >= first_
+            if m.any(): last[nm][m] = np.array(new)[last[nm][m] - first_]
+            readers[nm] = [(new[r - first_] if r >= first_ else r, m) for r, m in readers[nm]]
+
     def price(o, ins, both=False):
         xs = [x for x in ins if isinstance(x, dict)]
         n = max([o["n"]] + [x["n"] for x in xs])
@@ -126,14 +144,14 @@ def build(T, topo, core, nxt, par):
 
     def fill(o, c): return op("fill", "V", lambda q, e: q.memset(o["ap"], c), [], [o], price(o, []))
 
-    def mm(nm, lst, first=True, final=True, size=None):
+    def mm(nm, lst, first=True, final=True, size=None, slow=1, whole=None):
         size = size or len(lst)
 
         def fn(q, e):
             x = None
             for k, (o, l, r) in enumerate(lst): x = q.matmul(o["ap"], l["ap"], r["ap"], first and k % size == 0, final and k % size == size - 1)
             return x
-        return op(nm, "T", fn, [x for y in lst for x in y[1:]], [y[0] for y in lst], ("mm", [y[2]["n"] for y in lst]))
+        return op(nm, "T", fn, [x for y in lst for x in y[1:]], [whole] if whole else [y[0] for y in lst], ("mm", [slow * y[2]["n"] for y in lst]))
 
     def G(o, ins, fn): return op("const", "G", lambda q, e: fn(q), ins, [o], ("G", o["n"]))
 
@@ -158,28 +176,27 @@ def build(T, topo, core, nxt, par):
     copy("MU0", v("MU0"), v("M0"))
     copy("MC", w("MC", 0, 1024), v("MCI"))
     fill(w("MC", 1024, 16 * ncm), 0.0)
-    copy("MSK", v("MSK"), w("BLK", 0, 8, 16))
-    for x in range(8): ts("RMC", v("RMC", S[:, x, :]), v("CMB"), w("MSK", x, 1), OP.mult, BIG, OP.mult)
+    ts("MSK", v("MSK"), w("BLK", 0, 8, 16), BIG, OP.mult)
+    for x in range(8): lin("RMC", v("RMC", S[:, x, :]), v("CMB"), w("MSK", x, 1))
     copy("B8", w("B8", 0, 8), w("BLK", 0, 8, 16))
     ts("B8", w("B8", 8, 8), w("BLK", 0, 8, 16), -1.0, OP.mult)
-    ts("WS", v("WS"), v("WT"), 4.0 / BIG, OP.mult)
-    ts("W4", v("W4"), v("WT"), 4.0, OP.mult)
+    ts("WS", v("WS"), v("WT"), 1.0 / BIG, OP.mult)
     lin("RMW", v("RMW"), v("RMC"), v("WS"))
     ts("BW", v("BW"), v("BLK"), v("WT"), OP.mult)
-    ts("BW4", v("BW4"), v("BLK"), v("W4"), OP.mult)
-    ts("BN", v("BN"), v("BLK"), -BIG, OP.mult)
+    ts("BN", v("BN"), v("BLK"), STEP, OP.mult)
     ts("NID", NID, IDN, -1.0, OP.mult)
     copy("DVF", v("DVF"), v("DV"))
     for h, (c0, nc) in enumerate(chunks):
         b, n = 32 * (16 * c0 + 2 - h), 16 * nc
-        fill(w("AB", b, 16), 0.0), fill(w("AB", b + 16 + 32 * n, 16), 0.0), fill(w("M37", 33 * c0, n), 0.0)
+        fill(w("AB", b, 16), 0.0), fill(w("AB", b + 16 + 32 * n, 16), 0.0)
         for x in range(0, 16 * n, 1024):
             lin("AB%d" % h, w("AB", b + 17 + 2 * x, min(1024, 16 * n - x), 2), w("ON", 0, min(1024, 16 * n - x)), 0.0)
             lin("PB%d" % h, w("PB", b + 16 + 2 * x, min(1024, 16 * n - x), 2), w("ON", 0, min(1024, 16 * n - x)), 0.0)
         fill(w("AB", b + 47, n, 32), -256.0)
     fill(v("C", S[:, 0]), 0.0)
     LO, HI = S[0:64], S[64:128]
-    fill(v("NON"), -1.0), fill(v("PM", None, LO), -1.0), fill(v("PM", None, HI), 1.0), fill(v("BT", S[0:256], LO), BIG / 128), fill(v("BT", S[0:256], HI), 12 * BIG / 64), fill(v("BT", S[256:272]), 0.0)
+    fill(v("NON"), -1.0), fill(v("PM", None, LO), -1.0), fill(v("PM", None, HI), 1.0), fill(v("BT", None, LO), -STEP / 128), fill(v("BT", None, HI), -12.5 * STEP / 64), fill(v("HF"), 1.0 / 256)
+    fill(v("CU"), 0.0), fill(v("CU", S[128:256], LO), -32.0), fill(v("CU", S[128:256], HI), 1.0 / 128), copy("IDF", v("IDF"), IDN)
     ts("PR16", v("PR16"), v("PI"), 15, OP.bitwise_and)
     copy("R16", R16, v("PR16"))
     ts("R32", v("R32"), R16, 32.0, OP.mult)
@@ -195,11 +212,11 @@ def build(T, topo, core, nxt, par):
         sb, sc, sp = seg[h][0], w("SC", seg[h][0], nc * ln), w("SP", c0, nc)
         G(sc, [], lambda q, sc=sc, nc=nc, ln=ln: q.iota(sc["ap"], [[0, nc], [-1, ln]], 16, 0, **imp))
         G(sp, [], lambda q, sp=sp, nc=nc, gr=gr: q.iota(sp["ap"], [[0, nc // gr], [16, gr]], 1024, 0, **imp))
-        ts("RS", sc, sc, R16, OP.is_equal, 0.25, OP.mult)
+        ts("RS", sc, sc, R16, OP.is_equal)
         tt("RS", w("RS", sb, nc * ln - 1), w("SC", sb, nc * ln - 1), w("SC", sb + 1, nc * ln - 1), OP.subtract)
         ts("RS", w("RS", sb + ln - 1, nc, ln), sp, R16, OP.add)
-        ts("SPT", w("SPT", c0, nc), w("RS", sb + ln - 1, nc, ln), 4.0, OP.mult, TOP, OP.add)
-        fill(w("NE", sb, nc * ln), 1.0), fill(w("NE", sb, nc, ln), 0.0)
+        ts("SPT", w("SPT", c0, nc), w("RS", sb + ln - 1, nc, ln), -OFF, OP.add)
+        lin("NE", w("NE", sb, nc * ln), w("ON", 0, nc * ln)), fill(w("NE", sb, nc, ln), 0.0)
     unit, br = BIG / 64, {}
     for na in sorted(set(par["scalar"].values())):
         x = br[na] = len(br)
@@ -228,12 +245,12 @@ def build(T, topo, core, nxt, par):
         scan("K" + s, v("KB", S[32 * (a + n) - 1:(32 * a - 1 if a else None):-1]), v("AB", back), v("PB", back), OP.add, OP.max)
         if par["scalar"][h, 0] < 17: mm("zp" + s, [(w("P2", a, n), IDN, z0)])
         lin("Y" + s, w("Y", a, n), z0, 1.0, -255.0)
-        lin("Mb" + s, w("M37", 33 * c0 + n, n), ind(v("IOTA"), mu), 148.0, TOP)
-        ts("Ml" + s, w("M37", 33 * c0 + 2 * n, nc), mu, 148.0, OP.mult, TOP, OP.add)
-        ts("M4" + s, w("M4", c0, nc), mu, 4.0, OP.mult, TOP, OP.add)
+        lin("Mb" + s, w("M37", 17 * c0, n), ind(v("IOTA"), mu), 37.0, -OFF - 0.5)
+        ts("Ml" + s, w("M37", 17 * c0 + n, nc), mu, 37.0, OP.mult, -OFF - 0.5, OP.add)
+        ts("M4" + s, w("M4", c0, nc), mu, -OFF, OP.add)
         mm("e0" + s, [(xs, IDN, w("KB", 32 * a + 1, n, 32)), (xs, IDN, w("AB", b + 16, n, 32))])
         act("R0" + s, w("R0", a, n), xs, AF.Relu)
-        rows, w0, og = S[0:n], w("P5", 128, n), w("P5", 256 + a, n)
+        rows, w0, og = S[0:n], w("P5", 128, n), w("OG", a, n)
         for k4 in range(1, -1, -1):
             lst = []
             for k in range(8 * k4, 8 * k4 + 8):
@@ -257,20 +274,28 @@ def build(T, topo, core, nxt, par):
             def kk(k): return w("KB", 32 * a1 + (2 * k - 1 if k else 0), m, 32)
             per = 512 // m
             for k0 in range(0, na, per):
-                bank = "P%d" % (turn[0] % 2)
+                bank = "P%d" % par["dbanks"][turn[0] % len(par["dbanks"])]
                 turn[0] += 1
                 ks_ = range(k0, min(na, k0 + per))
                 mm("d" + js, [x for k in ks_ for x in ((w(bank, m * (k - k0), m), NID, kk(k)), (w(bank, m * (k - k0), m), IDN, w(z["el"][0][0], a1, m)))], size=2)
-                for k in ks_: act("c" + js, v("C", S[a1:a1 + m, k + 1]), w(bank, m * (k - k0), m), AF.Sign, 1.0, 0.5)
+                for k in ks_: act("s" + js, v("C", S[a1:a1 + m, k + 1]), w(bank, m * (k - k0), m), AF.Sign, 1.0, 0.5)
+                join(len(ks_), 4)
             for k in range(16 - j, na - 1, -1): tt("c" + js, v("C", S[a1:a1 + m, k + 1]), kk(k), w("P2", a1, m), OP.is_le)
+            join(17 - j - na, 3)
             o = w(XB, 18 * c1, 18 * cs)
             mm("n" + js, [(o, v("PM"), v("BR", S[br[na], 0:cs]))] + [(o, v("RMC", S[r]), v("C", S[a1 + r:a1 + m:16])) for r in range(16)])
         scan("KS" + js, w("KS", 18 * c0, 18 * nc), w(XB, 0, 18 * nc), w("KV", 18 * c0, 18 * nc), OP.max, OP.min)
         copy("KU" + js, ku, ks)
-        tt("VG" + js, vg, ind(w("AB", b, 32 * n + 32), ku), y, OP.max)
         lin("DG" + js, dg, ind(w("VB", 0, 32 * n + 32), ku), w("DVF", 2 * t + j, 1), 0.0, "A")
-        mm("x" + js, [(xs, IDN, z), (xs, NID, vg), (xs, NID, dg)])
-        ml = w("UI", 33 * c0 + 2 * n, nc)
+        if j and s in par["act2"]:
+            lin("VG" + js, vg, ind(w("AB", b, 32 * n + 32), ku))
+            mm("e" + js + "x", [(xs, IDN, z), (xs, NID, vg)])
+            act("Y1" + s, y, xs, AF.Relu, 1.0, -255.0)
+            mm("x" + js, [(xs, IDN, z), (xs, NID, vg), (xs, NID, dg), (xs, NID, y)])
+        else:
+            tt("VG" + js, vg, ind(w("AB", b, 32 * n + 32), ku), y, OP.max)
+            mm("x" + js, [(xs, IDN, z), (xs, NID, vg), (xs, NID, dg)])
+        ml = w("X", 17 * c0 + n, nc)
         if j:
             act("Z" + s, w("Z" if t < 3 else "ZF", a, n), xs, AF.Abs)
             act("NN" + s, w("NN", c0, nc), ks, AF.Sign, 1.0, -1.0)
@@ -278,31 +303,39 @@ def build(T, topo, core, nxt, par):
             tt("VF" + s, w("VF", c0, nc), w("NN", c0, nc), w("GO", c0, nc), OP.subtract)
             tt("TQ" + s, w("TQ", c0, nc), w("VF", c0, nc), w("D0", c0, nc), OP.mult)
             tt("MN" + s, w("MN", c0, nc), w("TQ", c0, nc), ml, OP.add)
-            ts("MS" + s, w("MS" if t < 3 else "YM", c0, nc), w("MN", c0, nc), -TOP, OP.add, 0.25, OP.mult)
+            ts("MS" + s, w("MS" if t < 3 else "YM", c0, nc), w("MN", c0, nc), OFF, OP.add)
             if t < 3: send("m", t + 1, h, "MS", c0, nc), send("z", t + 1, h, "Z", a, n)
             return
         act("Z1" + s, z1, xs, AF.Abs)
         if par["scalar"][h, 1] < 16 or s in par["zp"]: act("ZP" + s, w("P2", a, n), xs, AF.Abs)
-        lin("Y1" + s, y, z1, 1.0, -255.0)
-        mm("ub" + s, [(w("P6", 0, n), v("BW"), z1), (w("P6", n, n), v("BW4"), z1)], size=1)
-        mm("xl" + s, [(w("P6", 2 * n, nc), v("RMW", S[r]), w("Z1", a + r, nc, 16)) for r in range(16)])
+        if s not in par["act2"]: lin("Y1" + s, y, z1, 1.0, -255.0)
+        TB = "P%d" % (6 + h % 2)
+        tb, ub, uh, xb, xl, xx = w(TB, 0, 49 * nc), w(TB, 0, n), w(TB, n, n), w(TB, 2 * n, n), w(TB, 3 * n, nc), w(TB, 2 * n, 17 * nc)
+        mm("mc" + s, [(tb, ON, w("CU", 128 - n, 49 * nc))], True, False)
+        mm("mo" + s, [(xx, v("IDF"), w("M37", 17 * c0, 17 * nc))], False, False, slow=4, whole=tb)
+        mm("ub" + s, [(ub, v("BW"), z1), (uh, v("BW"), z1), (xb, v("BW"), z1)], False, False, whole=tb)
+        mm("xl" + s, [(xl, v("RMW", S[r]), w("Z1", a + r, nc, 16)) for r in range(16)], False, False, whole=tb)
         tt("cg" + s, v("C", S[a:a + n, 17]), w("KB", 32 * a + 31, n, 32), w("P2", a, n) if s in par["zp"] else z1, OP.is_le)
-        tc = w("P7", 0, n + nc)
-        mm("gn" + s, [(tc, v("PM"), w("BT", 256 - n, n + nc)), (w("P7", 0, n), v("BN"), v("C", S[a:a + n, 17]))])
-        tt("MI" + s, w("MI", 33 * c0, 33 * nc), w("P6", 0, 33 * nc), w("M37", 33 * c0, 33 * nc), OP.add)
-        ts("UI" + s, w("UI", 33 * c0, 33 * nc), w("MI", 33 * c0, 33 * nc), int(TOP) + 4095, OP.bitwise_and)
-        tt("X" + s, w("X", 17 * c0, 17 * nc), w("UI", 33 * c0 + n, 17 * nc), tc, OP.max)
-        og, gr = w("P5", 256 + a, n), par["group"][h]
+        mm("gn" + s, [(xb, v("PM"), w("BT", 0, n)), (xb, v("BN"), v("C", S[a:a + n, 17])), (xx, ON, w("HF", 0, 17 * nc))], False, True, whole=tb)
+        qx, qu, x = w("QX", 17 * c0, 17 * nc), w("QU", a, n), w("X", 17 * c0, 17 * nc)
+        lin("TX" + s, qx, xx, 1.0 / 1024, MAGIC)
+        act("QX" + s, qx, qx, AF.Relu, 1024.0, -2.0 ** 19 - 1024 * MAGIC)
+        tt("X" + s, x, xx, qx, OP.subtract)
+        lin("TU" + s, qu, uh, 1.0 / 4096, MAGIC)
+        lin("QU" + s, qu, qu, -4096.0, 4096 * MAGIC)
+        tt("U" + s, ub, ub, qu, OP.add)
+        gr = par["group"][h]
         (sb, ln), xw = seg[h], 2 if gr == 1 else 1
         tt("NF" + s, w("NE", sb + ln - 1, nc, ln), ml, w("SPT", c0, nc), OP.subtract)
         for c in range(nc - 1, -1, -1):
             hi = 17 * c0 + 16 * c + 15
             lo = hi - 16 * (c % gr + 1)
             ts("NE" + s, w("NE", sb + ln * c + 1, hi - lo), v("X", S[hi:(lo if lo >= 0 else None):-1]), w("X", 17 * c0 + n + c, 1), OP.not_equal)
+        join(nc, 4)
         scan("SC" + s, w("SC", sb, nc * ln), w("NE", sb, nc * ln), w("RS", sb, nc * ln), OP.mult, OP.add)
         copy("XF" + s, w("XF", 2 * c0, nc, xw), w("SC", sb + ln - 1, nc, ln))
-        tt("PP" + s, og, w("UI", 33 * c0, n), og, OP.mult)
-        tt("XP" + s, w("XP", a, n), w("W", a, n), og, OP.subtract)
+        tt("PP" + s, ub, ub, w("OG", a, n), OP.mult)
+        tt("XP" + s, w("XP", a, n), w("W", a, n), ub, OP.subtract)
         ts("NW" + s, w("NW", a, n), w("XP", a, n), 5, OP.arith_shift_right, 4095, OP.bitwise_and)
         for c in range(nc - gr, -1, -gr): copy("put" + s, ind(w("MC", 0, 1024 + 16 * ncm), w("XF", 2 * c0 + xw * c, gr)), w("NW", a + 16 * c, 16 * gr))
         tt("D0" + s, w("D0", c0, nc), w("M4", c0, nc), ml, OP.subtract)
@@ -322,7 +355,7 @@ def build(T, topo, core, nxt, par):
             if j == 0: head(t, h)
             one_pass(t, h, j)
         if t < 3:
-            pa = w("P6", 496, 16)
+            pa = w("P5", 496, 16)
             mm("A", [(pa, ON, v("GO"))])
             act("AC", v("JK"), pa, AF.Identity, -0.5, 1.0 / 64, v("AC"))
             ts("RY", v("RY"), v("AC"), MAGIC, OP.add, MAGIC, OP.subtract)
@@ -342,7 +375,7 @@ def first(lst, t):
     return lo
 
 
-def place(ops, par, links, prio):
+def place(ops, par, links, prio, fixed=None, tail=None):
     n, wake = len(ops), par["wake"]
     kids, need = [[] for _ in ops], [len(x) for x in links]
     for i in range(n):
@@ -354,8 +387,8 @@ def place(ops, par, links, prio):
         i = max(ready, key=lambda x: (prio[x], -x))
         ready.remove(i)
         o = ops[i]
-        est, best = max([start[d] + dur[d] + gap for d, gap in links[i]] + [0.0]), None
-        for e in par["pin"].get(o["name"], o["eng"]) if len(o["eng"]) > 1 else o["eng"] or [""]:
+        est, best = max([start[d] + dur[d] + gap for d, gap in links[i]] + [tail[i] if tail else 0.0]), None
+        for e in [fixed[i]] if fixed else par["pin"].get(o["name"], o["eng"]) if len(o["eng"]) > 1 else o["eng"] or [""]:
             c, t0, moved = cost(o["work"], e, par), est, True
             while moved and e:
                 moved = False
@@ -381,11 +414,17 @@ def schedule(ops, par):
     n, wake = len(ops), par["wake"]
     late = [o["done"][2] - o["work"][1] if o["done"] else 0.0 for o in ops]
     links = [[(d, late[d] + wake if ops[d]["eng"] and o["eng"] else late[d] * bool(o["eng"]) + wake) for d in o["hard"]] + [(d, 0.0) for d in o["soft"]] for o in ops]
-    due = [par["period"] * o["step"] + par["due"].get(o["name"], 0.0) + 1e-6 * i if o["step"] >= 0 else 999.0 for i, o in enumerate(ops)]
+    due = [par["period"] * o["step"] + par["due"].get(o["name"], 0.0) + par["due"].get("last", 0.0) * (o["step"] == 3 and o["name"] in SECOND) + par["sp"].get((o["name"], o["step"]), 0.0) + 1e-6 * i if o["step"] >= 0 else 999.0 for i, o in enumerate(ops)]
     for i in range(n - 1, -1, -1):
         for d, gap in links[i]:
             if ops[d]["step"] < 0: due[d] = min(due[d], due[i] - gap - cost(ops[d]["work"], ops[d]["eng"][0], par))
     start, dur, eng = place(ops, par, links, [-x for x in due])
+    back = [[] for _ in ops]
+    for i in range(n):
+        for d, gap in links[i]: back[d].append((i, gap))
+    for _ in range(par["just"]):
+        s2, _, _ = place(ops, par, back, [start[i] + dur[i] for i in range(n)], eng, [0.0 if back[i] else late[i] for i in range(n)])
+        start, _, _ = place(ops, par, links, [s2[i] + dur[i] for i in range(n)], eng)
     order = sorted(range(n), key=lambda i: (start[i], i))
     user, waits = {}, [set(o["hard"]) for o in ops]
     for i in order:
@@ -396,12 +435,12 @@ def schedule(ops, par):
 
 
 PLAN = {}
-CODE = "hmfmfyg3cxdxedhbdaewbgbcexe4bvaw8ncfdyg37qf3dygj9qcgcuc2h7ggbsgedbdu9tewb4agdjdge8ftbvf2c7foczezbpeh9obtaabib6akeodiajfzenf0bbcke9bna1eed0flawdycvadcffjbyebe8ftepedbsdoftffc8fgcjetceeabba4cjas8yea9tdqdzefefcufz9gaqepd1bqdvfccse9dcd47raa8z91bgeaezeqf7j2cte5cnelcehucjiid6drb8bf_BVBBAAAAAABAAAAVABBVAAABBAA"
+CODE = "jskhe0indrf3gbg300iud8chbijbaebmdegea9faepbhfqj7k0gvawkk95i0c4h3edaqgughf4gabr5hb7gnc4imhqgoc6dj9icf8y6t9vc9gveo7keh7nelezi4i7fhble5b3az5w65c4a9agi9eyedd6b1e2et2qjsc7crgne8goffd9bzd5lbk0a5bnca7ffsefbyb0aiepf8eud0c6b6enfogj5g65jjjqk46ej6gtd2apfp8oci8655icfhdpar64ahaddwhzdrc36t7zfc7bi1eb9n5gfffpl759fv9ea85v9s_VBVABABABABAAAAAAABBABAAAVAVABAAVAA"
 
 
 def unpack(ops, par):
     al, (d, f) = "0123456789abcdefghijklmnopqrstuvwxyz", CODE.split("_")
-    names, flex = sorted({o["name"] for o in ops if o["step"] >= 0 and o["eng"]}), sorted({o["name"] for o in ops if len(o["eng"]) > 1})
+    names, flex = sorted({o["name"] for o in ops if o["step"] >= 0 and o["eng"]} | {"last"}), sorted({o["name"] for o in ops if len(o["eng"]) > 1})
     due = {n: round((al.index(d[2 * i]) * 36 + al.index(d[2 * i + 1])) / 10 - 40, 1) for i, n in enumerate(names)}
     return dict(par, due=due, pin={n: {"B": "VA"}.get(c, c) for n, c in zip(flex, f)})
 

import numpy as np
from concourse.mybir import AluOpType as OP, ActivationFunctionType as AF

F, H, I, U = "float32", "bfloat16", "int32", "uint16"
S = np.s_
SB = {"MCI": (1024, I), "MC": (1280, F), "PR": (4096, H), "AD": (4096, H), "GL": (1024, H), "M0": (16, I), "DV": (8, H), "WT": (1, H),
      "DVF": (8, F), "WS": (1, F), "W4": (1, F), "OU": (256, U), "NO": (256, F), "O32": (256, F), "Z": (256, H), "ZF": (256, F), "MS": (16, U), "YM": (16, F),
      "KV": (288, F), "IOTA": (1024, F), "VB": (8224, H), "ON": (2048, H), "NON": (128, H), "IDN": (128, H), "NID": (128, H), "BLK": (128, H), "BLB": (128, H),
      "BW": (128, H), "BW4": (128, H), "BN": (128, H), "CMB": (256, H), "PM": (128, H), "MSK": (8, F), "PI": (1, I), "PR16": (1, I), "R16": (1, F), "R32": (1, F),
      "C37": (1, F), "B8": (16, H), "FT": (128, H), "SP": (16, F), "SPT": (16, F), "BT": (128, H), "KI": (288, F), "GO": (16, H), "JK": (16, F), "AC": (1, F), "RY": (1, F),
      "AB": (8320, H), "PB": (8320, H), "KB": (8192, H), "KS": (288, F), "KU": (16, U), "VG": (256, H), "DG": (256, H), "R0": (256, H), "Y": (256, H), "Z1": (256, H),
      "M37": (272, F), "QX": (272, F), "QU": (256, F), "X": (272, F), "OG": (256, F), "CU": (392, H), "HF": (136, H), "IDF": (128, F), "NE": (2200, F), "SC": (2200, F), "RS": (2200, F), "XF": (32, U), "W": (256, F), "XP": (256, I), "NW": (256, I)}
for _n in ("M4", "ML", "D0", "VF", "NN", "TQ", "MN"): SB[_n] = (16, F)
for _t in "0123": SB["ZI" + _t], SB["MU" + _t] = (256, H), (16, U)
SCRATCH = {k: ("sbuf", [128, w], d) for k, (w, d) in SB.items()}
SCRATCH["C"] = ("sbuf", [128, 256, 18], H)
for _n in ("RMC", "RMW"): SCRATCH[_n] = ("sbuf", [128, 16, 8, 16], H)
SCRATCH["BR"] = ("sbuf", [128, 12, 16, 18], H)
for _b in range(8): SCRATCH["P%d" % _b] = ("psum", [128, 512], F)
SEMAPHORES = ["sV", "sA", "sT", "sG", "so0", "so1", "so2"] + ["ld_" + n for n in ("m0", "mc", "pr", "ad", "gl", "z0", "wt", "dv")]
SEMAPHORES += ["%s%d%d" % (n, t, h) for n in ("zi", "mi", "zl", "ml") for t in range(1, 4) for h in range(3)]

BIG, OFF, STEP, MAGIC = 2.0 ** 25, 511.5 - 2.0 ** 19, 5 * 2.0 ** 18, 1.5 * 2.0 ** 23
PAR = {
    "cyc": 0.00083, "ovV": 0.0, "ovA": 0.0, "ovT": 0.03, "ovI": 0.05, "min": 64, "wake": 0.22, "cg": 1.56, "cs": 3.8, "pf": 0.5, "far": 2.0,
    "loads": (("S", "m0", "M0", 2.0), ("S", "mc", "MCI", 4.0), ("S", "pr", "PR", 6.5), ("S", "ad", "AD", 8.5), ("S", "gl", "GL", 9.2), ("S", "z0", "ZI0", 9.5),
              ("A", "wt", "WT", 2.5), ("A", "dv", "DV", 2.5)),
    "chunks": ((8, 8), (0, 8)),
    "passes": ((0, 0), (1, 0), (0, 1), (1, 1)),
    "scalar": {(0, 0): 0, (1, 0): 8, (0, 1): 12, (1, 1): 12},
    "split": (2, 2), "group": (8, 8), "dbanks": (0, 1), "act2": "01", "sp": {}, "spin": {}, "just": 1, "zp": "", "pieces": 2, "pin": {}, "bias": 0.0, "no": "01", "period": 20.0, "due": {},
}


DUE = "KU00=-6.6 p10=-3.4 p00=-3.1 p01=-2.6 OU0=-1.7 dma=-1.7 NE0=0.2 K0=0.8 a01=0.9 a00=1.2 G0=1.2 P00=1.3 p11=1.3 OU1=1.5 P01=1.5 a10=1.7 zp0=2.3 a11=2.5 c00=3.4 K1=3.4 VG10=3.4 zp1=3.5 G1=3.6 KS00=3.6 VG00=4.1 c10=4.4 cg1=4.4 x10=4.6 d00=4.9 n10=5 R00=5.1 n00=5.2 x00=5.2 Ml0=5.2 ZP0=5.4 Y0=5.6 M40=5.7 DG00=5.8 OG1=6.1 d10=6.4 us0=6.5 O320=6.5 D00=6.8 Z10=6.9 Z0=7.1 R01=7.6 KU10=7.7 M41=7.7 DG10=7.9 ZP1=7.9 VG01=7.9 e00=8 TQ0=8 PP0=8.1 xl1=8.2 Z11=8.3 W0=8.5 TQ1=8.6 gn0=8.9 ub1=8.9 Mb1=9 W1=9 Mb0=9.1 put1=9.2 NO0=9.2 DG01=9.2 GP1=9.2 SC1=9.2 NF1=9.3 Y1=9.5 O321=9.5 KS10=9.6 NE1=9.6 XF1=9.6 X0=9.9 W00=10.1 DM0=10.2 n11=10.2 cg0=10.3 NF0=10.4 PP1=10.5 KS11=10.5 xl0=10.6 OG0=10.6 ub0=10.8 NW0=10.8 MI0=10.9 X1=11 GP0=11.1 SC0=11.4 us1=11.5 XF0=11.5 UI1=11.5 NG1=11.5 W01=12 UI0=12 put0=12 d01=12 NG0=12.1 Ml1=12.2 c01=12.2 n01=12.3 sz0=12.6 D01=12.6 MI1=12.7 NN0=12.7 KS01=12.8 KU01=12.9 XP1=13 c11=13 GO0=13 VF0=13.1 NW1=13.4 Y11=13.4 e01=13.4 NO1=13.6 XP0=13.7 MS0=13.8 DM1=14 DG11=14.2 gn1=14.2 d11=14.5 MS1=14.8 GO1=15 VF1=15.1 AC=15.6 Y10=15.8 RY=16.3 VG11=16.5 NN1=16.5 sm1=16.8 sm0=17.8 Z1=18.6 MN0=19 MN1=19.3 A=20.3 KU11=20.3 PM=21.7 x11=23.4 x01=25.7 sz1=27"
PIN = "G0=A G1=V Mb0=A Mb1=A O320=A O321=VA P00=A P01=A RMN=VA RMW=A Y0=A Y1=VA Y10=VA Y11=A a00=A a01=V a10=A a11=A p00=VA p01=A p10=A p11=VA"
DUE = "K0=-10.8 dma=-7.1 Z1=-6.3 P01=-5.6 O320=-5.6 a01=-5.4 KU00=-5.3 p00=-4.9 gn0=-3.9 Y0=-2.3 X0=-2.2 GO0=-2.2 OU0=-2 DG00=-1.3 O321=-1 ZP0=-0.9 DG10=-0.5 a00=-0.1 G0=-0 NW0=0.2 p01=0.7 OU1=0.7 c00=1.5 KU10=1.6 KS00=1.8 VG00=2.1 P00=2.2 R00=2.2 c10=2.4 MS0=2.4 W00=2.6 p10=3.1 M40=3.1 p11=3.3 R01=3.4 cg1=3.5 a10=4.1 zp0=4.2 ub1=4.2 X1=4.2 Y1=4.3 M41=4.5 W0=4.9 KS10=4.9 us1=5 Ml1=5 a11=5.4 xl0=5.9 Ml0=6.4 VG10=6.6 xl1=6.6 Z11=6.8 Mb1=7 ub0=7.2 G1=7.3 n01=7.5 zp1=7.8 n00=7.8 ZP1=7.8 MN1=8.1 K1=8.5 us0=8.6 D01=8.6 NE0=8.8 sz0=8.8 W1=8.9 n10=9 Z0=9.1 cg0=9.1 PP1=9.1 NF1=9.2 NO0=9.4 SC1=9.4 OG0=9.5 TQ0=9.6 D00=9.8 Mb0=10 VF1=10 KS11=10.1 e00=10.4 n11=10.5 x10=10.6 UI0=10.9 NF0=11 put0=11.2 MI0=11.4 OG1=11.6 Z10=11.6 MI1=11.7 KU01=11.8 x00=12 XF1=12 VF0=12.1 UI1=12.3 NE1=12.4 c01=12.4 SC0=12.5 c11=12.8 XF0=12.9 XP1=13 PP0=13.1 KS01=13.2 NW1=13.2 VG11=13.2 e01=13.4 TQ1=13.5 W01=13.5 NO1=13.6 MS1=13.7 gn1=14 put1=14.4 VG01=14.9 XP0=15 DG11=15.1 RY=15.5 NN1=15.7 Y10=15.8 NN0=16.4 A=17.4 MN0=17.7 DG01=18.1 Y11=18.5 GO1=18.6 sm0=19.3 x11=19.9 KU11=21 sm1=21.5 x01=21.8 AC=22 sz1=24.7 PM=28.2"
PIN = "G0=VA G1=VA Mb0=VA Mb1=A O320=VA O321=A P00=VA P01=VA RMN=A RMW=VA Y0=VA Y1=VA Y10=VA Y11=A a00=A a01=VA a10=A a11=A p00=A p01=V p10=A p11=A zp0=V zp1=A"
PAR.update({"due": {k: float(x) for k, x in (y.split("=") for y in DUE.split())}, "pin": dict(y.split("=") for y in PIN.split())})
PAR.update({"scalar": {(0, 0): 8, (1, 0): 8, (0, 1): 0, (1, 1): 8}, "group": (2, 4), "zp": "01", "far": 1.5})


SECOND = [x + h + "1" for h in "01" for x in "d s c n KS KU VG DG x".split()] + [x + h for h in "01" for x in "NN GO VF TQ MN MS Z Y1 D0 M4".split()]


def cost(w, e, par):
    kind, n = w
    if kind == "fix": return n
    if kind == "sum": return sum(cost(x, e, par) for x in n)
    if kind == "mm": return par["ovT"] + sum(max(64, x) for x in n) * par["pf"] * par["cyc"]
    if kind == "G": return 0.17 + 2 * n * par["cyc"]
    if kind in ("cg", "cs"): return par["ov" + e] + par["ovI"] * (1.3 if e == "A" else 1.0) + n * par[kind] * par["cyc"]
    return par["ov" + e] + max(par["min"], n * (1.0 if e == "A" else kind)) * par["cyc"]


def build(T, topo, core, nxt, par):
    ops, last, readers, step = [], {}, {}, [-1]
    grid = {k: np.arange(int(np.prod(x[1][1:]))).reshape(x[1][1:]) for k, x in SCRATCH.items()}

    def v(name, ix=None, rows=S[:]):
        if ix is None: ap, el = T[name][rows], grid[name]
        else:
            ix = ix if isinstance(ix, tuple) else (ix,)
            ap, el = T[name][(rows,) + ix], grid[name][ix]
        return {"ap": ap, "el": [(name, np.ravel(el))], "n": int(np.size(el)), "b": 4 if SCRATCH[name][2] in (F, I) else 2, "ps": SCRATCH[name][0] == "psum"}

    def w(name, a, n, step=1): return v(name, S[a:a + (n - 1) * step + 1:step])

    def ind(win, off):
        return {"ap": win["ap"].indirect(off["ap"]), "el": win["el"], "off": off["el"], "n": 16 * off["n"], "b": 4, "ps": False}

    def op(name, eng, fn, ins, outs, work, done=None, after=()):
        i = len(ops)
        raw, war = set(after), set()
        rd = [e for x in ins + outs if isinstance(x, dict) for e in x.get("off", [])] + [e for x in ins if isinstance(x, dict) for e in x["el"]]
        wr = [e for x in outs for e in x["el"]]
        for nm, el in rd + wr:
            if nm not in last: last[nm], readers[nm] = np.full(grid[nm].size, -1), []
        for nm, el in rd: raw.update(np.unique(last[nm][el]).tolist())
        for nm, el in wr:
            war.update(np.unique(last[nm][el]).tolist())
            keep = []
            for r, m in readers[nm]:
                if m[el].any():
                    war.add(r)
                    m[el] = False
                if m.any(): keep.append((r, m))
            readers[nm] = keep
            last[nm][el] = i
        for nm, el in rd:
            m = np.zeros(grid[nm].size, bool)
            m[el] = True
            readers[nm].append((i, m))
        deps = (raw | war) - {-1, i}
        soft = {d for d in deps if eng == "T" and ops[d]["eng"] == "T"}
        ops.append({"name": name, "eng": eng, "fn": fn, "hard": deps - soft, "soft": soft, "work": work, "done": done, "step": step[0],
                    "banks": sorted({nm for nm, el in rd + wr if SCRATCH[nm][0] == "psum"})})
        return i

    def join(count, size):
        first_, made = len(ops) - count, ops[len(ops) - count:]
        del ops[first_:]
        runs = -(-count // size) if count else 0
        new = [first_ + x * runs // count for x in range(count)]
        for r in range(runs):
            part = [o for o, x in zip(made, new) if x == first_ + r]
            ops.append(dict(part[0], fn=lambda q, e, part=part: [o["fn"](q, e) for o in part][-1], hard=set().union(*[o["hard"] for o in part]),
                            work=("sum", [o["work"] for o in part]), banks=sorted({b for o in part for b in o["banks"]})))
        for nm in last:
            m = last[nm] >= first_
            if m.any(): last[nm][m] = np.array(new)[last[nm][m] - first_]
            readers[nm] = [(new[r - first_] if r >= first_ else r, m) for r, m in readers[nm]]

    def price(o, ins, both=False):
        xs = [x for x in ins if isinstance(x, dict)]
        n = max([o["n"]] + [x["n"] for x in xs])
        if "off" in o: return ("cs", n)
        if any("off" in x for x in xs): return ("cg", n)
        if both: return (1.0 if any(x["ps"] for x in xs) else 2.0, n)
        return (0.5 if o["b"] == 2 and all(x["b"] == 2 for x in xs if x["n"] > 1) else 1.0, n)

    def ap(x): return x["ap"] if isinstance(x, dict) else x

    def copy(nm, o, i): return op(nm, "V", lambda q, e: q.tensor_copy(o["ap"], i["ap"]), [i], [o], price(o, [i]))

    def ts(nm, o, i, s1, o1, s2=None, o2=None):
        fn = (lambda q, e: q.tensor_scalar(o["ap"], i["ap"], ap(s1), None, o1)) if o2 is None else (lambda q, e: q.tensor_scalar(o["ap"], i["ap"], ap(s1), ap(s2), o1, o2))
        return op(nm, "V", fn, [i, s1, s2], [o], price(o, [i]))

    def tt(nm, o, a, b, f): return op(nm, "V", lambda q, e: q.tensor_tensor(o["ap"], a["ap"], b["ap"], f), [a, b], [o], price(o, [a, b], True))

    def scan(nm, o, a, b, f0, f1): return op(nm, "V", lambda q, e: q.tensor_tensor_scan(o["ap"], a["ap"], b["ap"], 0.0, f0, f1), [a, b], [o], price(o, [a, b]))

    def act(nm, o, i, func, scale=1.0, bias=0.0, acc=None):
        kw = {"accum_out": acc["ap"]} if acc else {}
        return op(nm, "A", lambda q, e: q.activation(o["ap"], i["ap"], func, bias=ap(bias), scale=ap(scale), **kw), [i, scale, bias], [o] + ([acc] if acc else []), price(o, [i]))

    def lin(nm, o, i, scale=1.0, bias=0.0, eng="VA"):
        def fn(q, e):
            if e == "A": return q.activation(o["ap"], i["ap"], AF.Identity if bias else AF.Copy, bias=ap(bias), scale=ap(scale))
            if bias: return q.tensor_scalar(o["ap"], i["ap"], ap(scale), ap(bias), OP.mult, OP.add)
            return q.tensor_copy(o["ap"], i["ap"]) if scale == 1.0 else q.tensor_scalar(o["ap"], i["ap"], ap(scale), None, OP.mult)
        return op(nm, eng, fn, [i, scale, bias], [o], price(o, [i]))

    def fill(o, c): return op("fill", "V", lambda q, e: q.memset(o["ap"], c), [], [o], price(o, []))

    def mm(nm, lst, first=True, final=True, size=None, slow=1, whole=None):
        size = size or len(lst)

        def fn(q, e):
            x = None
            for k, (o, l, r) in enumerate(lst): x = q.matmul(o["ap"], l["ap"], r["ap"], first and k % size == 0, final and k % size == size - 1)
            return x
        return op(nm, "T", fn, [x for y in lst for x in y[1:]], [whole] if whole else [y[0] for y in lst], ("mm", [slow * y[2]["n"] for y in lst]))

    def G(o, ins, fn): return op("const", "G", lambda q, e: fn(q), ins, [o], ("G", o["n"]))

    def dma(q, o, i, ins, outs, sem, lat): return op("dma", q, lambda x, e: x.dma_start(o, i), ins, outs, ("fix", 0.1), (sem, 16, lat))

    chunks = par["chunks"]
    ncm = max(nc for _, nc in chunks)
    for q, name, dst, lat in par["loads"]: dma(q, T[dst][:], T[name][:], [], [v(dst)], "ld_" + name, lat)
    imp = {"allow_small_or_imprecise_dtypes": True}
    ON, IDN, NID, R16 = w("ON", 0, 128), v("IDN"), v("NID"), v("R16")
    fill(w("ON", 0, 256), 1.0), fill(w("ON", 256, 768), 1.0)
    G(v("PI"), [], lambda q: q.iota(T.PI[:], [[0, 1]], 0, 1))
    G(v("BLB"), [ON], lambda q: q.affine_select(T.BLB[:], ON["ap"], [[-16, 8], [0, 16]], OP.is_ge, 0.0, 0, 1))
    G(v("BLK"), [v("BLB")], lambda q: q.affine_select(T.BLK[:], T.BLB[:], [[16, 8], [0, 16]], OP.is_ge, 0.0, 15, -1))
    G(v("CMB"), [w("ON", 0, 256)], lambda q: q.affine_select(T.CMB[:], T.ON[:, 0:256], [[-1, 16], [1, 16]], OP.is_equal, 0.0, 0, 0))
    G(IDN, [ON], lambda q: q.affine_select(T.IDN[:], ON["ap"], [[-1, 128]], OP.is_equal, 0.0, 0, 1))
    KI = w("KI", 0, 18 * ncm)
    G(KI, [], lambda q: q.iota(KI["ap"], [[512, ncm], [2, 18]], 14, 0, **imp))
    G(v("IOTA"), [], lambda q: q.iota(T.IOTA[:], [[1, 1024]], 0, 0, **imp))
    VB = w("VB", 0, 512 * ncm + 32)
    G(VB, [], lambda q: q.iota(VB["ap"], [[0, 256 * ncm + 16], [-1, 2]], 1, 0, **imp))
    copy("MU0", v("MU0"), v("M0"))
    copy("MC", w("MC", 0, 1024), v("MCI"))
    fill(w("MC", 1024, 16 * ncm), 0.0)
    ts("MSK", v("MSK"), w("BLK", 0, 8, 16), BIG, OP.mult)
    for x in range(8): lin("RMC", v("RMC", S[:, x, :]), v("CMB"), w("MSK", x, 1))
    copy("B8", w("B8", 0, 8), w("BLK", 0, 8, 16))
    ts("B8", w("B8", 8, 8), w("BLK", 0, 8, 16), -1.0, OP.mult)
    ts("WS", v("WS"), v("WT"), 1.0 / BIG, OP.mult)
    lin("RMW", v("RMW"), v("RMC"), v("WS"))
    ts("BW", v("BW"), v("BLK"), v("WT"), OP.mult)
    ts("BN", v("BN"), v("BLK"), STEP, OP.mult)
    ts("NID", NID, IDN, -1.0, OP.mult)
    copy("DVF", v("DVF"), v("DV"))
    for h, (c0, nc) in enumerate(chunks):
        b, n = 32 * (16 * c0 + 2 - h), 16 * nc
        fill(w("AB", b, 16), 0.0), fill(w("AB", b + 16 + 32 * n, 16), 0.0)
        for x in range(0, 16 * n, 1024):
            lin("AB%d" % h, w("AB", b + 17 + 2 * x, min(1024, 16 * n - x), 2), w("ON", 0, min(1024, 16 * n - x)), 0.0)
            lin("PB%d" % h, w("PB", b + 16 + 2 * x, min(1024, 16 * n - x), 2), w("ON", 0, min(1024, 16 * n - x)), 0.0)
        fill(w("AB", b + 47, n, 32), -256.0)
    fill(v("C", S[:, 0]), 0.0)
    LO, HI = S[0:64], S[64:128]
    fill(v("NON"), -1.0), fill(v("PM", None, LO), -1.0), fill(v("PM", None, HI), 1.0), fill(v("BT", None, LO), -STEP / 128), fill(v("BT", None, HI), -12.5 * STEP / 64), fill(v("HF"), 1.0 / 256)
    fill(v("CU"), 0.0), fill(v("CU", S[128:256], LO), -32.0), fill(v("CU", S[128:256], HI), 1.0 / 128), copy("IDF", v("IDF"), IDN)
    ts("PR16", v("PR16"), v("PI"), 15, OP.bitwise_and)
    copy("R16", R16, v("PR16"))
    ts("R32", v("R32"), R16, 32.0, OP.mult)
    ts("C37", v("C37"), R16, 592.0, OP.mult, -196608.0, OP.add)
    for c0, nc in chunks:
        ts("KV", w("KV", 18 * c0, 18 * nc), w("KI", 0, 18 * nc), v("R32"), OP.add)
        fill(w("KV", 18 * c0, nc, 18), 1.0), fill(w("KV", 18 * c0 + 17, nc, 18), 512.0 * nc + 17)
    seg, pos = {}, 0
    for h, (c0, nc) in enumerate(chunks):
        gr = par["group"][h]
        ln = 16 * gr + 2
        seg[h], pos = (pos, ln), pos + nc * ln
        sb, sc, sp = seg[h][0], w("SC", seg[h][0], nc * ln), w("SP", c0, nc)
        G(sc, [], lambda q, sc=sc, nc=nc, ln=ln: q.iota(sc["ap"], [[0, nc], [-1, ln]], 16, 0, **imp))
        G(sp, [], lambda q, sp=sp, nc=nc, gr=gr: q.iota(sp["ap"], [[0, nc // gr], [16, gr]], 1024, 0, **imp))
        ts("RS", sc, sc, R16, OP.is_equal)
        tt("RS", w("RS", sb, nc * ln - 1), w("SC", sb, nc * ln - 1), w("SC", sb + 1, nc * ln - 1), OP.subtract)
        ts("RS", w("RS", sb + ln - 1, nc, ln), sp, R16, OP.add)
        ts("SPT", w("SPT", c0, nc), w("RS", sb + ln - 1, nc, ln), -OFF, OP.add)
        lin("NE", w("NE", sb, nc * ln), w("ON", 0, nc * ln)), fill(w("NE", sb, nc, ln), 0.0)
    unit, br = BIG / 64, {}
    for na in sorted(set(par["scalar"].values())):
        x = br[na] = len(br)
        for k, a0, a1 in ((S[0:1], 0.0, 32 * unit), (S[1:1 + na], -unit, -8 * unit), (S[1 + na:18], -unit / 2, -12 * unit)):
            if k.start < k.stop: fill(v("BR", (x, S[0:ncm], k), LO), a0), fill(v("BR", (x, S[0:ncm], k), HI), a1)

    rid, pid, _ = topo.addr(nxt)
    mask, ne = topo.mask(core, nxt), len(topo.engines(core, nxt))
    sent, turn = {}, [0]

    def send(kind, t, h, src, a, n):
        o, i = T["%s%d" % ({"z": "ZI", "m": "MU"}[kind], t)][:, a:a + n], w(src, a, n)
        sent[kind, t, h] = op("s%s%d" % (kind, h), "G", lambda q, e: q.remote_dma(o, i["ap"], T.sem["%si%d%d" % (kind, t, h)], T.sem["%sl%d%d" % (kind, t, h)], pid, rid, mask),
                              [i], [], ("fix", 0.5), ("%sl%d%d" % (kind, t, h), ne, 1.5))

    def head(t, h):
        (c0, nc), s = chunks[h], str(h)
        a, n, b = 16 * c0, 16 * nc, 32 * (16 * c0 + 2 - h)
        mu, z0, xs = w("MU%d" % t, c0, nc), w("ZI%d" % t, a, n), w("P%d" % (3 + h % 2), 288, n)
        m = n // par["pieces"]
        for c in range(par["pieces"]): lin("p%d%d" % (h, c), w("PB", b + 15 + 32 * m * c, 16 * m, 2), ind(v("PR"), w("OU", a + m * c, m)))
        for c in range(par["pieces"]): lin("a%d%d" % (h, c), w("AB", b + 16 + 32 * m * c, 16 * m, 2), ind(v("AD"), w("OU", a + m * c, m)), -1.0)
        lin("P0" + s, w("PB", b + 16, n, 32), w("PB", b + 15, n, 32))
        lin("G" + s, w("PB", b + 47, n, 32), ind(v("GL"), mu))
        back = S[b + 15 + 32 * n:b + 15:-1]
        scan("K" + s, v("KB", S[32 * (a + n) - 1:(32 * a - 1 if a else None):-1]), v("AB", back), v("PB", back), OP.add, OP.max)
        if par["scalar"][h, 0] < 17: mm("zp" + s, [(w("P2", a, n), IDN, z0)])
        lin("Y" + s, w("Y", a, n), z0, 1.0, -255.0)
        lin("Mb" + s, w("M37", 17 * c0, n), ind(v("IOTA"), mu), 37.0, -OFF - 0.5)
        ts("Ml" + s, w("M37", 17 * c0 + n, nc), mu, 37.0, OP.mult, -OFF - 0.5, OP.add)
        ts("M4" + s, w("M4", c0, nc), mu, -OFF, OP.add)
        mm("e0" + s, [(xs, IDN, w("KB", 32 * a + 1, n, 32)), (xs, IDN, w("AB", b + 16, n, 32))])
        act("R0" + s, w("R0", a, n), xs, AF.Relu)
        rows, w0, og = S[0:n], w("P5", 128, n), w("OG", a, n)
        for k4 in range(1, -1, -1):
            lst = []
            for k in range(8 * k4, 8 * k4 + 8):
                o = v("P5", S[k:113 + k:16], rows)
                lst += [(o, w("KB", 32 * a + 2 * k + 1, n, 32), w("B8", 0, 8)), (o, w("KB", 32 * a + 2 * k, n, 32) if k else w("R0", a, n), w("B8", 8, 8))]
            mm("us" + s, lst, size=2)
        act("FT" + s, v("FT", None, rows), v("P5", S[0:128], rows), AF.Sign, -1.0, 253.5)
        mm("ft" + s, [(w0, v("FT", None, rows), v("IDN", S[0:n], rows))])
        lin("W0" + s, w0, w0, v("C37"), v("C37"))
        tt("OG" + s, og, w("NO", a, n), w0, OP.max)
        tt("W" + s, w("W", a, n), w("O32", a, n), w0, OP.add)

    def one_pass(t, h, j):
        (c0, nc), s, js = chunks[h], str(h), "%d%d" % (h, j)
        a, n, b, XB = 16 * c0, 16 * nc, 32 * (16 * c0 + 2 - h), "P%d" % (3 + h % 2)
        z, y, z1, vg, dg, xs = w("Z1" if j else "ZI%d" % t, a, n), w("Y", a, n), w("Z1", a, n), w("VG", a, n), w("DG", a, n), w(XB, 288, n)
        ks, ku, na = w("KS", 18 * c0 + 17, nc, 18), w("KU", c0, nc), par["scalar"][h, j]
        cs = nc // par["split"][h]
        for c1 in range(0, nc, cs):
            m, a1 = 16 * cs, a + 16 * c1
            def kk(k): return w("KB", 32 * a1 + (2 * k - 1 if k else 0), m, 32)
            per = 512 // m
            for k0 in range(0, na, per):
                bank = "P%d" % par["dbanks"][turn[0] % len(par["dbanks"])]
                turn[0] += 1
                ks_ = range(k0, min(na, k0 + per))
                mm("d" + js, [x for k in ks_ for x in ((w(bank, m * (k - k0), m), NID, kk(k)), (w(bank, m * (k - k0), m), IDN, w(z["el"][0][0], a1, m)))], size=2)
                for k in ks_: act("s" + js, v("C", S[a1:a1 + m, k + 1]), w(bank, m * (k - k0), m), AF.Sign, 1.0, 0.5)
                join(len(ks_), 4)
            for k in range(16 - j, na - 1, -1): tt("c" + js, v("C", S[a1:a1 + m, k + 1]), kk(k), w("P2", a1, m), OP.is_le)
            join(17 - j - na, 3)
            o = w(XB, 18 * c1, 18 * cs)
            mm("n" + js, [(o, v("PM"), v("BR", S[br[na], 0:cs]))] + [(o, v("RMC", S[r]), v("C", S[a1 + r:a1 + m:16])) for r in range(16)])
        scan("KS" + js, w("KS", 18 * c0, 18 * nc), w(XB, 0, 18 * nc), w("KV", 18 * c0, 18 * nc), OP.max, OP.min)
        copy("KU" + js, ku, ks)
        lin("DG" + js, dg, ind(w("VB", 0, 32 * n + 32), ku), w("DVF", 2 * t + j, 1), 0.0, "A")
        if j and s in par["act2"]:
            lin("VG" + js, vg, ind(w("AB", b, 32 * n + 32), ku))
            mm("e" + js + "x", [(xs, IDN, z), (xs, NID, vg)])
            act("Y1" + s, y, xs, AF.Relu, 1.0, -255.0)
            mm("x" + js, [(xs, IDN, z), (xs, NID, vg), (xs, NID, dg), (xs, NID, y)])
        else:
            tt("VG" + js, vg, ind(w("AB", b, 32 * n + 32), ku), y, OP.max)
            mm("x" + js, [(xs, IDN, z), (xs, NID, vg), (xs, NID, dg)])
        ml = w("X", 17 * c0 + n, nc)
        if j:
            act("Z" + s, w("Z" if t < 3 else "ZF", a, n), xs, AF.Abs)
            act("NN" + s, w("NN", c0, nc), ks, AF.Sign, 1.0, -1.0)
            ts("GO" + s, w("GO", c0, nc), ks, 512.0 * nc + 17, OP.is_equal)
            tt("VF" + s, w("VF", c0, nc), w("NN", c0, nc), w("GO", c0, nc), OP.subtract)
            tt("TQ" + s, w("TQ", c0, nc), w("VF", c0, nc), w("D0", c0, nc), OP.mult)
            tt("MN" + s, w("MN", c0, nc), w("TQ", c0, nc), ml, OP.add)
            ts("MS" + s, w("MS" if t < 3 else "YM", c0, nc), w("MN", c0, nc), OFF, OP.add)
            if t < 3: send("m", t + 1, h, "MS", c0, nc), send("z", t + 1, h, "Z", a, n)
            return
        act("Z1" + s, z1, xs, AF.Abs)
        if par["scalar"][h, 1] < 16 or s in par["zp"]: act("ZP" + s, w("P2", a, n), xs, AF.Abs)
        if s not in par["act2"]: lin("Y1" + s, y, z1, 1.0, -255.0)
        TB = "P%d" % (6 + h % 2)
        tb, ub, uh, xb, xl, xx = w(TB, 0, 49 * nc), w(TB, 0, n), w(TB, n, n), w(TB, 2 * n, n), w(TB, 3 * n, nc), w(TB, 2 * n, 17 * nc)
        mm("mc" + s, [(tb, ON, w("CU", 128 - n, 49 * nc))], True, False)
        mm("mo" + s, [(xx, v("IDF"), w("M37", 17 * c0, 17 * nc))], False, False, slow=4, whole=tb)
        mm("ub" + s, [(ub, v("BW"), z1), (uh, v("BW"), z1), (xb, v("BW"), z1)], False, False, whole=tb)
        mm("xl" + s, [(xl, v("RMW", S[r]), w("Z1", a + r, nc, 16)) for r in range(16)], False, False, whole=tb)
        tt("cg" + s, v("C", S[a:a + n, 17]), w("KB", 32 * a + 31, n, 32), w("P2", a, n) if s in par["zp"] else z1, OP.is_le)
        mm("gn" + s, [(xb, v("PM"), w("BT", 0, n)), (xb, v("BN"), v("C", S[a:a + n, 17])), (xx, ON, w("HF", 0, 17 * nc))], False, True, whole=tb)
        qx, qu, x = w("QX", 17 * c0, 17 * nc), w("QU", a, n), w("X", 17 * c0, 17 * nc)
        lin("TX" + s, qx, xx, 1.0 / 1024, MAGIC)
        act("QX" + s, qx, qx, AF.Relu, 1024.0, -2.0 ** 19 - 1024 * MAGIC)
        tt("X" + s, x, xx, qx, OP.subtract)
        lin("TU" + s, qu, uh, 1.0 / 4096, MAGIC)
        lin("QU" + s, qu, qu, -4096.0, 4096 * MAGIC)
        tt("U" + s, ub, ub, qu, OP.add)
        gr = par["group"][h]
        (sb, ln), xw = seg[h], 2 if gr == 1 else 1
        tt("NF" + s, w("NE", sb + ln - 1, nc, ln), ml, w("SPT", c0, nc), OP.subtract)
        for c in range(nc - 1, -1, -1):
            hi = 17 * c0 + 16 * c + 15
            lo = hi - 16 * (c % gr + 1)
            ts("NE" + s, w("NE", sb + ln * c + 1, hi - lo), v("X", S[hi:(lo if lo >= 0 else None):-1]), w("X", 17 * c0 + n + c, 1), OP.not_equal)
        join(nc, 4)
        scan("SC" + s, w("SC", sb, nc * ln), w("NE", sb, nc * ln), w("RS", sb, nc * ln), OP.mult, OP.add)
        copy("XF" + s, w("XF", 2 * c0, nc, xw), w("SC", sb + ln - 1, nc, ln))
        tt("PP" + s, ub, ub, w("OG", a, n), OP.mult)
        tt("XP" + s, w("XP", a, n), w("W", a, n), ub, OP.subtract)
        ts("NW" + s, w("NW", a, n), w("XP", a, n), 5, OP.arith_shift_right, 4095, OP.bitwise_and)
        for c in range(nc - gr, -1, -gr): copy("put" + s, ind(w("MC", 0, 1024 + 16 * ncm), w("XF", 2 * c0 + xw * c, gr)), w("NW", a + 16 * c, 16 * gr))
        tt("D0" + s, w("D0", c0, nc), w("M4", c0, nc), ml, OP.subtract)

    for t in range(4):
        step[0] = t
        for h, (c0, nc) in enumerate(chunks):
            a, n, s, mu = 16 * c0, 16 * nc, str(h), w("MU%d" % t, c0, nc)
            if t:
                op("m in", "", None, [], [mu], ("fix", 0.0), ("mi%d%d" % (t, h), ne, par["far"]), [sent["m", t, h]])
                op("z in", "", None, [], [w("ZI%d" % t, a, n)], ("fix", 0.0), ("zi%d%d" % (t, h), ne, par["far"]), [sent["z", t, h]])
            copy("OU" + s, w("OU", a, n), ind(w("MC", 0, 1024) if t else v("MCI"), mu))
            if s in par["no"]: lin("NO" + s, w("NO", a, n), ind(w("MC", 0, 1024), mu), -1.0, 0.0, "A")
            else: ts("NO" + s, w("NO", a, n), w("OU", a, n), -1.0, OP.mult)
            lin("O32" + s, w("O32", a, n), w("NO", a, n), -32.0)
        for h, j in par["passes"]:
            if j == 0: head(t, h)
            one_pass(t, h, j)
        if t < 3:
            pa = w("P5", 496, 16)
            mm("A", [(pa, ON, v("GO"))])
            act("AC", v("JK"), pa, AF.Identity, -0.5, 1.0 / 64, v("AC"))
            ts("RY", v("RY"), v("AC"), MAGIC, OP.add, MAGIC, OP.subtract)
            act("PM", v("PM", None, LO), v("NON", None, LO), AF.Sign, v("AC", None, LO), v("RY", None, LO))
    dma("S", T.ymc[:], T.MC[:, 0:1024], [v("MC", S[0:1024 + 16 * ncm])], [], "so2", 3.5)
    dma("S", T.yz[:], T.ZF[:], [v("ZF")], [], "so0", 2.5)
    dma("S", T.ym[:], T.YM[:], [v("YM")], [], "so1", 2.0)
    return ops


def first(lst, t):
    lo, hi = 0, len(lst)
    while lo < hi:
        mid = (lo + hi) // 2
        if lst[mid][1] > t: hi = mid
        else: lo = mid + 1
    return lo


def place(ops, par, links, prio, fixed=None, tail=None):
    n, wake = len(ops), par["wake"]
    kids, need = [[] for _ in ops], [len(x) for x in links]
    for i in range(n):
        for d, _ in links[i]: kids[d].append(i)
    busy = {k: [] for k in list("VATGS") + ["P%d" % b for b in range(8)]}
    start, dur, eng = [0.0] * n, [0.0] * n, [""] * n
    ready = [i for i in range(n) if need[i] == 0]
    while ready:
        i = max(ready, key=lambda x: (prio[x], -x))
        ready.remove(i)
        o = ops[i]
        est, best = max([start[d] + dur[d] + gap for d, gap in links[i]] + [tail[i] if tail else 0.0]), None
        for e in [fixed[i]] if fixed else par["pin"].get(o["name"], o["eng"]) if len(o["eng"]) > 1 else o["eng"] or [""]:
            c, t0, moved = cost(o["work"], e, par), est, True
            while moved and e:
                moved = False
                for k in [e] + o["banks"]:
                    lst = busy[k]
                    for x in range(first(lst, t0 - wake), len(lst)):
                        a, b, who = lst[x]
                        gap = wake if who != e else 0.0
                        if a >= t0 + c + wake: break
                        if a < t0 + c + gap and t0 < b + gap: t0, moved = b + gap, True
            key = t0 + c + (par["bias"] if e == "V" else 0.0)
            if best is None or key < best[0]: best = (key, e, t0, c)
        _, e, t0, c = best
        start[i], dur[i], eng[i] = t0, c, e
        for k in ([e] if e else []) + o["banks"]: busy[k].insert(first(busy[k], t0), (t0, t0 + c, e))
        for k in kids[i]:
            need[k] -= 1
            if need[k] == 0: ready.append(k)
    return start, dur, eng


def schedule(ops, par):
    n, wake = len(ops), par["wake"]
    late = [o["done"][2] - o["work"][1] if o["done"] else 0.0 for o in ops]
    links = [[(d, late[d] + wake if ops[d]["eng"] and o["eng"] else late[d] * bool(o["eng"]) + wake) for d in o["hard"]] + [(d, 0.0) for d in o["soft"]] for o in ops]
    due = [par["period"] * o["step"] + par["due"].get(o["name"], 0.0) + par["due"].get("last", 0.0) * (o["step"] == 3 and o["name"] in SECOND) + par["sp"].get((o["name"], o["step"]), 0.0) + 1e-6 * i if o["step"] >= 0 else 999.0 for i, o in enumerate(ops)]
    for i in range(n - 1, -1, -1):
        for d, gap in links[i]:
            if ops[d]["step"] < 0: due[d] = min(due[d], due[i] - gap - cost(ops[d]["work"], ops[d]["eng"][0], par))
    start, dur, eng = place(ops, par, links, [-x for x in due])
    back = [[] for _ in ops]
    for i in range(n):
        for d, gap in links[i]: back[d].append((i, gap))
    for _ in range(par["just"]):
        s2, _, _ = place(ops, par, back, [start[i] + dur[i] for i in range(n)], eng, [0.0 if back[i] else late[i] for i in range(n)])
        start, _, _ = place(ops, par, links, [s2[i] + dur[i] for i in range(n)], eng)
    order = sorted(range(n), key=lambda i: (start[i], i))
    user, waits = {}, [set(o["hard"]) for o in ops]
    for i in order:
        for k in ops[i]["banks"]:
            waits[i] |= {d for x, d in user.setdefault(k, {}).items() if x != eng[i]}
            user[k][eng[i]] = i
    return order, eng, waits, start, dur


PLAN = {}
CODE = "jskhe0indrf3gbg300iud8chbijbaebmdegea9faepbhfqj7k0gvawkk95i0c4h3edaqgughf4gabr5hb7gnc4imhqgoc6dj9icf8y6t9vc9gveo7keh7nelezi4i7fhble5b3az5w65c4a9agi9eyedd6b1e2et2qjsc7crgne8goffd9bzd5lbk0a5bnca7ffsefbyb0aiepf8eud0c6b6enfogj5g65jjjqk46ej6gtd2apfp8oci8655icfhdpar64ahaddwhzdrc36t7zfc7bi1eb9n5gfffpl759fv9ea85v9s_VBVABABABABAAAAAAABBABAAAVAVABAAVAA"


def unpack(ops, par):
    al, (d, f) = "0123456789abcdefghijklmnopqrstuvwxyz", CODE.split("_")
    names, flex = sorted({o["name"] for o in ops if o["step"] >= 0 and o["eng"]} | {"last"}), sorted({o["name"] for o in ops if len(o["eng"]) > 1})
    due = {n: round((al.index(d[2 * i]) * 36 + al.index(d[2 * i + 1])) / 10 - 40, 1) for i, n in enumerate(names)}
    return dict(par, due=due, pin={n: {"B": "VA"}.get(c, c) for n, c in zip(flex, f)})


def rank_program(g, core, T, topo):
    rank = T.rank_of(core)
    if rank is None:
        return
    ops = build(T, topo, core, T.cores[(rank + 1) % len(T.cores)], PAR)
    if not PLAN: PLAN["all"] = schedule(ops, unpack(ops, PAR))
    order, eng, waits, _, _ = PLAN["all"]
    Q = {"V": g.vector, "A": g.scalar, "T": g.tensor, "G": g, "S": g.sync}
    cnt = {e: 0 for e in Q}
    done, know = {}, {}
    known = {e: {} for e in Q}
    for i in order:
        o, e = ops[i], eng[i]
        if not e:
            done[i] = o["done"][:2]
            know[i] = {done[i][0]: done[i][1]}
            continue
        kn = known[e]
        wants = {}
        for d in waits[i]:
            s, c = done[d]
            if kn.get(s, 0) < c and wants.get(s, (0, 0))[0] < c: wants[s] = (c, d)
        for s in sorted(wants, key=lambda s: -wants[s][1]):
            c, d = wants[s]
            if kn.get(s, 0) >= c: continue
            Q[e].wait_ge(T.sem[s], c)
            for a, b in know[d].items():
                if kn.get(a, 0) < b: kn[a] = b
        x = o["fn"](Q[e], e)
        if o["done"]:
            done[i] = o["done"][:2]
            if o["name"] == "dma": x.then_inc(T.sem[done[i][0]], done[i][1])
        else:
            cnt[e] += 1
            done[i] = ("s" + e, cnt[e])
            x.then_inc(T.sem["s" + e], 1)
        know[i] = dict(kn)
        know[i][done[i][0]] = done[i][1]
    kn = known["S"]
    for i in reversed(order):
        s, c = done[i]
        if kn.get(s, 0) < c:
            g.sync.wait_ge(T.sem[s], c)
            kn[s] = c
